import numpy as np, ml_dtypes
CORES = [113,118,241,246]
N = 4
BF = ml_dtypes.bfloat16
def gentries(a):
    return np.ascontiguousarray(a.reshape(8, 16, -1).transpose(0, 2, 1)).reshape(8, -1)
def gtable(e):
    e = np.asarray(e); return np.ascontiguousarray(e.reshape(8, -1, 16).transpose(0, 2, 1)).reshape(128, -1).astype(np.int32)
V, K, CAP, S, RO, TH = 2304, 512, 192, 5, 3, 8
def trees(rng, x, span):
    n = N * 8; v = np.arange(V); back = 1 + (span[..., None] * rng.random((N, 8, V)) ** 2).astype(np.int64)
    p = np.where((rng.random((N, 8, V)) < 0.003) | (v == 0), v, np.maximum(v - back, 0))
    ids = np.argsort(rng.random((N, 8, V)), axis=-1); inv = np.argsort(ids, axis=-1)
    xo = np.ascontiguousarray(np.take_along_axis(x, ids[:, :, None, :], 3).reshape(n, 16, V).transpose(2, 0, 1)).astype(np.int16)
    po = np.ascontiguousarray(p.reshape(n, V).T); a = np.arange(n)
    jo = np.zeros((V, n), np.int64); lo = np.zeros((V, n), np.int64); mo = np.zeros((V, n, 16), np.int16)
    for i in range(V):
        pi = po[i]; top = pi == i; ji = jo[pi, a]; lp = lo[pi, a]; lj = lo[ji, a]; same = lp == lj
        jo[i] = np.where(top, i, np.where(same, jo[ji, a], pi)); lo[i] = np.where(top, 0, np.where(same, lp + lj + 1, 1))
        mo[i] = np.where(top[:, None], 0, np.where(same[:, None], np.maximum(xo[i], np.maximum(mo[pi, a], mo[ji, a])), xo[i]))
    j = jo.T.reshape(N, 8, V); l = lo.T.reshape(N, 8, V); m = mo.transpose(1, 2, 0).reshape(N, 8, 16, V)
    go = lambda e: np.take_along_axis(e, inv, 2)
    return np.take_along_axis(m, inv[:, :, None, :], 3).astype(np.int64), np.take_along_axis(ids, go(p), 2), np.take_along_axis(ids, go(j), 2), go(l)
def spans(rng):
    return np.stack([rng.permutation(np.array([0, 3, 8, 30, 100, 400, 1500, V])) for _ in range(N)])
def asks(rng, top):
    a = (top[..., None] * rng.random((N, 8, K)))[:, :, None, :]
    return np.minimum((256 * (a + (1 - a) * rng.random((N, 8, 16, K)))).astype(np.int64), 255)
def tops(rng):
    return np.stack([rng.permutation(np.array([0.3, 0.5, 0.6, 0.7, 0.8, 0.9, 0.95, 0.99])) for _ in range(N)])
def pack(x, m, par, jump, ln, q, u, w):
    b = lambda e: np.ascontiguousarray(e.reshape(N, 128, -1)).astype(np.float32).astype(BF)
    return {"x": b(x), "m": b(m), "par": par.astype(np.int32), "jump": jump.astype(np.int32), "ln": ln.astype(np.int32), "q": b(q),
            "u0": np.stack([gtable(e) for e in u]), "w": np.ascontiguousarray(w.reshape(N, 128, 1)).astype(np.int32)}
def setup_inputs(rng):
    x = rng.integers(0, 256, (N, 8, 16, V)); m, par, jump, ln = trees(rng, x, spans(rng))
    return pack(x, m, par, jump, ln, asks(rng, tops(rng)), rng.integers(0, V, (N, 8, K)), rng.integers(0, 256, (N, 8, 16)))
def setup_inputs_room(rng):
    x = rng.integers(0, 255, (N, 8, 16, V)); m, par, jump, ln = trees(rng, x, spans(rng))
    n = rng.choice(np.array([0, 1, CAP - 1, CAP, CAP + 1, K]), (N, 8))
    n[0] = (CAP, CAP + 1, K, CAP - 1, 1, 0, CAP, CAP + 1); n[1] = (CAP, K, CAP - 1, K, K, CAP, 1, 0)
    fail = np.argsort(rng.random((N, 8, K)), axis=-1) < n[..., None]
    place = np.argsort(rng.random((N, 8, 16, K)), axis=2)
    q = np.where(place < np.where(fail, TH - 1, TH)[:, :, None, :], 0, 255)
    return pack(x, m, par, jump, ln, q, rng.integers(0, V, (N, 8, K)), rng.integers(0, 256, (N, 8, 16)))
def setup_inputs_votes(rng):
    v = np.stack([rng.permutation(np.array([0, 1, 63, 100, 127, 128, 200, 254])) for _ in range(N)])[:, :, None, None]
    x = v + rng.integers(0, 2, (N, 8, 16, V)); m, par, jump, ln = trees(rng, x, spans(rng))
    z = rng.random((N, 8, 16, K)); q = np.minimum(v + (z > 0.3) + (z > 0.8), 255)
    w = np.where(v[..., 0] == 254, rng.integers(250, 256, (N, 8, 16)), rng.integers(0, 256, (N, 8, 16)))
    return pack(x, m, par, jump, ln, q, rng.integers(0, V, (N, 8, K)), w)
def setup_inputs_free(rng):
    x = rng.integers(0, 256, (N, 8, 16, V)); m = (rng.integers(0, 256, (N, 8, 16, V)) * rng.random((N, 8, 1, V))).astype(np.int64)
    m[:, ::2] = rng.integers(0, 256, (N, 4, 16, V)); v = np.arange(V)
    par = rng.integers(0, V, (N, 8, V)); jump = rng.integers(0, V, (N, 8, V)); ln = rng.choice(np.array([0, 1, 2, V - 1]), (N, 8, V))
    par[:, 1] = rng.choice(np.array([0, V - 1]), (N, V)); jump[:, 1] = rng.choice(np.array([0, V - 1]), (N, V))
    par[:, 2] = v; ln[:, 3] = V - 1; jump[:, 4] = par[:, 4]; jump[:, 5] = v; par[:, 6] = (v + 1) % V
    ln[:, 6] = V - 1 - rng.integers(0, 4, (N, V)); ln[:, 7] = 1000 + rng.integers(0, 4, (N, V))
    ln[:, 0] = rng.integers(0, 256, (N, 1)) + rng.choice(np.array([0, 256, 512, 1024, 2048]), (N, V))
    l = rng.integers(1024, V // 2, (N, 1)); l[0] = V // 2 - 1; l[1] = 300 + rng.integers(0, 8); l[2] = 1024
    ln[:, 4] = np.where(rng.random((N, V)) < 0.5, l, 2 * l + 1)
    return pack(x, m, par, jump, ln, asks(rng, tops(rng)), rng.integers(0, V, (N, 8, K)), rng.integers(0, 256, (N, 8, 16)))
def setup_inputs_alike(rng):
    x = rng.integers(0, 256, (N, 8, 16, V)); s = spans(rng); s[:, 2] = 0; m, par, jump, ln = trees(rng, x, s)
    par[:, 3] = np.arange(V); jump[:, 3] = np.arange(V); ln[:, 3] = 0; m[:, 3] = 0
    c = rng.integers(0, V, (N, 8, 4)); c[:, 0] = (0, V - 1, 0, V - 1); w = rng.integers(0, 256, (N, 8, 16)); w[:, 1] = 0
    u = np.take_along_axis(c, rng.integers(0, 4, (N, 8, K)), 2)
    q = np.take_along_axis(asks(rng, tops(rng)), rng.integers(0, 4, (N, 8, 1, K)), 3)
    return pack(x, m, par, jump, ln, q, u, w)
def setup_inputs_spread(rng):
    x = (np.exp2(8 * rng.random((N, 8, 1, V))) * rng.random((N, 8, 16, V))).astype(np.int64); m, par, jump, ln = trees(rng, x, spans(rng))
    q = (np.exp2(8 * rng.random((N, 8, 1, K))) * rng.random((N, 8, 16, K))).astype(np.int64)
    u = (V * rng.random((N, 8, K)) ** 3).astype(np.int64); w = np.exp2(8 * rng.random((N, 8, 16))).astype(np.int64)
    return pack(x, m, par, jump, ln, q, np.minimum(u, V - 1), np.minimum(w, 255))
def check_inputs(d):
    bad = []
    for k in ("x", "m", "q"):
        a = np.asarray(d[k]).astype(np.float32)
        if not np.all((a >= 0) & (a <= 255) & (a == np.floor(a))): bad.append("whole numbers from 0 to 255 in " + k)
    for k, hi in (("par", V - 1), ("jump", V - 1), ("ln", V - 1), ("u0", V - 1), ("w", 255)):
        if np.min(d[k]) < 0 or np.max(d[k]) > hi: bad.append("range of " + k)
    return bad
def wpick(e, i):
    return np.take_along_axis(e, i[:, :, None, :], 3)
def npick(e, i):
    return np.take_along_axis(e, i, 2)
def votes(e, ask):
    return np.sum((e >= ask).astype(np.int64), axis=2)
def reference(x, m, par, jump, ln, q, u0, w):
    W = V + RO * K
    X = np.zeros((N, 8, 16, W), np.int64); Y = np.zeros((N, 8, 16, W), np.int64); P = np.zeros((N, 8, W), np.int64); J = np.zeros((N, 8, W), np.int64); L = np.zeros((N, 8, W), np.int64)
    X[..., :V] = x.astype(np.float32).reshape(N, 8, 16, V); Y[..., :V] = m.astype(np.float32).reshape(N, 8, 16, V)
    P[..., :V] = par; J[..., :V] = jump; L[..., :V] = ln
    ask = q.astype(np.float32).astype(np.int64).reshape(N, 8, 16, K); wt = w.astype(np.int64).reshape(N, 8, 16, 1)
    u = np.stack([gentries(a) for a in u0]).astype(np.int64)
    for t in range(RO):
        for s in range(S):
            rest = votes(wpick(X, u), ask) >= TH; far = votes(wpick(Y, u), ask) < TH
            u = np.where(rest, u, np.where(far, npick(J, u), npick(P, u)))
        j = npick(J, u); lp = npick(L, u); lj = npick(L, j); same = lp == lj; o = V + K * t
        X[..., o:o + K] = ask; P[..., o:o + K] = u
        J[..., o:o + K] = np.where(same, npick(J, j), u); L[..., o:o + K] = np.where(same, lp + lj + 1, 1)
        Y[..., o:o + K] = np.where(same[:, :, None, :], np.maximum(ask, np.maximum(wpick(Y, u), wpick(Y, j))), ask)
        if t < RO - 1:
            xu = wpick(X, u); fail = votes(xu, ask) < TH
            before = np.add.accumulate(fail.astype(np.int64), axis=2) - fail
            come = np.zeros((N, 8, 16, CAP), np.int64); got = np.zeros((N, 8, 1), np.int64)
            for r in range(N):
                for g in range(8):
                    c = np.flatnonzero(fail[r, g])[:CAP]; d = (r + 1) % N
                    come[d, g, :, :c.size] = ask[r, g][:, c]; got[d, g, 0] = c.size
            hit = fail & (before < got)
            ask = np.where(hit[:, :, None, :], wpick(come, np.minimum(before, CAP - 1)), (ask + xu + t) & 255)
            u = o + (np.sum(wt * ask, axis=2) & (K - 1))
    return {"ypar": P[..., V:].astype(np.float32), "yjump": J[..., V:].astype(np.float32), "ym": np.ascontiguousarray(Y[..., V:]).reshape(N, 128, RO * K).astype(np.float32).astype(BF)}

@@ -1,0 +1,509 @@
+from concourse.mybir import AluOpType as A, ActivationFunctionType as F
+
+V, K, CAP, S, RO = 2304, 512, 192, 5, 3
+W = V + RO * K
+H = K // 2
+BIG = 32768.0
+OPT = {"thr": 1}
+BF, FP, I32, U16 = "bfloat16", "float32", "int32", "uint16"
+SCRATCH = {}
+for _dt, _w, _names in (
+        (BF, [W], "X M TB"), (I32, [576], "raw loi"), (BF, [576], "hi lo"), (BF, [520], "R"), (BF, [144], "E Ew Ej"),
+        (BF, [128], "ones idn blk tri"), (BF, [64, 16], "rows"), (FP, [8], "cols"), (BF, [1040], "BM"),
+        (BF, [H, 4], "st0 st1"), (BF, [256], "d0"), (FP, [256], "so"), (U16, [32], "off joff soff goff"),
+        (I32, [32], "u0s hs"), (I32, [4], "ws"), (FP, [1], "wf"), (FP, [32], "i16 ai bb kk yy"), (BF, [33], "fail cum"),
+        (FP, [33], "ci nf tt msg0 msg1 lmsg0 lmsg1"), (I32, [2 * K], "W2"), (FP, [K], "ob0 ob1 ob2"),
+        (BF, [K], "bx qin0 qin1 q1 Gp Gj Mp t2 ab mr")):
+    for _n in _names.split():
+        SCRATCH[_n] = ("sbuf", [128] + _w, _dt)
+for _b in range(8):
+    SCRATCH["ps%d" % _b] = ("psum", [128, 512], FP)
+SEMAPHORES = ["v", "a", "p", "g", "sent", "rq0", "rq1", "rm0", "rm1"] + ["d%d" % _i for _i in range(24)]
+
+
+def emit(g, T, ops):
+    Q = {"v": g.vector, "a": g.scalar, "p": g.tensor, "g": g, "s": g.sync}
+    lastw, readers, bank = {}, {}, {}
+    known = {e: {} for e in Q}
+    seq = {e: 0 for e in Q}
+    need = set()
+    for i, o in enumerate(ops):
+        e = o["e"]
+        deps = set()
+        for r in o["r"]:
+            if r in lastw:
+                deps.add(lastw[r])
+        for r in o["w"]:
+            if r in lastw:
+                deps.add(lastw[r])
+            deps.update(readers.get(r, []))
+        for b in o["b"]:
+            for e2, j in bank.get(b, {}).items():
+                if e2 != e:
+                    deps.add(j)
+            bank.setdefault(b, {})[e] = i
+        for r in o["r"]:
+            readers.setdefault(r, []).append(i)
+        for r in o["w"]:
+            lastw[r] = i
+            readers[r] = []
+        o["waits"] = []
+        if e is not None:
+            for j in sorted(deps, reverse=True):
+                key, n = ops[j]["id"]
+                if known[e].get(key, 0) >= n:
+                    continue
+                o["waits"].append(j)
+                need.add(j)
+                for k2, n2 in ops[j]["clock"].items():
+                    if known[e].get(k2, 0) < n2:
+                        known[e][k2] = n2
+        if o["sem"] is None:
+            seq[e] += 1
+            o["id"] = (e, seq[e])
+        else:
+            o["id"] = (o["sem"], 1)
+        o["clock"] = dict(known[e]) if e is not None else {}
+        o["clock"][o["id"][0]] = o["id"][1]
+    total, waited = {}, {}
+    for i, o in enumerate(ops):
+        if o["sem"] is None:
+            if i in need:
+                total[o["e"]] = total.get(o["e"], 0) + 1
+                o["sig"] = (o["e"], total[o["e"]])
+        else:
+            total[o["sem"]] = total.get(o["sem"], 0) + o["n"]
+            o["sig"] = (o["sem"], total[o["sem"]])
+    for i, o in enumerate(ops):
+        if o["e"] is None:
+            continue
+        for j in o["waits"]:
+            s, n = ops[j]["sig"]
+            Q[o["e"]].wait_ge(T.sem[s], n)
+            waited[s] = max(waited.get(s, 0), n)
+        ins = o["f"]()
+        if o["kind"] == "dma":
+            ins.then_inc(T.sem[o["sem"]], 16)
+        elif o["kind"] == "op" and i in need:
+            ins.then_inc(T.sem[o["e"]], 1)
+    for s in total:
+        if waited.get(s, 0) < total[s]:
+            g.wait_ge(T.sem[s], total[s])
+
+
+def rank_program(g, core, T, topo):
+    rank = T.rank_of(core)
+    if rank is None:
+        return
+    N = len(T.cores)
+    nxt, prv = T.cores[(rank + 1) % N], T.cores[(rank - 1) % N]
+    rid, pid = topo.addr(nxt, core)
+    mask, n_out, n_in = topo.mask(core, nxt), len(topo.engines(core, nxt)), len(topo.engines(prv, core))
+    Ve, Sc, Pe = g.vector, g.scalar, g.tensor
+    ops, nd = [], [0]
+    ps = [T["ps%d" % b] for b in range(8)]
+    st = [T.st0, T.st1]
+    X, M, TB = T.X, T.M, T.TB
+
+    def op(e, f, r=(), w=(), b=()):
+        ops.append({"e": e, "f": f, "r": list(r), "w": list(w), "b": list(b), "sem": None, "kind": "op"})
+
+    def dma(e, out, in_, r=(), w=()):
+        q = g.sync if e == "s" else g.scalar
+        ops.append({"e": e, "f": lambda: q.dma_start(out, in_), "r": list(r), "w": list(w), "b": [],
+                    "sem": "d%d" % nd[0], "n": 16, "kind": "dma"})
+        nd[0] += 1
+
+    def send(out, in_, sem, r, land):
+        ops.append({"e": "g", "f": lambda: g.remote_dma(out, in_, T.sem[sem], T.sem.sent, pid, rid, mask),
+                    "r": list(r), "w": [], "b": [], "sem": "sent", "n": n_out, "kind": "send"})
+        ops.append({"e": None, "r": [], "w": [land], "b": [], "sem": sem, "n": n_in, "kind": "arrive"})
+
+    def mm(out, pairs, r, w, b, start=True, stop=True):
+        def f():
+            for i, (l, x) in enumerate(pairs):
+                ins = Pe.matmul(out, l, x, start and i == 0, stop and i == len(pairs) - 1)
+            return ins
+        op("p", f, r, w, b)
+
+    def tolist(out, lh, rhs, r, w, b):
+        mm(out, [(lh[:, 15 - i:143 - i], rhs(i)) for i in range(16)], r, w, b)
+
+    def memset(ap, c, w, b=()):
+        op("v", lambda: Ve.memset(ap, c), (), w, b)
+
+    def act(out, in_, fn, r, w, b=(), bias=0.0, scale=1.0):
+        op("a", lambda: Sc.activation(out, in_, fn, bias=bias, scale=scale), r, w, b)
+
+    def copy(out, in_, r, w, b=()):
+        op("v", lambda: Ve.tensor_copy(out, in_), r, w, b)
+
+    def tt(out, a, c, f, r, w, b=()):
+        op("v", lambda: Ve.tensor_tensor(out, a, c, f), r, w, b)
+
+    def ts(out, a, s1, f1, r, w, b=(), s2=None, f2=None):
+        if f2 is None:
+            op("v", lambda: Ve.tensor_scalar(out, a, s1, None, f1), r, w, b)
+        else:
+            op("v", lambda: Ve.tensor_scalar(out, a, s1, s2, f1, f2), r, w, b)
+
+    def sel(out, in_, pat, cmp, fill, base, cm, r, w):
+        op("g", lambda: g.affine_select(out, in_, pat, cmp, fill, base, cm), r, w)
+
+    def put(ap, pat, base, val, name):
+        sel(ap, ap, pat, A.not_equal, val, base, 1, [name], [name])
+
+    def col(k):
+        return T.cols[:, k:k + 1]
+
+    def xr(t):
+        return ["n0"] + ["n%d%d" % (i, h) for i in range(1, t + 1) for h in (0, 1)]
+
+    def win(B, t, offs, a, b):
+        return B[:, 0:V + K * t].indirect(offs[:, a:b])
+
+    for k, src in enumerate((T.par, T.jump, T.ln)):
+        dma("a" if k == 1 else "s", T.raw[32 * k:32 * k + 32, :], src[:], w=["raw%d" % k])
+    dma("a", T.u0s[:], T.u0[:], w=["u0s"])
+    dma("a", X[:, V:V + K], T.q[:], w=["Xn10", "Xn11"])
+    dma("s", X[:, 0:V], T.x[:], w=["Xn0"])
+    dma("a", M[:, 0:V], T.m[:], w=["Mn0"])
+    dma("s", T.ws[:, 0:1], T.w[:], w=["ws"])
+    Rf = (0, 1, 2, 3, 4, 6, 7)
+    Rn = ["R%d" % f for f in Rf]
+    op("g", lambda: g.iota(T.raw[96:128, :], [[1, 576]], 0, 576), w=["raw3"])
+    memset(T.ones[:], 1.0, ["ones"])
+    memset(T.R[:], 0.0, Rn)
+    memset(T.rows[0:1, 0:56, :], 0.0, ["row%d" % k for k in range(12)])
+    memset(T.E[:], 0.0, ["E"])
+    op("g", lambda: g.iota(T.rows[0:1, 56:64, :], [[0, 8], [1, 16]], 0, 0, allow_small_or_imprecise_dtypes=True), ["raw3"], ["row12"])
+    for f, k in zip(Rf, (0, 0, 1, 2, 3, 1, 0)):
+        sel(T.R[:, 8 + f:520:16], T.ones[:, 0:32], [[-1, 4], [0 if k == 3 else -4, 8]], A.is_equal, 0.0, -32 * k, 1, ["ones"], ["R%d" % f])
+    sel(T.E[:, 15::16], T.ones[:, 0:9], [[-16, 9]], A.is_ge, 0.0, 0, 1, ["ones"], ["E"])
+    op("g", lambda: g.iota(T.i16[:], [[16, 32]], K, 0, allow_small_or_imprecise_dtypes=True), w=["i16"])
+    sel(T.E[:, 15::16], T.E[:, 15::16], [[16, 9]], A.is_ge, 0.0, 15, -1, ["E"], ["E"])
+    segs = [(0, 2, 0, 8, 1.0), (0, 2, 1, 8, -1.0), (0, 3, 2, 8, 1.0), (2, 3, 1, 8, 1.0), (0, 1, 4, 8, -1.0),
+            (0, 1, 6, 8, -1.0), (0, 1, 7, 8, 1.0), (4, 7, 13, 16, 1.0)] + [(4 + t, 5 + t, 4, 16, float(V + K * t)) for t in range(RO)]
+    for i, (a, b, f, step, c) in enumerate(segs):
+        memset(T.rows[0:1, 8 * a:8 * b, f::step], c, ["row%d" % i])
+    memset(T.rows[0:1, 24:32, 0:8], -4128.0, ["row11"])
+    memset(T.d0[:], 0.0, ["d00", "d01"])
+    names = ["SLp", "SLn", "Mc1", "Mc2", "Mc3", "Ma0", "Ma1", "Ma3", "Ma7", "Mb", "Ms", "Zc", "Mo", "Ni"]
+    memset(T.BM[:], 0.0, names)
+    memset(T.cum[:, 0:1], 0.0, ["cum0"])
+    memset(T.nf[:, 32:33], 0.0, ["nf32"])
+    memset(T.ci[:, 32:33], 0.0, ["ci32"])
+
+    def turn():
+        for k in range(8):
+            ins = Pe.matmul(ps[7][:, 300 + k:301 + k], T.rows[0:1, 8 * k:8 * k + 8, :], T.ones[0:1, 0:1], True, True)
+        return ins
+    op("p", turn, ["ones"] + ["row%d" % k for k in range(13)], ["pc"], [7])
+    act(T.d0[:, 2::8], T.ones[:, 0:32], F.Sigmoid, ["ones"], ["d00", "d01"], scale=400.0)
+    act(T.cols[:], ps[7][:, 300:308], F.Identity, ["pc"], ["cols"], [7])
+    raws = ["raw%d" % k for k in range(4)]
+    for hf in range(2):
+        c = slice(288 * hf, 288 * hf + 288)
+        ts(T.loi[:, c], T.raw[:, c], 31, A.bitwise_and, raws, ["loi%d" % hf])
+        ts(T.hi[:, c], T.raw[:, c], 4112.5, A.add, raws, ["hi%d" % hf])
+        copy(T.lo[:, c], T.loi[:, c], ["loi%d" % hf], ["lo%d" % hf])
+    copy(T.off[:], T.u0s[:], ["u0s"], ["off0", "off1"])
+    for h in range(2):
+        memset(ps[h][:, 0:128], 0.0, ["pu%d" % h, "pe%d" % h], [h])
+    memset(T.fail[:, 32:33], 0.0, ["fail32"])
+    for h in range(2):
+        copy(ps[h][:, 3:128:8], T.u0s[:, 16 * h:16 * h + 16], ["u0s"], ["pu%d" % h], [h])
+    parts = []
+    for hf in range(2):
+        for c in range(4):
+            i = 4 * hf + c
+            b = 2 + i % 6
+            cs = slice(288 * hf, 288 * hf + 288)
+            mm(ps[b][:, 0:288], [(T.R[:, 8 + 128 * c:136 + 128 * c], T.hi[:, cs]), (T.R[:, 128 * c:128 * c + 128], T.lo[:, cs])],
+               Rn + ["hi%d" % hf, "lo%d" % hf], ["pb%d" % b], [b])
+            out = TB[:, 576 * c + 288 * hf:576 * c + 288 * hf + 288]
+            if i in (3, 5, 7):
+                ts(out, ps[b][:, 0:288], col(3), A.add, ["pb%d" % b, "cols"], ["tb%d" % i], [b])
+            else:
+                act(out, ps[b][:, 0:288], F.Identity, ["pb%d" % b, "cols"], ["tb%d" % i], [b], bias=col(3))
+            parts.append("tb%d" % i)
+    act(T.ai[:], T.i16[:], F.Identity, ["i16", "cols"], ["ai"], bias=col(7))
+    act(T.Ej[:], T.E[:], F.Identity, ["E", "cols"], ["Ej"], scale=col(1))
+    act(T.ci[:, 0:32], T.ai[:], F.Identity, ["ai"], ["ci"], bias=float(2 * K - 1), scale=-1.0)
+    send(T.qin0[:], X[:, V:V + K], "rq0", ["Xn10", "Xn11", "Xn0", "Mn0"], "qin0")
+    SLp, SLn, Mc, Ma, Mb, Ms, Zc, Ni = [T.BM[:, 128 * k:128 * k + 128] for k in range(8)]
+    Mo, Mo2 = T.BM[:, 1024:1040], T.BM[:, 1032:1040]
+
+    def bm(k, f, step):
+        return T.BM[:, 128 * k + f:128 * k + 128:step]
+    sel(T.blk[:], T.ones[:], [[-16, 8], [0, 16]], A.is_ge, 0.0, 0, 1, ["ones"], ["blk"])
+    sel(T.idn[:], T.ones[:], [[-1, 128]], A.is_equal, 0.0, 0, 1, ["ones"], ["idn"])
+    sel(T.blk[:], T.blk[:], [[16, 8], [0, 16]], A.is_ge, 0.0, 15, -1, ["blk"], ["blk"])
+    put(Zc, [[-16, 8], [0, 16]], 0, -BIG, "Zc")
+    sel(T.tri[:], T.blk[:], [[16, 8], [1, 16]], A.is_ge, 0.0, -1, -1, ["blk"], ["tri"])
+    put(Ni, [[-1, 128]], 0, -1.0, "Ni")
+    for i, f in enumerate((3, 11, 13)):
+        put(bm(0, 0, 16), [[-16, 8]], -f, 1.0, "SLp")
+        put(bm(1, 0, 16), [[-16, 8]], -f, -1.0, "SLn")
+        step = 8 if i == 0 else 4
+        put(bm(2, i + 1, step), [[-16, 8], [0, 16 // step]], 0, -BIG, "Mc%d" % (i + 1))
+        put(bm(4, 2, 4), [[-8, 16], [0, 2]], -i, (1.0, -1.0, 1.0)[i], "Mb")
+        if i < 2:
+            put(Mo, [[0, 2], [-16, 8]], -8 * i, 1.0, "Mo")
+    put(bm(3, 3, 8), [[-8, 16]], -3, 2.0, "Ma3")
+    put(Mo2, [[-16, 8]], -2, 1.0, "Mo")
+    put(bm(3, 0, 8), [[-8, 16]], -4, 1.0, "Ma0")
+    put(Mo2, [[-16, 8]], -10, 1.0, "Mo")
+    put(bm(3, 1, 8), [[-8, 16]], -4, 1.0, "Ma1")
+    put(Mo2, [[-16, 8]], -1, -1.0, "Mo")
+    put(bm(3, 11, 16), [[-16, 8]], -13, 2.0, "Ma3")
+    put(bm(3, 7, 8), [[-8, 16]], -4, 1.0, "Ma7")
+    put(Mo2, [[-16, 8]], -9, -1.0, "Mo")
+    put(bm(5, 4, 8), [[-8, 16]], -4, 1.0, "Ms")
+    both, h0, h1 = (0, 1), (0,), (1,)
+
+    def nm(n, hs):
+        return [n + str(h) for h in hs]
+
+    def rng(hs):
+        return slice(H * hs[0], H * hs[-1] + H), 16 * hs[0], 16 * hs[-1] + 16
+
+    for t in range(RO):
+        o = V + K * t
+        Xr, Mr, Tr = ["X" + n for n in xr(t)], ["M" + n for n in xr(t)], parts + ["T" + n for n in xr(t)[1:]]
+        qn = nm("Xn%d" % (t + 1), both)
+
+        def q(h):
+            return X[:, o + H * h:o + H * h + H]
+
+        def gx(h):
+            tt(st[h][:, :, 3], win(X, t, T.off, 16 * h, 16 * h + 16), q(h), A.is_ge, Xr + [qn[h], "off%d" % h], ["sx%d" % h])
+
+        def gm(h):
+            tt(st[h][:, :, 2], win(M, t, T.off, 16 * h, 16 * h + 16), q(h), A.is_ge, Mr + [qn[h], "off%d" % h], ["sm%d" % h])
+
+        def g1(h):
+            act(st[h][:, :, 1], win(TB, t, T.off, 16 * h, 16 * h + 16), F.Identity, Tr + ["cols", "off%d" % h], ["se%d" % h], scale=col(0))
+
+        def g2(h):
+            act(st[h][:, :, 0], st[h][:, :, 1], F.Identity, ["se%d" % h, "cols"], ["sd%d" % h], scale=col(2))
+
+        def pe(h):
+            tolist(ps[h][:, 0:128:2], T.E, lambda i: st[h][:, i::16, :], ["E"] + [n + str(h) for n in ("sx", "sm", "se", "sd")], ["pe%d" % h], [h])
+
+        def thresh(h, e="a"):
+            a, b = T.d0[:, 128 * h + 1:128 * h + 125:2], ps[h][:, 4:128:2]
+            if e == "a":
+                act(a, b, F.Sigmoid, ["pe%d" % h], ["d0%d" % h], [h], bias=3000.0, scale=-400.0)
+            else:
+                ts(a, b, 7.5, A.is_lt, ["pe%d" % h], ["d0%d" % h], [h])
+
+        def newu(h, last):
+            u, c = T.so[:, 128 * h + 3:128 * h + 128:8], slice(128 * h, 128 * h + 128)
+            op("v", lambda: Ve.tensor_tensor_scan(T.so[:, c], T.d0[:, c], ps[h][:, 0:128], 0.0, A.mult, A.add),
+               ["d0%d" % h, "pe%d" % h, "pu%d" % h], ["so%d" % h], [h])
+            copy(T.off[:, 16 * h:16 * h + 16], u, ["so%d" % h], ["off%d" % h])
+            if not last:
+                copy(ps[h][:, 3:128:8], u, ["so%d" % h], ["pu%d" % h], [h])
+
+        def start1(h):
+            copy(T.hs[:, 16 * h:16 * h + 16], ps[h][:, 192:208], ["ph%d" % h], ["hs%d" % h], [h])
+
+        def start2(h):
+            a, c = T.hs[:, 16 * h:16 * h + 16], float(o - K)
+            ts(a, a, K - 1, A.bitwise_and, ["hs%d" % h], ["hs%d" % h])
+            ts(T.off[:, 16 * h:16 * h + 16], a, c, A.add, ["hs%d" % h], ["off%d" % h])
+            ts(ps[h][:, 3:128:8], a, c, A.add, ["hs%d" % h], ["pu%d" % h], [h])
+
+        if t > 0:
+            start1(0)
+            start2(0)
+        for k in range(2 * S):
+            h = k % 2
+            gx(h)
+            g1(h)
+            if k == 0:
+                if t > 0:
+                    start1(1)
+            elif OPT["thr"] == 1:
+                thresh(1 - h)
+            g2(h)
+            if k > 0 and OPT["thr"] == 2:
+                thresh(1 - h)
+            gm(h)
+            pe(h)
+            if k > 0:
+                newu(1 - h, k == 2 * S - 1)
+            elif t > 0:
+                start2(1)
+            if k == 3 and t == 1:
+                act(T.q1[:], X[:, o:o + K], F.Identity, qn, ["q1"], bias=1.0)
+
+        def gat(dst, name, B, Br, offs, on, hs, e="a"):
+            c, a, b = rng(hs)
+            if e == "a":
+                act(dst[:, c], win(B, t, offs, a, b), F.Identity, Br + nm(on, hs), nm(name, hs))
+            else:
+                copy(dst[:, c], win(B, t, offs, a, b), Br + nm(on, hs), nm(name, hs))
+
+        def cx(h):
+            tt(T.bx[:, H * h:H * h + H], win(X, t, T.off, 16 * h, 16 * h + 16), q(h), A.is_ge, Xr + [qn[h], "off%d" % h], ["bx%d" % h])
+            tolist(ps[0][:, 128 + 16 * h:144 + 16 * h], T.E, lambda i: T.bx[:, H * h + i:H * h + H:16], ["E", "bx%d" % h], ["px%d" % h], [0])
+
+        def jl(hs):
+            c, a, b = rng(hs)
+            k = 2 + hs[0]
+            tolist(ps[k][:, a:b], T.Ej, lambda i: T.Gp[:, c.start + i:c.stop:16], ["Ej"] + nm("Gp", hs), ["pb%d" % k], [k])
+
+        def jc(hs):
+            c, a, b = rng(hs)
+            k = 2 + hs[0]
+            copy(T.joff[:, a:b], ps[k][:, a:b], ["pb%d" % k], nm("joff", hs), [k])
+
+        def bound1(hs):
+            c, a, b = rng(hs)
+            tt(T.t2[:, c], win(M, t, T.joff, a, b), T.Mp[:, c], A.max, Mr + nm("joff", hs) + nm("Mp", hs), nm("t2", hs))
+
+        def differ(hs, e="a"):
+            c, b = rng(hs)[0], 2 + hs[0]
+            mm(ps[b][:, c], [(SLp, T.Gp[:, c]), (SLn, T.Gj[:, c])], ["SLp", "SLn"] + nm("Gp", hs) + nm("Gj", hs), ["pb%d" % b], [b])
+            if e == "a":
+                act(T.ab[:, c], ps[b][:, c], F.Abs, ["pb%d" % b], nm("ab", hs), [b])
+            else:
+                ts(T.ab[:, c], ps[b][:, c], 0.0, A.not_equal, ["pb%d" % b], nm("ab", hs), [b])
+
+        def bound2(hs, e):
+            c, b = rng(hs)[0], 6 + hs[0]
+            more = [(Ni, X[:, o + c.start:o + c.stop])] if e == "a" else []
+            mm(ps[b][:, c], more + [(T.idn[:], T.t2[:, c]), (Zc, T.ab[:, c])],
+               ["idn", "Zc", "Ni"] + nm("t2", hs) + nm("ab", hs) + [qn[h] for h in hs], ["pb%d" % b], [b])
+            if e == "a":
+                act(T.mr[:, c], ps[b][:, c], F.Relu, ["pb%d" % b], nm("mr", hs), [b])
+
+        def bound3(hs, e, dq="s"):
+            c, b = rng(hs)[0], 6 + hs[0]
+            cc, yc = slice(o + c.start, o + c.stop), slice(K * t + c.start, K * t + c.stop)
+            mn, qs = nm("Mn%d" % (t + 1), hs), [qn[h] for h in hs]
+            if e == "a":
+                mm(ps[b][:, c], [(T.idn[:], X[:, cc]), (T.idn[:], T.mr[:, c])], ["idn"] + nm("mr", hs) + qs, ["pb%d" % b], [b])
+                act(M[:, cc], ps[b][:, c], F.Identity, ["pb%d" % b], mn, [b])
+            else:
+                tt(M[:, cc], ps[b][:, c], X[:, cc], A.max, ["pb%d" % b] + qs, mn, [b])
+            dma(dq, T.ym[:, yc], M[:, cc], mn)
+
+        def table1(hs):
+            c, b = rng(hs)[0], 4 + hs[0]
+            mm(ps[b][:, c], [(Ms, TB[:, c]), (Ma, T.Gp[:, c]), (Mb, T.Gj[:, c])], names + parts + nm("Gp", hs) + nm("Gj", hs), [], [b], True, False)
+
+        def table2(hs):
+            c, b = rng(hs)[0], 4 + hs[0]
+            cc = slice(o + c.start, o + c.stop)
+            mm(ps[b][:, c], [(Mc, T.ab[:, c])], names + nm("ab", hs), ["pb%d" % b], [b], False, True)
+            act(TB[:, cc], ps[b][:, c], F.Relu, ["pb%d" % b, "cols"], nm("Tn%d" % (t + 1), hs), [b], bias=col(4 + t))
+
+        def outs(hs, e):
+            c, b, ob = rng(hs)[0], 2 + hs[0], T["ob%d" % t]
+            cc = slice(o + c.start, o + c.stop)
+            mm(ps[b][0:16, c], [(Mo, TB[:, cc])], ["Mo"] + nm("Tn%d" % (t + 1), hs), ["pb%d" % b], [b])
+            if e == "a":
+                act(ob[0:16, c], ps[b][0:16, c], F.Identity, ["pb%d" % b], nm("ob%d" % t, hs), [b])
+            else:
+                copy(ob[0:16, c], ps[b][0:16, c], ["pb%d" % b], nm("ob%d" % t, hs), [b])
+
+        def store(e1, e2):
+            ob, yc = T["ob%d" % t], slice(K * t, K * t + K)
+            dma(e1, T.yjump[:, yc], ob[8:16, :], nm("ob%d" % t, both))
+            dma(e2, T.ypar[:, yc], ob[0:8, :], nm("ob%d" % t, both))
+
+        def alt(hs):
+            c, a, b = rng(hs)
+            src = X[:, o + c.start:o + c.stop] if t == 0 else T.q1[:, c]
+            tt(T.W2[:, K + c.start:K + c.stop], win(X, t, T.off, a, b), src, A.add, Xr + qn + ["q1"] + nm("off", hs), nm("alt", hs))
+
+        if t == RO - 1:
+            gat(T.Gp, "Gp", TB, Tr, T.off, "off", h0)
+            thresh(1)
+            gat(T.Mp, "Mp", M, Mr, T.off, "off", h0, "v")
+            jl(h0)
+            newu(1, True)
+            gat(T.Gp, "Gp", TB, Tr, T.off, "off", h1)
+            jc(h0)
+            gat(T.Mp, "Mp", M, Mr, T.off, "off", h1, "v")
+            jl(h1)
+            gat(T.Gj, "Gj", TB, Tr, T.joff, "joff", h0)
+            bound1(h0)
+            jc(h1)
+            gat(T.Gj, "Gj", TB, Tr, T.joff, "joff", h1)
+            bound1(h1)
+            differ(h0)
+            table1(h0)
+            differ(h1, "v")
+            table1(h1)
+            table2(h0)
+            bound2(h0, "v")
+            table2(h1)
+            bound2(h1, "v")
+            bound3(h0, "v")
+            outs(h0, "a")
+            bound3(h1, "v")
+            outs(h1, "a")
+            store("a", "s")
+            break
+        msg, lmsg, qin = T["msg%d" % t], T["lmsg%d" % t], T["qin%d" % t]
+        grp = [h0, h1]
+        gat(T.Gp, "Gp", TB, Tr, T.off, "off", h0)
+        thresh(1)
+        cx(0)
+        newu(1, True)
+        gat(T.Gp, "Gp", TB, Tr, T.off, "off", h1)
+        cx(1)
+        gat(T.Mp, "Mp", M, Mr, T.off, "off", both)
+        px = ["px0", "px1"]
+        alt(h0)
+        ts(T.fail[:, 0:32], ps[0][:, 128:160], 7.5, A.is_lt, px, ["fail"], [0])
+        ts(T.nf[:, 0:32], ps[0][:, 128:160], 7.5, A.is_ge, px, ["nf"], [0], float(K), A.mult)
+        op("v", lambda: Ve.tensor_tensor_scan(T.cum[:, 1:33], T.fail[:, 0:32], T.fail[:, 0:32], 0.0, A.add, A.max), ["fail"], ["cum"])
+        tt(T.tt[:], T.nf[:], T.ci[:], A.min, ["nf", "nf32", "ci", "ci32"], ["tt"])
+        mm(ps[1][:, 128:161], [(T.tri[:], T.fail[:]), (T.blk[:], T.cum[:])], ["tri", "blk", "fail", "fail32", "cum", "cum0"], ["pp"], [1])
+        jl(both)
+        tt(msg[:], ps[1][:, 128:161], T.tt[:], A.add, ["pp", "tt"], ["msg%d" % t], [1])
+        send(lmsg[:], msg[:], "rm%d" % t, ["msg%d" % t], "lmsg%d" % t)
+        alt(h1)
+        jc(both)
+        for hs in grp:
+            gat(T.Gj, "Gj", TB, Tr, T.joff, "joff", hs)
+        tt(T.bb[:], ps[1][:, 128:160], T.nf[:, 0:32], A.add, ["pp", "nf"], ["bb"], [1])
+        if t == 0:
+            copy(T.wf[:], T.ws[:, 0:1], ["ws"], ["wf"])
+            act(T.Ew[:], T.E[:], F.Identity, ["E", "wf"], ["Ew"], scale=T.wf[:, 0:1])
+        bound1(both)
+        ts(T.kk[:], T.bb[:], CAP - 0.5, A.is_ge, ["bb"], ["kk"], (), 4096.0, A.mult)
+        ts(T.W2[:, K:], T.W2[:, K:], 255, A.bitwise_and, nm("alt", both), nm("alt", both))
+        tt(T.bb[:], T.bb[:], T.kk[:], A.max, ["bb", "kk"], ["bb"])
+        for hs in grp:
+            differ(hs)
+            table1(hs)
+        for hs in grp:
+            table2(hs)
+        for hs in grp:
+            bound2(hs, "a")
+        ln = "lmsg%d" % t
+        ts(T.yy[:], T.bb[:], lmsg[:, 32:33], A.is_ge, ["bb", ln], ["yy"], (), 4096.0, A.mult)
+        copy(T.soff[:], lmsg[:, 0:32], [ln], ["soff"])
+        tt(T.yy[:], T.yy[:], T.bb[:], A.max, ["yy", "bb"], ["yy"])
+        copy(T.W2[:, 0:K].indirect(T.soff[:, 0:32]), qin[:], ["soff", "qin%d" % t], ["come"])
+        tt(T.yy[:], T.yy[:], T.ai[:], A.min, ["yy", "ai"], ["yy"])
+        for hs in grp:
+            bound3(hs, "a")
+        copy(T.goff[:], T.yy[:], ["yy"], ["goff"])
+        for hs in grp:
+            outs(hs, "a")
+        store("s", "s")
+        q2 = nm("Xn%d" % (t + 2), both)
+        for h in both:
+            c0 = o + K + H * h
+            copy(X[:, c0:c0 + H], T.W2[:, 0:2 * K].indirect(T.goff[:, 16 * h:16 * h + 16]), ["come", "alt0", "alt1", "goff"], [q2[h]])
+            tolist(ps[h][:, 192:208], T.Ew, lambda i: X[:, c0 + i:c0 + H:16], ["Ew", q2[h]], ["ph%d" % h], [h])
+        if t + 1 < RO - 1:
+            send(T["qin%d" % (t + 1)][:], X[:, o + K:o + 2 * K], "rq%d" % (t + 1), q2, "qin%d" % (t + 1))
+    emit(g, T, ops)

@@ -4,52 +4,131 @@ V, K, CAP, S, RO = 2304, 512, 192, 5, 3
 W = V + RO * K
 H = K // 2
 BIG = 32768.0
-OPT = {"thr": 1}
+MID = 1920.0
+C0 = 12582912.0
+OPT = {"xa": 192, "x4": 0, "xn": 2, "bound": "aa", "mp": "av", "alt": "va", "ab": "aa", "lmp": "vv", "lab": "av", "lout": "a",
+       "line": ("S",), "mn": 1, "tbv": (3, 5, 7), "cyc": 0.95, "gat": 1.4, "sct": 3.5, "far": 250.0, "own": 100.0, "fly": 1900.0}
 BF, FP, I32, U16 = "bfloat16", "float32", "int32", "uint16"
 SCRATCH = {}
 for _dt, _w, _names in (
         (BF, [W], "X M TB"), (I32, [576], "raw loi"), (BF, [576], "hi lo"), (BF, [520], "R"), (BF, [144], "E Ew Ej"),
-        (BF, [128], "ones idn blk tri"), (BF, [64, 16], "rows"), (FP, [8], "cols"), (BF, [1040], "BM"),
-        (BF, [H, 4], "st0 st1"), (BF, [256], "d0"), (FP, [256], "so"), (U16, [32], "off joff soff goff"),
-        (I32, [32], "u0s hs"), (I32, [4], "ws"), (FP, [1], "wf"), (FP, [32], "i16 ai bb kk yy"), (BF, [33], "fail cum"),
-        (FP, [33], "ci nf tt msg0 msg1 lmsg0 lmsg1"), (I32, [2 * K], "W2"), (FP, [K], "ob0 ob1 ob2"),
-        (BF, [K], "bx qin0 qin1 q1 Gp Gj Mp t2 ab mr")):
+        (BF, [128], "ones idn blk tri triA n256"), (BF, [64, 16], "rows"), (FP, [8], "cols"), (BF, [1648], "BM"),
+        (BF, [H, 2], "st0 st1"), (BF, [K, 2], "sx0 sx1"), (FP, [128], "d0 idf nif"), (FP, [S, 128], "so"), (U16, [192], "off"),
+        (U16, [32], "poff joff goff"), (FP, [192], "po"), (FP, [64], "go"),
+        (I32, [32], "u0s hs"), (I32, [4], "ws"), (FP, [1], "wf got room"), (FP, [32], "i16 ai v0"),
+        (U16, [16], "ma0 ma1 la0 la1"), (U16, [17], "mb0 mb1 lb0 lb1"), (BF, [2 * K], "W2"), (FP, [128], "ob0 ob1 ob2"),
+        (BF, [K], "bx qin0 qin1 Gp Gj Mp Xp t2 ab mr xs wrap q1")):
     for _n in _names.split():
         SCRATCH[_n] = ("sbuf", [128] + _w, _dt)
 for _b in range(8):
     SCRATCH["ps%d" % _b] = ("psum", [128, 512], FP)
-SEMAPHORES = ["v", "a", "p", "g", "sent", "rq0", "rq1", "rm0", "rm1"] + ["d%d" % _i for _i in range(24)]
+SEMAPHORES = ["v", "a", "p", "g", "sent", "rq0", "rq1", "ra0", "ra1", "rb0", "rb1"] + ["d%d" % _i for _i in range(24)]
+ORDER = []
 
 
-def emit(g, T, ops):
-    Q = {"v": g.vector, "a": g.scalar, "p": g.tensor, "g": g, "s": g.sync}
-    lastw, readers, bank = {}, {}, {}
-    known = {e: {} for e in Q}
-    seq = {e: 0 for e in Q}
-    need = set()
+def needs(ops):
+    lastw, readers, out = {}, {}, []
     for i, o in enumerate(ops):
-        e = o["e"]
-        deps = set()
-        for r in o["r"]:
-            if r in lastw:
-                deps.add(lastw[r])
+        deps = set(lastw[r] for r in o["r"] + o["w"] if r in lastw)
         for r in o["w"]:
-            if r in lastw:
-                deps.add(lastw[r])
             deps.update(readers.get(r, []))
-        for b in o["b"]:
-            for e2, j in bank.get(b, {}).items():
-                if e2 != e:
-                    deps.add(j)
-            bank.setdefault(b, {})[e] = i
         for r in o["r"]:
             readers.setdefault(r, []).append(i)
         for r in o["w"]:
             lastw[r] = i
             readers[r] = []
+        out.append(deps - {i})
+    return out
+
+
+def arrange(ops):
+    n = len(ops)
+    pre = [[(j, OPT["own"] if ops[j]["e"] == ops[i]["e"] and ops[j]["kind"] == "op" else OPT["far"]) for j in d] for i, d in enumerate(needs(ops))]
+    inorder, tags = {}, {}
+    for i, o in enumerate(ops):
+        for k in o.get("line", ()):
+            if k in tags:
+                pre[i].append((tags[k], 0.0))
+            tags[k] = i
+        if o["kind"] == "arrive":
+            pre[i].append((i - 1, 0.0))
+        elif o["kind"] != "op":
+            if o["e"] in inorder:
+                pre[i].append((inorder[o["e"]], -1e6))
+            inorder[o["e"]] = i
+    chain = [0.0] * n
+    for i in range(n - 1, -1, -1):
+        chain[i] += ops[i]["c"] + ops[i]["late"]
+        for j, d in pre[i]:
+            chain[j] = max(chain[j], max(d, -ops[j]["late"]) + chain[i])
+    start, end, free, bank, pipe = {}, {}, {}, {}, [0.0]
+    todo = list(range(n))
+    while todo:
+        est, ready = {}, []
+        for i in todo[:160]:
+            o, ok = ops[i], True
+            t = free.get(o["e"], 0.0)
+            for j, d in pre[i]:
+                if j in end:
+                    t = max(t, end[j] + d)
+                else:
+                    ok = False
+                    t = max(t, est[j] + ops[j]["c"] + ops[j]["late"] + d)
+            for b in o["b"]:
+                if b in bank and bank[b][0] != o["e"]:
+                    t = max(t, bank[b][1] + OPT["far"])
+            est[i] = t
+            if ok:
+                ready.append(i)
+        ready.sort(key=lambda i: (est[i], -chain[i]))
+        pick = None
+        for i in ready:
+            a, c = est[i], ops[i]["c"]
+            if not any(ops[h]["e"] == ops[i]["e"] and h != i and est[h] < a + c and chain[h] > chain[i]
+                       and max(est[h] + chain[h], est[h] + ops[h]["c"] + chain[i]) < max(a + chain[i], a + c + chain[h]) for h in est):
+                pick = i
+                break
+        if pick is None:
+            pick = max(ready, key=lambda i: chain[i] - est[i])
+        o = ops[pick]
+        start[pick] = est[pick]
+        end[pick] = free[o["e"]] = est[pick] + o["c"]
+        if o["kind"] == "dma":
+            pipe[0] = max(pipe[0], end[pick] + 800.0) + o["late"] - 1300.0
+            end[pick] = pipe[0] + 500.0
+        elif o["kind"] == "send":
+            end[pick] += o["late"]
+        if o["e"] is None:
+            free[None] = 0.0
+        for b in o["b"]:
+            bank[b] = (o["e"], end[pick])
+        todo.remove(pick)
+    return list(start)
+
+
+def emit(g, T, ops):
+    Q = {"v": g.vector, "a": g.scalar, "p": g.tensor, "g": g, "s": g.sync}
+    before = needs(ops)
+    if not ORDER:
+        ORDER.extend(arrange(ops))
+    order = ORDER
+    place = {i: k for k, i in enumerate(order)}
+    bank = {}
+    known = {e: {} for e in Q}
+    seq = {e: 0 for e in Q}
+    need = set()
+    for i in order:
+        o = ops[i]
+        e = o["e"]
+        deps = set(before[i])
+        for b in o["b"]:
+            for e2, j in bank.get(b, {}).items():
+                if e2 != e:
+                    deps.add(j)
+            bank.setdefault(b, {})[e] = i
         o["waits"] = []
         if e is not None:
-            for j in sorted(deps, reverse=True):
+            for j in sorted(deps, key=lambda j: -place[j]):
                 key, n = ops[j]["id"]
                 if known[e].get(key, 0) >= n:
                     continue
@@ -66,7 +145,8 @@ def emit(g, T, ops):
         o["clock"] = dict(known[e]) if e is not None else {}
         o["clock"][o["id"][0]] = o["id"][1]
     total, waited = {}, {}
-    for i, o in enumerate(ops):
+    for i in order:
+        o = ops[i]
         if o["sem"] is None:
             if i in need:
                 total[o["e"]] = total.get(o["e"], 0) + 1
@@ -74,7 +154,8 @@ def emit(g, T, ops):
         else:
             total[o["sem"]] = total.get(o["sem"], 0) + o["n"]
             o["sig"] = (o["sem"], total[o["sem"]])
-    for i, o in enumerate(ops):
+    for i in order:
+        o = ops[i]
         if o["e"] is None:
             continue
         for j in o["waits"]:
@@ -102,56 +183,70 @@ def rank_program(g, core, T, topo):
     Ve, Sc, Pe = g.vector, g.scalar, g.tensor
     ops, nd = [], [0]
     ps = [T["ps%d" % b] for b in range(8)]
-    st = [T.st0, T.st1]
-    X, M, TB = T.X, T.M, T.TB
+    st, sx = [T.st0, T.st1], [T.sx0, T.sx1]
+    X, M, TB, BM = T.X, T.M, T.TB, T.BM
+    cyc = OPT["cyc"]
 
-    def op(e, f, r=(), w=(), b=()):
-        ops.append({"e": e, "f": f, "r": list(r), "w": list(w), "b": list(b), "sem": None, "kind": "op"})
+    def op(e, f, r=(), w=(), b=(), n=0, gat=0, sct=0):
+        c = cyc * max(n, 64) + 10
+        if gat or sct:
+            c = cyc * (gat * OPT["gat"] + sct * OPT["sct"]) + (50 if e == "v" else 65)
+        ops.append({"e": e, "f": f, "r": list(r), "w": list(w), "b": list(b), "sem": None, "kind": "op", "c": c, "late": 0.0})
 
-    def dma(e, out, in_, r=(), w=()):
+    def dma(e, out, in_, size, r=(), w=()):
         q = g.sync if e == "s" else g.scalar
         ops.append({"e": e, "f": lambda: q.dma_start(out, in_), "r": list(r), "w": list(w), "b": [],
-                    "sem": "d%d" % nd[0], "n": 16, "kind": "dma"})
+                    "sem": "d%d" % nd[0], "n": 16, "kind": "dma", "c": 60.0, "late": 1500.0 + size / 250.0})
         nd[0] += 1
 
-    def send(out, in_, sem, r, land):
+    def send(out, in_, size, sem, r, land):
         ops.append({"e": "g", "f": lambda: g.remote_dma(out, in_, T.sem[sem], T.sem.sent, pid, rid, mask),
-                    "r": list(r), "w": [], "b": [], "sem": "sent", "n": n_out, "kind": "send"})
-        ops.append({"e": None, "r": [], "w": [land], "b": [], "sem": sem, "n": n_in, "kind": "arrive"})
+                    "r": list(r), "w": [], "b": [], "sem": "sent", "n": n_out, "kind": "send", "c": 300.0, "late": OPT["fly"] + size / 128.0})
+        ops.append({"e": None, "r": [], "w": [land], "b": [], "sem": sem, "n": n_in, "kind": "arrive", "c": 0.0, "late": 0.0})
 
-    def mm(out, pairs, r, w, b, start=True, stop=True):
+    def mm(out, pairs, r, w, b, n=64, start=True, stop=True, line=True):
         def f():
             for i, (l, x) in enumerate(pairs):
                 ins = Pe.matmul(out, l, x, start and i == 0, stop and i == len(pairs) - 1)
             return ins
-        op("p", f, r, w, b)
+        op("p", f, r, w, b, len(pairs) * max(n, 64) / 2)
+        ops[-1]["line"] = b if line else ()
 
-    def tolist(out, lh, rhs, r, w, b):
-        mm(out, [(lh[:, 15 - i:143 - i], rhs(i)) for i in range(16)], r, w, b)
+    def turns(lh, rhs):
+        return [(lh[:, 15 - i:143 - i], rhs(i)) for i in range(16)]
 
-    def memset(ap, c, w, b=()):
-        op("v", lambda: Ve.memset(ap, c), (), w, b)
+    def memset(ap, c, w, n=0):
+        op("v", lambda: Ve.memset(ap, c), (), w, (), n)
 
-    def act(out, in_, fn, r, w, b=(), bias=0.0, scale=1.0):
-        op("a", lambda: Sc.activation(out, in_, fn, bias=bias, scale=scale), r, w, b)
+    def act(out, in_, fn, r, w, b=(), bias=0.0, scale=1.0, n=0, gat=0):
+        op("a", lambda: Sc.activation(out, in_, fn, bias=bias, scale=scale), r, w, b, n, gat)
 
-    def copy(out, in_, r, w, b=()):
-        op("v", lambda: Ve.tensor_copy(out, in_), r, w, b)
+    def copy(out, in_, r, w, b=(), n=0, gat=0, sct=0):
+        op("v", lambda: Ve.tensor_copy(out, in_), r, w, b, n, gat, sct)
 
-    def tt(out, a, c, f, r, w, b=()):
-        op("v", lambda: Ve.tensor_tensor(out, a, c, f), r, w, b)
+    def tt(out, a, c, f, r, w, b=(), n=0, gat=0):
+        op("v", lambda: Ve.tensor_tensor(out, a, c, f), r, w, b, n, gat)
 
-    def ts(out, a, s1, f1, r, w, b=(), s2=None, f2=None):
+    def ts(out, a, s1, f1, r, w, b=(), n=0, s2=None, f2=None):
         if f2 is None:
-            op("v", lambda: Ve.tensor_scalar(out, a, s1, None, f1), r, w, b)
+            op("v", lambda: Ve.tensor_scalar(out, a, s1, None, f1), r, w, b, n)
         else:
-            op("v", lambda: Ve.tensor_scalar(out, a, s1, s2, f1, f2), r, w, b)
+            op("v", lambda: Ve.tensor_scalar(out, a, s1, s2, f1, f2), r, w, b, n)
 
-    def sel(out, in_, pat, cmp, fill, base, cm, r, w):
-        op("g", lambda: g.affine_select(out, in_, pat, cmp, fill, base, cm), r, w)
+    def scan(out, a, c, first, f1, f2, r, w, b=(), n=0):
+        op("v", lambda: Ve.tensor_tensor_scan(out, a, c, first, f1, f2), r, w, b, n)
 
-    def put(ap, pat, base, val, name):
-        sel(ap, ap, pat, A.not_equal, val, base, 1, [name], [name])
+    def iota(out, pat, base, cm, r, w, n, small=True):
+        if small:
+            op("g", lambda: g.iota(out, pat, base, cm, allow_small_or_imprecise_dtypes=True), r, w, (), 2 * n + 140)
+        else:
+            op("g", lambda: g.iota(out, pat, base, cm), r, w, (), 2 * n + 140)
+
+    def sel(out, in_, pat, cmp, fill, base, cm, r, w, n=128):
+        op("g", lambda: g.affine_select(out, in_, pat, cmp, fill, base, cm), r, w, (), 2 * n + 180)
+
+    def put(ap, pat, base, val, name, n=16):
+        sel(ap, ap, pat, A.not_equal, val, base, 1, [name], [name], n)
 
     def col(k):
         return T.cols[:, k:k + 1]
@@ -162,348 +257,305 @@ def rank_program(g, core, T, topo):
     def win(B, t, offs, a, b):
         return B[:, 0:V + K * t].indirect(offs[:, a:b])
 
+    def nm(n, hs):
+        return [n + str(h) for h in hs]
+
+    def part(base):
+        return lambda a, b, step=1: BM[:, base + a:base + b:step]
+    fl, dv, fail, cum, prod, cc = part(1040), part(1232), part(1344), part(1384), part(1424), part(1464)
+    crow0, crow1 = BM[0:1, 1296:1312], BM[0:1, 1312:1344]
+    dl = ps[7]
+    both = (0, 1)
+
     for k, src in enumerate((T.par, T.jump, T.ln)):
-        dma("a" if k == 1 else "s", T.raw[32 * k:32 * k + 32, :], src[:], w=["raw%d" % k])
-    dma("a", T.u0s[:], T.u0[:], w=["u0s"])
-    dma("a", X[:, V:V + K], T.q[:], w=["Xn10", "Xn11"])
-    dma("s", X[:, 0:V], T.x[:], w=["Xn0"])
-    dma("a", M[:, 0:V], T.m[:], w=["Mn0"])
-    dma("s", T.ws[:, 0:1], T.w[:], w=["ws"])
-    Rf = (0, 1, 2, 3, 4, 6, 7)
+        dma("a" if k == 1 else "s", T.raw[32 * k:32 * k + 32, :], src[:], 32 * V, w=["raw%d" % k])
+    dma("a", T.u0s[:], T.u0[:], 128 * 128, w=["u0s"])
+    dma("a", X[:, V:V + K], T.q[:], 256 * K, w=["Xn10", "Xn11"])
+    dma("s", M[:, 0:V], T.m[:], 256 * V, w=["Mn0"])
+    dma("s", X[:, 0:V], T.x[:], 256 * V, w=["Xn0"])
+    dma("s", T.ws[:, 0:1], T.w[:], 512, w=["ws"])
+    Rf = (0, 2, 4, 5)
     Rn = ["R%d" % f for f in Rf]
-    op("g", lambda: g.iota(T.raw[96:128, :], [[1, 576]], 0, 576), w=["raw3"])
+    iota(T.raw[96:128, :], [[1, 576]], 0, 576, [], ["raw3"], 576, False)
     memset(T.ones[:], 1.0, ["ones"])
-    memset(T.R[:], 0.0, Rn)
-    memset(T.rows[0:1, 0:56, :], 0.0, ["row%d" % k for k in range(12)])
-    memset(T.E[:], 0.0, ["E"])
-    op("g", lambda: g.iota(T.rows[0:1, 56:64, :], [[0, 8], [1, 16]], 0, 0, allow_small_or_imprecise_dtypes=True), ["raw3"], ["row12"])
-    for f, k in zip(Rf, (0, 0, 1, 2, 3, 1, 0)):
-        sel(T.R[:, 8 + f:520:16], T.ones[:, 0:32], [[-1, 4], [0 if k == 3 else -4, 8]], A.is_equal, 0.0, -32 * k, 1, ["ones"], ["R%d" % f])
-    sel(T.E[:, 15::16], T.ones[:, 0:9], [[-16, 9]], A.is_ge, 0.0, 0, 1, ["ones"], ["E"])
-    op("g", lambda: g.iota(T.i16[:], [[16, 32]], K, 0, allow_small_or_imprecise_dtypes=True), w=["i16"])
-    sel(T.E[:, 15::16], T.E[:, 15::16], [[16, 9]], A.is_ge, 0.0, 15, -1, ["E"], ["E"])
-    segs = [(0, 2, 0, 8, 1.0), (0, 2, 1, 8, -1.0), (0, 3, 2, 8, 1.0), (2, 3, 1, 8, 1.0), (0, 1, 4, 8, -1.0),
-            (0, 1, 6, 8, -1.0), (0, 1, 7, 8, 1.0), (4, 7, 13, 16, 1.0)] + [(4 + t, 5 + t, 4, 16, float(V + K * t)) for t in range(RO)]
+    memset(T.R[:], 0.0, Rn, 260)
+    segs = [(0, 1, 0, 8, 1.0), (0, 1, 1, 8, 4096.0), (0, 1, 2, 8, 4096.0), (0, 1, 3, 8, -4096.0),
+            (1, 2, 0, 16, -MID), (1, 2, slice(1, 3), 0, -MID * 4096), (1, 2, 3, 16, MID * 4096),
+            (2, 3, 1, 8, 1.0), (2, 3, 2, 8, 1.0), (2, 3, 3, 8, -1.0), (3, 4, slice(0, 6, 2), 0, -4128.0),
+            (3, 4, 5, 16, -4128.0), (4, 7, 14, 16, 1.0)]
+    segs += [(4 + t, 5 + t, 5, 16, float(V + K * t)) for t in range(RO)]
+    rown = ["row%d" % k for k in range(len(segs))]
+    memset(T.rows[0:1, 0:56, :], 0.0, rown, 448)
+    memset(T.E[:], 0.0, ["E"], 72)
+    iota(T.rows[0:1, 56:64, :], [[0, 8], [1, 16]], 0, 0, ["raw3"], ["rowp"], 128)
+    for k, f in enumerate(Rf):
+        sel(T.R[:, 8 + f:520:16], T.ones[:, 0:32], [[-1, 4], [0 if k == 3 else -4, 8]], A.is_equal, 0.0, -32 * k, 1, ["ones"], ["R%d" % f], 32)
+    sel(T.E[:, 15::16], T.ones[:, 0:9], [[-16, 9]], A.is_ge, 0.0, 0, 1, ["ones"], ["E"], 9)
+    iota(T.i16[:], [[16, 32]], 0, 0, [], ["i16"], 32)
+    sel(T.E[:, 15::16], T.E[:, 15::16], [[16, 9]], A.is_ge, 0.0, 15, -1, ["E"], ["E"], 9)
     for i, (a, b, f, step, c) in enumerate(segs):
-        memset(T.rows[0:1, 8 * a:8 * b, f::step], c, ["row%d" % i])
-    memset(T.rows[0:1, 24:32, 0:8], -4128.0, ["row11"])
-    memset(T.d0[:], 0.0, ["d00", "d01"])
-    names = ["SLp", "SLn", "Mc1", "Mc2", "Mc3", "Ma0", "Ma1", "Ma3", "Ma7", "Mb", "Ms", "Zc", "Mo", "Ni"]
-    memset(T.BM[:], 0.0, names)
-    memset(T.cum[:, 0:1], 0.0, ["cum0"])
-    memset(T.nf[:, 32:33], 0.0, ["nf32"])
-    memset(T.ci[:, 32:33], 0.0, ["ci32"])
+        memset(T.rows[0:1, 8 * a:8 * b, slice(f, 16, step) if step else f], c, [rown[i]])
 
     def turn():
         for k in range(8):
             ins = Pe.matmul(ps[7][:, 300 + k:301 + k], T.rows[0:1, 8 * k:8 * k + 8, :], T.ones[0:1, 0:1], True, True)
         return ins
-    op("p", turn, ["ones"] + ["row%d" % k for k in range(13)], ["pc"], [7])
-    act(T.d0[:, 2::8], T.ones[:, 0:32], F.Sigmoid, ["ones"], ["d00", "d01"], scale=400.0)
-    act(T.cols[:], ps[7][:, 300:308], F.Identity, ["pc"], ["cols"], [7])
+    op("p", turn, ["ones", "rowp"] + rown, ["pu7"], [7], 256)
+    op("a", lambda: Sc.activation(T.d0[:, 1::4], T.ones[:, 0:32], F.Sigmoid, scale=400.0), ["ones"], ["d0c"], (), 1400)
+    act(T.cols[:], ps[7][:, 300:308], F.Identity, ["pu7", "d0c"], ["cols"], [7])
+    act(T.d0[:, 0::4], T.ones[:, 0:32], F.Identity, ["ones"], ["d0a"], scale=0.0)
+    act(T.d0[:, 2::4], T.ones[:, 0:32], F.Identity, ["ones"], ["d0b"], scale=-4097.0)
+    for h in both:
+        act(ps[h][:, 1:64:4], T.ones[:, 0:16], F.Identity, ["ones"], ["pk%d" % h], [h], scale=-C0)
     raws = ["raw%d" % k for k in range(4)]
-    for hf in range(2):
+    for hf in both:
         c = slice(288 * hf, 288 * hf + 288)
-        ts(T.loi[:, c], T.raw[:, c], 31, A.bitwise_and, raws, ["loi%d" % hf])
-        ts(T.hi[:, c], T.raw[:, c], 4112.5, A.add, raws, ["hi%d" % hf])
-        copy(T.lo[:, c], T.loi[:, c], ["loi%d" % hf], ["lo%d" % hf])
-    copy(T.off[:], T.u0s[:], ["u0s"], ["off0", "off1"])
-    for h in range(2):
-        memset(ps[h][:, 0:128], 0.0, ["pu%d" % h, "pe%d" % h], [h])
-    memset(T.fail[:, 32:33], 0.0, ["fail32"])
-    for h in range(2):
-        copy(ps[h][:, 3:128:8], T.u0s[:, 16 * h:16 * h + 16], ["u0s"], ["pu%d" % h], [h])
+        ts(T.loi[:, c], T.raw[:, c], 31, A.bitwise_and, raws, ["loi%d" % hf], n=288)
+        ts(T.hi[:, c], T.raw[:, c], 4112.5, A.add, raws, ["hi%d" % hf], n=288)
+        copy(T.lo[:, c], T.loi[:, c], ["loi%d" % hf], ["lo%d" % hf], n=288)
+    copy(T.off[:, 0:32], T.u0s[:], ["u0s"], ["off00", "off01"])
+    Mcn, Man, Mbn = nm("Mc", (2, 3, 4)), nm("Ma", (0, 1, 3, 4)), ["Mb2"]
+    memset(BM[:, 0:768], 0.0, Mcn + Man + Mbn + ["Ms", "Mo", "Mo2", "SLp"], 384)
+    memset(BM[:, 768:1648], 0.0, ["Zc", "Ni", "zero", "crow0", "crow1", "cc0", "cc1", "SLn"], 440)
+    SLp, SLn = BM[:, 0:128], BM[:, 1520:1648]
     parts = []
-    for hf in range(2):
+    for hf in both:
         for c in range(4):
             i = 4 * hf + c
             b = 2 + i % 6
             cs = slice(288 * hf, 288 * hf + 288)
+            wide = ["pb%d" % b, "pu%d" % b]
             mm(ps[b][:, 0:288], [(T.R[:, 8 + 128 * c:136 + 128 * c], T.hi[:, cs]), (T.R[:, 128 * c:128 * c + 128], T.lo[:, cs])],
-               Rn + ["hi%d" % hf, "lo%d" % hf], ["pb%d" % b], [b])
+               Rn + ["hi%d" % hf, "lo%d" % hf], wide, [b], 288)
             out = TB[:, 576 * c + 288 * hf:576 * c + 288 * hf + 288]
-            if i in (3, 5, 7):
-                ts(out, ps[b][:, 0:288], col(3), A.add, ["pb%d" % b, "cols"], ["tb%d" % i], [b])
+            if i in OPT["tbv"]:
+                ts(out, ps[b][:, 0:288], col(3), A.add, wide + ["cols"], ["tb%d" % i], [b], 288)
             else:
-                act(out, ps[b][:, 0:288], F.Identity, ["pb%d" % b, "cols"], ["tb%d" % i], [b], bias=col(3))
+                act(out, ps[b][:, 0:288], F.Identity, wide + ["cols"], ["tb%d" % i], [b], bias=col(3), n=288)
             parts.append("tb%d" % i)
-    act(T.ai[:], T.i16[:], F.Identity, ["i16", "cols"], ["ai"], bias=col(7))
-    act(T.Ej[:], T.E[:], F.Identity, ["E", "cols"], ["Ej"], scale=col(1))
-    act(T.ci[:, 0:32], T.ai[:], F.Identity, ["ai"], ["ci"], bias=float(2 * K - 1), scale=-1.0)
-    send(T.qin0[:], X[:, V:V + K], "rq0", ["Xn10", "Xn11", "Xn0", "Mn0"], "qin0")
-    SLp, SLn, Mc, Ma, Mb, Ms, Zc, Ni = [T.BM[:, 128 * k:128 * k + 128] for k in range(8)]
-    Mo, Mo2 = T.BM[:, 1024:1040], T.BM[:, 1032:1040]
+    Mc, Ma, Mb, Ms, Zc, Ni = [BM[:, 128 * k:128 * k + 128] for k in range(2, 8)]
+    Mo1, Mo2 = BM[:, 131:163:4], BM[:, 163:195:4]
 
     def bm(k, f, step):
-        return T.BM[:, 128 * k + f:128 * k + 128:step]
-    sel(T.blk[:], T.ones[:], [[-16, 8], [0, 16]], A.is_ge, 0.0, 0, 1, ["ones"], ["blk"])
+        return BM[:, 128 * k + f:128 * k + 128:step]
     sel(T.idn[:], T.ones[:], [[-1, 128]], A.is_equal, 0.0, 0, 1, ["ones"], ["idn"])
+    sel(T.idf[:], T.ones[:], [[-1, 128]], A.is_equal, 0.0, 0, 1, ["ones"], ["idf"])
+    sel(T.blk[:], T.ones[:], [[-16, 8], [0, 16]], A.is_ge, 0.0, 0, 1, ["ones"], ["blk"])
+    put(Ni, [[-1, 128]], 0, -1.0, "Ni", 128)
     sel(T.blk[:], T.blk[:], [[16, 8], [0, 16]], A.is_ge, 0.0, 15, -1, ["blk"], ["blk"])
-    put(Zc, [[-16, 8], [0, 16]], 0, -BIG, "Zc")
+    sel(T.nif[:], T.idf[:], [[-1, 128]], A.not_equal, -1.0, 0, 1, ["idf"], ["nif"])
+    sel(T.n256[:], T.idn[:], [[-1, 128]], A.not_equal, -256.0, 0, 1, ["idn"], ["n256"])
+    put(Zc, [[-16, 8], [0, 16]], -6, -BIG, "Zc", 128)
     sel(T.tri[:], T.blk[:], [[16, 8], [1, 16]], A.is_ge, 0.0, -1, -1, ["blk"], ["tri"])
-    put(Ni, [[-1, 128]], 0, -1.0, "Ni")
-    for i, f in enumerate((3, 11, 13)):
-        put(bm(0, 0, 16), [[-16, 8]], -f, 1.0, "SLp")
-        put(bm(1, 0, 16), [[-16, 8]], -f, -1.0, "SLn")
-        step = 8 if i == 0 else 4
-        put(bm(2, i + 1, step), [[-16, 8], [0, 16 // step]], 0, -BIG, "Mc%d" % (i + 1))
-        put(bm(4, 2, 4), [[-8, 16], [0, 2]], -i, (1.0, -1.0, 1.0)[i], "Mb")
-        if i < 2:
-            put(Mo, [[0, 2], [-16, 8]], -8 * i, 1.0, "Mo")
-    put(bm(3, 3, 8), [[-8, 16]], -3, 2.0, "Ma3")
-    put(Mo2, [[-16, 8]], -2, 1.0, "Mo")
-    put(bm(3, 0, 8), [[-8, 16]], -4, 1.0, "Ma0")
-    put(Mo2, [[-16, 8]], -10, 1.0, "Mo")
-    put(bm(3, 1, 8), [[-8, 16]], -4, 1.0, "Ma1")
-    put(Mo2, [[-16, 8]], -1, -1.0, "Mo")
-    put(bm(3, 11, 16), [[-16, 8]], -13, 2.0, "Ma3")
-    put(bm(3, 7, 8), [[-8, 16]], -4, 1.0, "Ma7")
-    put(Mo2, [[-16, 8]], -9, -1.0, "Mo")
-    put(bm(5, 4, 8), [[-8, 16]], -4, 1.0, "Ms")
-    both, h0, h1 = (0, 1), (0,), (1,)
+    sel(T.triA[:], T.tri[:], [[-1, 128]], A.not_equal, -float(H), 0, 1, ["tri"], ["triA"])
+    for i, f in enumerate((4, 12, 14)):
+        put(BM[:, 6:128:16], [[-16, 8]], -f, 1.0, "SLp")
+        put(BM[:, 902 + 624:1024 + 624:16], [[-16, 8]], -f, -1.0, "SLn")
+        put(bm(2, i + 2, 8), [[-16, 8], [0, 2]], -6, -BIG, "Mc%d" % (i + 2))
+        put(bm(4, 2, 8), [[-8, 16]], -1 - i, (1.0, 1.0, -1.0)[i], "Mb2")
+        put(bm(3, (0, 1, 3)[i], 8), [[-8, 16]], -5, 1.0, "Ma%d" % (0, 1, 3)[i])
+        for d in (0, 8):
+            put(Mo2, [[-16, 8]], -1 - i - d, (1.0, 1.0, -1.0)[i], "Mo2")
+            if i == 0:
+                put(Mo1, [[-16, 8]], -d, 1.0, "Mo")
+    put(bm(3, 4, 8), [[-8, 16]], -4, 2.0, "Ma4")
+    put(bm(5, 5, 8), [[-8, 16]], -5, 1.0, "Ms")
+    put(bm(3, 12, 16), [[-16, 8]], -14, 2.0, "Ma4")
+    send(T.qin0[:], X[:, V:V + K], 256 * K, "rq0", ["Xn10", "Xn11", "Xn0", "Mn0"], "qin0")
+    act(T.ai[:], T.i16[:], F.Identity, ["i16", "cols"], ["ai"], bias=col(7))
+    act(T.Ej[:], T.E[:], F.Identity, ["E", "cols"], ["Ej"], scale=col(2), n=144)
+    for h in both:
+        act(cc(16 * h, 16 * h + 16), T.ai[:, 0:16], F.Identity, ["ai"], ["cc%d" % h], bias=H - 1.0, scale=-1.0)
+    act(T.ai[:], T.ai[:], F.Identity, ["ai"], ["ai"], bias=K - CAP + 0.5)
+    act(crow0, T.ones[0:1, 0:16], F.Identity, ["ones"], ["crow0"], scale=float(H))
+    act(crow1, T.ones[0:1, 0:32], F.Identity, ["ones"], ["crow1"], scale=H - CAP + 0.5)
+    copy(T.wf[:], T.ws[:, 0:1], ["ws"], ["wf"])
+    act(T.Ew[:], T.E[:], F.Identity, ["E", "wf"], ["Ew"], scale=T.wf[:, 0:1], n=144)
 
-    def nm(n, hs):
-        return [n + str(h) for h in hs]
-
-    def rng(hs):
-        return slice(H * hs[0], H * hs[-1] + H), 16 * hs[0], 16 * hs[-1] + 16
-
-    for t in range(RO):
+    def one_round(t):
         o = V + K * t
+        last = t == RO - 1
         Xr, Mr, Tr = ["X" + n for n in xr(t)], ["M" + n for n in xr(t)], parts + ["T" + n for n in xr(t)[1:]]
         qn = nm("Xn%d" % (t + 1), both)
 
         def q(h):
             return X[:, o + H * h:o + H * h + H]
 
-        def gx(h):
-            tt(st[h][:, :, 3], win(X, t, T.off, 16 * h, 16 * h + 16), q(h), A.is_ge, Xr + [qn[h], "off%d" % h], ["sx%d" % h])
+        def half(B, h):
+            return B[:, H * h:H * h + H]
 
-        def gm(h):
-            tt(st[h][:, :, 2], win(M, t, T.off, 16 * h, 16 * h + 16), q(h), A.is_ge, Mr + [qn[h], "off%d" % h], ["sm%d" % h])
+        def at(B, offs, a):
+            return win(B, t, offs, a, a + 16)
 
-        def g1(h):
-            act(st[h][:, :, 1], win(TB, t, T.off, 16 * h, 16 * h + 16), F.Identity, Tr + ["cols", "off%d" % h], ["se%d" % h], scale=col(0))
+        def node(s, h):
+            return T.so[:, s, 64 * h + 3:64 * h + 64:4]
 
-        def g2(h):
-            act(st[h][:, :, 0], st[h][:, :, 1], F.Identity, ["se%d" % h, "cols"], ["sd%d" % h], scale=col(2))
+        def xtest(s):
+            n, b, out = OPT["x4" if s == S - 1 else "xa"], 4 + s % 2, sx[s // 2 % 2]
+            cut = [32 * ((K - n) // 32 * i // OPT["xn"]) for i in range(OPT["xn"] + 1)]
+            for i, (a, e) in enumerate(zip(cut, cut[1:])):
+                tt(out[:, a:e, s % 2], win(X, t, T.off, 32 * s + a // 16, 32 * s + e // 16), X[:, o + a:o + e], A.is_ge,
+                   Xr + qn + nm("off%d" % s, both if e > H else (0,)), ["sx%d%d" % (s % 4, i)], gat=e - a)
+            if n:
+                act(T.xs[:, 0:n], win(X, t, T.off, 32 * s + (K - n) // 16, 32 * s + 32), F.Identity, Xr + ["off%d1" % s], ["xs"], gat=n)
+                mm(ps[b][:, 0:n], [(Ni, X[:, o + K - n:o + K]), (T.idn[:], T.xs[:, 0:n])], ["Ni", "idn", "xs"] + qn, ["pb%d" % b], [b], n)
+                act(out[:, K - n:K, s % 2], ps[b][:, 0:n], F.Sigmoid, ["pb%d" % b], ["sx%d9" % (s % 4)], [b], bias=200.0, scale=400.0, n=n)
 
-        def pe(h):
-            tolist(ps[h][:, 0:128:2], T.E, lambda i: st[h][:, i::16, :], ["E"] + [n + str(h) for n in ("sx", "sm", "se", "sd")], ["pe%d" % h], [h])
+        def xsum(s0, n):
+            B, b = sx[s0 // 2 % 2], 2 + s0 // 2 % 2
+            mm(ps[b][:, 0:32 * n], turns(T.E, lambda i: B[:, i::16, 0:n]),
+               ["E"] + ["sx%d%d" % (s % 4, i) for s in range(s0, s0 + n) for i in list(range(OPT["xn"])) + [9]], ["pb%d" % b], [b])
+            for s in range(s0, s0 + n):
+                act(fl(5 - s, 192, 6), ps[b][:, s % 2:32 * n:n], F.Sigmoid, ["pb%d" % b, "zero"], ["fl%d" % (5 - s)], [b], bias=3000.0, scale=-400.0)
 
-        def thresh(h, e="a"):
-            a, b = T.d0[:, 128 * h + 1:128 * h + 125:2], ps[h][:, 4:128:2]
+        for s in range(S):
+            for h in both:
+                a, on = 32 * s + 16 * h, "off%d%d" % (s, h)
+                if s == 0 and t > 0:
+                    hs = T.hs[:, 16 * h:16 * h + 16]
+                    copy(hs, ps[h][:, 192:208], ["ph%d" % h], ["hs%d" % h], [h])
+                    ts(hs, hs, K - 1, A.bitwise_and, ["hs%d" % h], ["hs%d" % h])
+                    ts(T.off[:, a:a + 16], hs, float(o - K), A.add, ["hs%d" % h], [on])
+                act(st[h][:, :, 1], at(TB, T.off, a), F.Identity, Tr + ["cols", on], ["sz%d" % h], scale=col(0), bias=col(1), gat=H)
+                ops[-1]["line"] = OPT["line"]
+                n = H // OPT["mn"]
+                for i in range(OPT["mn"]):
+                    tt(st[h][:, n * i:n * i + n, 0], win(M, t, T.off, a + n * i // 16, a + (n * i + n) // 16), X[:, o + H * h + n * i:o + H * h + n * i + n],
+                       A.is_ge, Mr + [qn[h], on], ["sm%d%d" % (h, i)], gat=n)
+                mm(ps[h][:, 0:64:2], turns(T.E, lambda i: st[h][:, i::16, :]), ["E", "sz%d" % h] + nm("sm%d" % h, range(OPT["mn"])), ["pm%d" % h, "pz%d" % h], [h])
+            for h in both:
+                a = 32 * s + 16 * h
+                act(T.d0[:, 64 * h + 3:64 * h + 64:4], ps[h][:, 0:64:4], F.Sigmoid, ["pm%d" % h], ["d0%d" % h], [h], bias=-3000.0, scale=400.0)
+                ops[-1]["line"] = OPT["line"]
+                act(ps[h][:, 3:64:4], ps[h][:, 2:64:4], F.Identity, ["pz%d" % h], ["pj%d" % h], [h], bias=C0, scale=1 / 4096)
+                act(ps[h][:, 0:64:4], ps[h][:, 2:64:4], F.Identity, ["pz%d" % h], ["pm%d" % h], [h], bias=C0, scale=1 / 4096)
+                ops[-1]["line"] = OPT["line"]
+                scan(T.so[:, s, 64 * h:64 * h + 64], T.d0[:, 64 * h:64 * h + 64], ps[h][:, 0:64], 0.0, A.mult, A.add,
+                     ["d0a", "d0b", "d0c"] + [n + str(h) for n in ("d0", "pm", "pz", "pj", "pk")], ["so%d%d" % (s, h)], [h])
+                if s < S - 1 or not last:
+                    ts(T.off[:, a + 32:a + 48], node(s, h), MID - C0, A.add, ["so%d%d" % (s, h)], ["off%d%d" % (s + 1, h)])
+            xtest(s)
+            if s % 2 or s == S - 1:
+                xsum(s - s % 2, 1 + s % 2)
+            if s == 0:
+                ts(T.v0[:], T.hs[:] if t else T.u0s[:], C0 - MID + (o - K if t else 0), A.add, ["hs0", "hs1", "u0s"], ["v0"])
+            if s < S - 1:
+                a, an = (T.so[:, s - 1, 3::4], nm("so%d" % (s - 1), both)) if s else (T.v0[:], ["v0"])
+                now = nm("so%d" % s, both)
+                if s == 0:
+                    mm(dl[:, 5:192:6], [(T.idf[:], a)], ["idf"] + an + now, ["dl5", "pb7"], [7], 256)
+                mm(dl[:, 4 - s:192:6], [(T.nif[:], a), (T.idf[:], T.so[:, s, 3::4])], ["idf", "nif", "dl5"] + an + now, ["dl%d" % (4 - s)], [7], 256)
+        dls = ["dl00", "dl01"] + ["dl%d" % k for k in range(1, 6)]
+        fls = ["fl%d" % k for k in range(1, 6)]
+        for h in both:
+            tt(dl[:, 96 * h:96 * h + 96:6], node(S - 1, h), node(S - 2, h), A.subtract, ["so%d%d" % (S - 1, h), "so%d%d" % (S - 2, h), "dl5"], ["dl0%d" % h], [7])
+            c = slice(96 * h, 96 * h + 96)
+            scan(T.po[:, c], fl(c.start, c.stop), dl[:, c], 0.0, A.mult, A.add, ["zero", dls[h]] + dls[2:] + fls, ["po%d" % h], [7], 96)
+            ts(T.poff[:, 16 * h:16 * h + 16], T.po[:, 96 * h + 5:96 * h + 96:6], MID - C0, A.add, ["po%d" % h], ["poff%d" % h])
+
+        if not last:
+            msg, land, qin = [T["ma%d" % t], T["mb%d" % t]], [T["la%d" % t], T["lb%d" % t]], T["qin%d" % t]
+            for h in both:
+                a, b, n = 16 * h, 2 + h, 16 + h
+                tt(half(T.bx, h), at(X, T.off, 32 * S + a), q(h), A.is_ge, Xr + [qn[h], "off%d%d" % (S, h)], ["bx%d" % h], gat=H)
+                mm(ps[b][:, 64:80], [(T.n256[:], fl(96 * h + k, 96 * h + 96, 6)) for k in range(1, 6)], ["n256"] + fls, ["px%d" % h], [b], stop=False)
+                mm(ps[b][:, 64:80], turns(T.E, lambda i: T.bx[:, H * h + i:H * h + H:16]), ["E", "bx%d" % h], ["py%d" % h], [b], start=False)
+                ts(fail(a, a + 16), ps[b][:, 64:80], 7.5 - 256 * S, A.is_lt, ["px%d" % h, "py%d" % h, "zero"], ["fail%d" % h], [b])
+                scan(cum(a + 1, a + 17), fail(a, a + 16), fail(a, a + 16), cum(16, 17) if h else 0.0, A.add, A.max,
+                     ["fail%d" % h] + nm("cum", range(h)), ["cum%d" % h])
+                tt(prod(a, a + 16), fail(a, a + 16), cc(a, a + 16), A.mult, ["fail%d" % h, "cc%d" % h], ["prod%d" % h])
+                first = [] if h else [(T.ones[0:1, :], crow0)]
+                mm(ps[b][:, 96:96 + n], first + [(T.idn[:], cc(a, a + n)), (T.tri[:] if h else T.triA[:], fail(a, a + n)), (T.blk[:], cum(a, a + n)), (Ni, prod(a, a + n))],
+                   ["ones", "crow0", "idn", "cc%d" % h, "tri", "triA", "Ni", "blk", "fail%d" % h, "prod%d" % h] + nm("cum", range(h + 1)), ["pp%d" % h], [b])
+                copy(msg[h][:], ps[b][:, 96:96 + n], ["pp%d" % h], ["msg%d%d" % (t, h)], [b])
+                send(land[h][:], msg[h][:], 0, "r%s%d" % ("ab"[h], t), ["msg%d%d" % (t, h)], "land%d%d" % (t, h))
+
+        def gather(dst, name, B, Br, offs, on, h, e):
             if e == "a":
-                act(a, b, F.Sigmoid, ["pe%d" % h], ["d0%d" % h], [h], bias=3000.0, scale=-400.0)
+                act(half(dst, h), at(B, offs, 16 * h), F.Identity, Br + [on + str(h)], [name + str(h)], gat=H)
             else:
-                ts(a, b, 7.5, A.is_lt, ["pe%d" % h], ["d0%d" % h], [h])
+                copy(half(dst, h), at(B, offs, 16 * h), Br + [on + str(h)], [name + str(h)], gat=H)
 
-        def newu(h, last):
-            u, c = T.so[:, 128 * h + 3:128 * h + 128:8], slice(128 * h, 128 * h + 128)
-            op("v", lambda: Ve.tensor_tensor_scan(T.so[:, c], T.d0[:, c], ps[h][:, 0:128], 0.0, A.mult, A.add),
-               ["d0%d" % h, "pe%d" % h, "pu%d" % h], ["so%d" % h], [h])
-            copy(T.off[:, 16 * h:16 * h + 16], u, ["so%d" % h], ["off%d" % h])
-            if not last:
-                copy(ps[h][:, 3:128:8], u, ["so%d" % h], ["pu%d" % h], [h])
-
-        def start1(h):
-            copy(T.hs[:, 16 * h:16 * h + 16], ps[h][:, 192:208], ["ph%d" % h], ["hs%d" % h], [h])
-
-        def start2(h):
-            a, c = T.hs[:, 16 * h:16 * h + 16], float(o - K)
-            ts(a, a, K - 1, A.bitwise_and, ["hs%d" % h], ["hs%d" % h])
-            ts(T.off[:, 16 * h:16 * h + 16], a, c, A.add, ["hs%d" % h], ["off%d" % h])
-            ts(ps[h][:, 3:128:8], a, c, A.add, ["hs%d" % h], ["pu%d" % h], [h])
-
-        if t > 0:
-            start1(0)
-            start2(0)
-        for k in range(2 * S):
-            h = k % 2
-            gx(h)
-            g1(h)
-            if k == 0:
-                if t > 0:
-                    start1(1)
-            elif OPT["thr"] == 1:
-                thresh(1 - h)
-            g2(h)
-            if k > 0 and OPT["thr"] == 2:
-                thresh(1 - h)
-            gm(h)
-            pe(h)
-            if k > 0:
-                newu(1 - h, k == 2 * S - 1)
-            elif t > 0:
-                start2(1)
-            if k == 3 and t == 1:
-                act(T.q1[:], X[:, o:o + K], F.Identity, qn, ["q1"], bias=1.0)
-
-        def gat(dst, name, B, Br, offs, on, hs, e="a"):
-            c, a, b = rng(hs)
-            if e == "a":
-                act(dst[:, c], win(B, t, offs, a, b), F.Identity, Br + nm(on, hs), nm(name, hs))
+        ob = T["ob%d" % t]
+        for h in both:
+            a, b, b2 = 16 * h, 4 + h, 6 + h
+            Gp, Gj, ab, new = half(T.Gp, h), half(T.Gj, h), half(T.ab, h), slice(o + H * h, o + H * h + H)
+            G = ["Gp%d" % h, "Gj%d" % h]
+            gather(T.Gp, "Gp", TB, Tr, T.poff, "poff", h, "a")
+            mm(ps[h][:, 64:80], turns(T.Ej, lambda i: T.Gp[:, H * h + i:H * h + H:16]), ["Ej", G[0]], ["pl%d" % h], [h])
+            copy(T.joff[:, a:a + 16], ps[h][:, 64:80], ["pl%d" % h], ["joff%d" % h], [h])
+            gather(T.Gj, "Gj", TB, Tr, T.joff, "joff", h, "a")
+            gather(T.Mp, "Mp", M, Mr, T.poff, "poff", h, OPT["lmp" if last else "mp"][h])
+            tt(half(T.t2, h), at(M, T.joff, a), half(T.Mp, h), A.max, Mr + ["joff%d" % h, "Mp%d" % h], ["t2%d" % h], gat=H)
+            pt, tab, pd, dif = nm("pt%d" % h, range(3)), ps[b2][:, 0:H], ["pb%d" % b, "pd%d" % b], ps[b][:, 0:H]
+            mm(dif, [(SLp, Gp)], ["SLp", G[0]], pd[:1], [b], H, True, False)
+            mm(dif, [(SLn, Gj)], ["SLn", G[1]], pd[1:], [b], H, False, True)
+            mm(tab, ([] if last else [(Ms, TB[:, H * h:H * h + H])]) + [(Ma, Gp)], Man + ["Ms", G[0]] + parts, [pt[0], "pb%d" % b2] + (dls if h else []), [b2], H, True, False)
+            mm(tab, [(Mb, Gj)], Mbn + [G[1]], [pt[1]], [b2], H, False, False)
+            if OPT["lab" if last else "ab"][h] == "a":
+                act(ab, dif, F.Abs, pd, ["ab%d" % h], [b], n=H)
             else:
-                copy(dst[:, c], win(B, t, offs, a, b), Br + nm(on, hs), nm(name, hs))
-
-        def cx(h):
-            tt(T.bx[:, H * h:H * h + H], win(X, t, T.off, 16 * h, 16 * h + 16), q(h), A.is_ge, Xr + [qn[h], "off%d" % h], ["bx%d" % h])
-            tolist(ps[0][:, 128 + 16 * h:144 + 16 * h], T.E, lambda i: T.bx[:, H * h + i:H * h + H:16], ["E", "bx%d" % h], ["px%d" % h], [0])
-
-        def jl(hs):
-            c, a, b = rng(hs)
-            k = 2 + hs[0]
-            tolist(ps[k][:, a:b], T.Ej, lambda i: T.Gp[:, c.start + i:c.stop:16], ["Ej"] + nm("Gp", hs), ["pb%d" % k], [k])
-
-        def jc(hs):
-            c, a, b = rng(hs)
-            k = 2 + hs[0]
-            copy(T.joff[:, a:b], ps[k][:, a:b], ["pb%d" % k], nm("joff", hs), [k])
-
-        def bound1(hs):
-            c, a, b = rng(hs)
-            tt(T.t2[:, c], win(M, t, T.joff, a, b), T.Mp[:, c], A.max, Mr + nm("joff", hs) + nm("Mp", hs), nm("t2", hs))
-
-        def differ(hs, e="a"):
-            c, b = rng(hs)[0], 2 + hs[0]
-            mm(ps[b][:, c], [(SLp, T.Gp[:, c]), (SLn, T.Gj[:, c])], ["SLp", "SLn"] + nm("Gp", hs) + nm("Gj", hs), ["pb%d" % b], [b])
-            if e == "a":
-                act(T.ab[:, c], ps[b][:, c], F.Abs, ["pb%d" % b], nm("ab", hs), [b])
+                ts(ab, dif, 0.0, A.not_equal, pd, ["ab%d" % h], [b], H)
+            mm(tab, [(Mc, ab)], Mcn + ["ab%d" % h], [pt[2]], [b2], H, False, True)
+            act(TB[:, new], tab, F.Relu, pt + ["pb%d" % b2, "cols"], ["Tn%d%d" % (t + 1, h)], [b2], bias=col(4 + t), n=H)
+            mn, pu, bnd = ["Mn%d%d" % (t + 1, h)], ["pu%d" % b, "pv%d" % b], ps[b][:, H:K]
+            onv = last or OPT["bound"][h] == "v"
+            mm(bnd, ([] if onv else [(Ni, q(h))]) + [(T.idn[:], half(T.t2, h))], ["idn", "Ni", "t2%d" % h, qn[h]], pu[:1], [b], H, True, False)
+            mm(bnd, [(Zc, ab)], ["Zc", "ab%d" % h], pu[1:], [b], H, False, True)
+            if onv:
+                tt(M[:, new], bnd, q(h), A.max, pu + [qn[h]], mn, [b], H)
             else:
-                ts(T.ab[:, c], ps[b][:, c], 0.0, A.not_equal, ["pb%d" % b], nm("ab", hs), [b])
+                mm(dif, [(T.idn[:], q(h))], ["idn", qn[h]], pd[:1], [b], H, True, False)
+                act(half(T.mr, h), bnd, F.Relu, pu, ["mr%d" % h], [b], n=H)
+                mm(dif, [(T.idn[:], half(T.mr, h))], ["idn", "mr%d" % h], pd[1:], [b], H, False, True)
+                act(M[:, new], dif, F.Identity, pd, mn, [b], n=H)
+            dma("s", T.ym[:, K * t + H * h:K * t + H * h + H], M[:, new], 256 * H, mn)
+        for h in both:
+            mm(ps[6][0:64, H:H + 128], [(BM[:, 131 - c:195 - c], TB[:, o + 128 * c:o + 128 * c + 128]) for c in (2 * h, 2 * h + 1)],
+               ["Mo", "Mo2", "Tn%d%d" % (t + 1, h)] + (["Tn%d0" % (t + 1)] if h else []), ["pu6" if h == 0 else "pv6"], [6], 128, h == 0, h == 1)
+        if last and OPT["lout"] == "v":
+            copy(ob[0:64, :], ps[6][0:64, H:H + 128], ["pu6", "pv6"], ["ob%d" % t], [6], 128)
+        else:
+            act(ob[0:64, :], ps[6][0:64, H:H + 128], F.Identity, ["pu6", "pv6"], ["ob%d" % t], [6], n=128)
+        dma("a" if last else "s", T.yjump[:, K * t:K * t + K], ob[32:64, :], 32 * K, ["ob%d" % t])
+        dma("s", T.ypar[:, K * t:K * t + K], ob[0:32, :], 32 * K, ["ob%d" % t])
+        if last:
+            return
 
-        def bound2(hs, e):
-            c, b = rng(hs)[0], 6 + hs[0]
-            more = [(Ni, X[:, o + c.start:o + c.stop])] if e == "a" else []
-            mm(ps[b][:, c], more + [(T.idn[:], T.t2[:, c]), (Zc, T.ab[:, c])],
-               ["idn", "Zc", "Ni"] + nm("t2", hs) + nm("ab", hs) + [qn[h] for h in hs], ["pb%d" % b], [b])
-            if e == "a":
-                act(T.mr[:, c], ps[b][:, c], F.Relu, ["pb%d" % b], nm("mr", hs), [b])
-
-        def bound3(hs, e, dq="s"):
-            c, b = rng(hs)[0], 6 + hs[0]
-            cc, yc = slice(o + c.start, o + c.stop), slice(K * t + c.start, K * t + c.stop)
-            mn, qs = nm("Mn%d" % (t + 1), hs), [qn[h] for h in hs]
-            if e == "a":
-                mm(ps[b][:, c], [(T.idn[:], X[:, cc]), (T.idn[:], T.mr[:, c])], ["idn"] + nm("mr", hs) + qs, ["pb%d" % b], [b])
-                act(M[:, cc], ps[b][:, c], F.Identity, ["pb%d" % b], mn, [b])
+        for h in both:
+            alt, out, pa = ps[h][:, H:K], T.W2[:, K + H * h:K + H * h + H], ["pa%d" % h, "pw%d" % h]
+            if OPT["alt"][h] == "a":
+                gather(T.Xp, "Xp", X, Xr, T.poff, "poff", h, "a")
+                for c, name, b in ((ps[2 + h][:, H:K], "ps%d" % h, 2 + h), (alt, pa[0], h)):
+                    mm(c, [(T.idn[:], q(h)), (T.idn[:], half(T.Xp, h))], ["idn", qn[h], "Xp%d" % h], [name], [b], H, True, b != h)
+                act(half(T.wrap, h), ps[2 + h][:, H:K], F.Sigmoid, ["ps%d" % h], ["wrap%d" % h], [2 + h], bias=400.0 * (t - 255.5), scale=400.0, n=H)
+                t0 = float(t)
             else:
-                tt(M[:, cc], ps[b][:, c], X[:, cc], A.max, ["pb%d" % b] + qs, mn, [b])
-            dma(dq, T.ym[:, yc], M[:, cc], mn)
-
-        def table1(hs):
-            c, b = rng(hs)[0], 4 + hs[0]
-            mm(ps[b][:, c], [(Ms, TB[:, c]), (Ma, T.Gp[:, c]), (Mb, T.Gj[:, c])], names + parts + nm("Gp", hs) + nm("Gj", hs), [], [b], True, False)
-
-        def table2(hs):
-            c, b = rng(hs)[0], 4 + hs[0]
-            cc = slice(o + c.start, o + c.stop)
-            mm(ps[b][:, c], [(Mc, T.ab[:, c])], names + nm("ab", hs), ["pb%d" % b], [b], False, True)
-            act(TB[:, cc], ps[b][:, c], F.Relu, ["pb%d" % b, "cols"], nm("Tn%d" % (t + 1), hs), [b], bias=col(4 + t))
-
-        def outs(hs, e):
-            c, b, ob = rng(hs)[0], 2 + hs[0], T["ob%d" % t]
-            cc = slice(o + c.start, o + c.stop)
-            mm(ps[b][0:16, c], [(Mo, TB[:, cc])], ["Mo"] + nm("Tn%d" % (t + 1), hs), ["pb%d" % b], [b])
-            if e == "a":
-                act(ob[0:16, c], ps[b][0:16, c], F.Identity, ["pb%d" % b], nm("ob%d" % t, hs), [b])
-            else:
-                copy(ob[0:16, c], ps[b][0:16, c], ["pb%d" % b], nm("ob%d" % t, hs), [b])
-
-        def store(e1, e2):
-            ob, yc = T["ob%d" % t], slice(K * t, K * t + K)
-            dma(e1, T.yjump[:, yc], ob[8:16, :], nm("ob%d" % t, both))
-            dma(e2, T.ypar[:, yc], ob[0:8, :], nm("ob%d" % t, both))
-
-        def alt(hs):
-            c, a, b = rng(hs)
-            src = X[:, o + c.start:o + c.stop] if t == 0 else T.q1[:, c]
-            tt(T.W2[:, K + c.start:K + c.stop], win(X, t, T.off, a, b), src, A.add, Xr + qn + ["q1"] + nm("off", hs), nm("alt", hs))
-
-        if t == RO - 1:
-            gat(T.Gp, "Gp", TB, Tr, T.off, "off", h0)
-            thresh(1)
-            gat(T.Mp, "Mp", M, Mr, T.off, "off", h0, "v")
-            jl(h0)
-            newu(1, True)
-            gat(T.Gp, "Gp", TB, Tr, T.off, "off", h1)
-            jc(h0)
-            gat(T.Mp, "Mp", M, Mr, T.off, "off", h1, "v")
-            jl(h1)
-            gat(T.Gj, "Gj", TB, Tr, T.joff, "joff", h0)
-            bound1(h0)
-            jc(h1)
-            gat(T.Gj, "Gj", TB, Tr, T.joff, "joff", h1)
-            bound1(h1)
-            differ(h0)
-            table1(h0)
-            differ(h1, "v")
-            table1(h1)
-            table2(h0)
-            bound2(h0, "v")
-            table2(h1)
-            bound2(h1, "v")
-            bound3(h0, "v")
-            outs(h0, "a")
-            bound3(h1, "v")
-            outs(h1, "a")
-            store("a", "s")
-            break
-        msg, lmsg, qin = T["msg%d" % t], T["lmsg%d" % t], T["qin%d" % t]
-        grp = [h0, h1]
-        gat(T.Gp, "Gp", TB, Tr, T.off, "off", h0)
-        thresh(1)
-        cx(0)
-        newu(1, True)
-        gat(T.Gp, "Gp", TB, Tr, T.off, "off", h1)
-        cx(1)
-        gat(T.Mp, "Mp", M, Mr, T.off, "off", both)
-        px = ["px0", "px1"]
-        alt(h0)
-        ts(T.fail[:, 0:32], ps[0][:, 128:160], 7.5, A.is_lt, px, ["fail"], [0])
-        ts(T.nf[:, 0:32], ps[0][:, 128:160], 7.5, A.is_ge, px, ["nf"], [0], float(K), A.mult)
-        op("v", lambda: Ve.tensor_tensor_scan(T.cum[:, 1:33], T.fail[:, 0:32], T.fail[:, 0:32], 0.0, A.add, A.max), ["fail"], ["cum"])
-        tt(T.tt[:], T.nf[:], T.ci[:], A.min, ["nf", "nf32", "ci", "ci32"], ["tt"])
-        mm(ps[1][:, 128:161], [(T.tri[:], T.fail[:]), (T.blk[:], T.cum[:])], ["tri", "blk", "fail", "fail32", "cum", "cum0"], ["pp"], [1])
-        jl(both)
-        tt(msg[:], ps[1][:, 128:161], T.tt[:], A.add, ["pp", "tt"], ["msg%d" % t], [1])
-        send(lmsg[:], msg[:], "rm%d" % t, ["msg%d" % t], "lmsg%d" % t)
-        alt(h1)
-        jc(both)
-        for hs in grp:
-            gat(T.Gj, "Gj", TB, Tr, T.joff, "joff", hs)
-        tt(T.bb[:], ps[1][:, 128:160], T.nf[:, 0:32], A.add, ["pp", "nf"], ["bb"], [1])
-        if t == 0:
-            copy(T.wf[:], T.ws[:, 0:1], ["ws"], ["wf"])
-            act(T.Ew[:], T.E[:], F.Identity, ["E", "wf"], ["Ew"], scale=T.wf[:, 0:1])
-        bound1(both)
-        ts(T.kk[:], T.bb[:], CAP - 0.5, A.is_ge, ["bb"], ["kk"], (), 4096.0, A.mult)
-        ts(T.W2[:, K:], T.W2[:, K:], 255, A.bitwise_and, nm("alt", both), nm("alt", both))
-        tt(T.bb[:], T.bb[:], T.kk[:], A.max, ["bb", "kk"], ["bb"])
-        for hs in grp:
-            differ(hs)
-            table1(hs)
-        for hs in grp:
-            table2(hs)
-        for hs in grp:
-            bound2(hs, "a")
-        ln = "lmsg%d" % t
-        ts(T.yy[:], T.bb[:], lmsg[:, 32:33], A.is_ge, ["bb", ln], ["yy"], (), 4096.0, A.mult)
-        copy(T.soff[:], lmsg[:, 0:32], [ln], ["soff"])
-        tt(T.yy[:], T.yy[:], T.bb[:], A.max, ["yy", "bb"], ["yy"])
-        copy(T.W2[:, 0:K].indirect(T.soff[:, 0:32]), qin[:], ["soff", "qin%d" % t], ["come"])
-        tt(T.yy[:], T.yy[:], T.ai[:], A.min, ["yy", "ai"], ["yy"])
-        for hs in grp:
-            bound3(hs, "a")
-        copy(T.goff[:], T.yy[:], ["yy"], ["goff"])
-        for hs in grp:
-            outs(hs, "a")
-        store("s", "s")
+                act(half(T.q1, h), q(h), F.Identity, [qn[h]], ["q1%d" % h], bias=t - 256.0, n=H)
+                tt(half(T.Xp, h), at(X, T.poff, 16 * h), half(T.q1, h), A.add, Xr + ["q1%d" % h, "poff%d" % h], ["Xp%d" % h], gat=H)
+                mm(alt, [(T.idn[:], half(T.Xp, h))], ["idn", "Xp%d" % h], pa[:1], [h], H, True, False)
+                act(half(T.wrap, h), half(T.Xp, h), F.Sigmoid, ["Xp%d" % h], ["wrap%d" % h], bias=200.0, scale=400.0, n=H)
+                t0 = 256.0
+            mm(alt, [(T.n256[:], half(T.wrap, h))], ["n256", "wrap%d" % h], pa[1:], [h], H, False, True)
+            act(out, alt, F.Identity, pa, ["alt%d" % h], [h], bias=t0, n=H)
+            if h:
+                copy(T.got[:], land[1][:, 16:17], ["land%d1" % t], ["got"])
+            copy(T.W2[:, 0:K].indirect(land[h][:, 0:16]), half(qin, h), ["land%d%d" % (t, h), "qin%d" % t], ["come"], sct=H)
+        mm(ps[3][:, 129:192:2], [(T.ones[0:1, :], crow1), (T.triA[:], fail(0, 32)), (T.blk[:], cum(0, 32))],
+           ["ones", "crow1", "triA", "blk", "fail0", "fail1", "cum0", "cum1"], ["pr"], [3])
+        tt(ps[3][:, 128:192:2], T.ai[:], ps[3][:, 129:192:2], A.subtract, ["ai", "pr"], ["pq"], [3])
+        act(T.room[:], T.got[:], F.Relu, ["got"], ["room"], bias=400.0 * CAP, scale=-400.0)
+        act(dv(1, 64, 2), ps[3][:, 129:192:2], F.Sigmoid, ["pr", "room", "zero"], ["dv1"], [3], bias=T.room[:, 0:1], scale=400.0)
+        scan(T.go[:], dv(0, 64), ps[3][:, 128:192], 0.0, A.mult, A.add, ["zero", "dv1", "pr", "pq"], ["go"], [3])
+        ts(T.goff[:], T.go[:, 1::2], CAP - 0.5, A.add, ["go"], ["goff"])
         q2 = nm("Xn%d" % (t + 2), both)
         for h in both:
             c0 = o + K + H * h
-            copy(X[:, c0:c0 + H], T.W2[:, 0:2 * K].indirect(T.goff[:, 16 * h:16 * h + 16]), ["come", "alt0", "alt1", "goff"], [q2[h]])
-            tolist(ps[h][:, 192:208], T.Ew, lambda i: X[:, c0 + i:c0 + H:16], ["Ew", q2[h]], ["ph%d" % h], [h])
-        if t + 1 < RO - 1:
-            send(T["qin%d" % (t + 1)][:], X[:, o + K:o + 2 * K], "rq%d" % (t + 1), q2, "qin%d" % (t + 1))
+            copy(X[:, c0:c0 + H], T.W2[:, 0:2 * K].indirect(T.goff[:, 16 * h:16 * h + 16]), ["come", "alt0", "alt1", "goff"], [q2[h]], gat=H)
+            mm(ps[h][:, 192:208], turns(T.Ew, lambda i: X[:, c0 + i:c0 + H:16]), ["Ew", q2[h]], ["ph%d" % h], [h])
+        if t + 2 < RO:
+            send(T["qin%d" % (t + 1)][:], X[:, o + K:o + 2 * K], 256 * K, "rq%d" % (t + 1), q2, "qin%d" % (t + 1))
+
+    for t in range(RO):
+        one_round(t)
     emit(g, T, ops)

@@ -5,18 +5,37 @@ W = V + RO * K
 H = K // 2
 BIG = 32768.0
 MID = 1920.0
-C0 = 12582912.0
-OPT = {"xa": 192, "x4": 0, "xn": 2, "bound": "aa", "mp": "av", "alt": "va", "ab": "aa", "lmp": "vv", "lab": "av", "lout": "a",
-       "line": ("S",), "mn": 1, "tbv": (3, 5, 7), "cyc": 0.95, "gat": 1.4, "sct": 3.5, "far": 250.0, "own": 100.0, "fly": 1900.0}
+C0 = 12582913.0
+C2 = 3072.0
+BACK = C2 - MID / 4096
+P = 6
+OPT = {"war": 0, "up": (0.0, 0.0), "dup": 0.0, "xa": (320, 320, 320, 320, 160), "xn": 2, "bound": "aa", "mp": "aa", "alt": "vv", "ab": "aa", "lmp": "va", "lab": "aa",
+       "line": ("S",), "mn": 1, "tbv": (12, 13, 14, 15), "cuts": (0, 144, 288, 432, 576), "zat": 3,
+       "d3": "vv", "pm": (0, 0), "jm": (0, 1), "gp": ("aa", "av"), "gj": ("aa", "av"), "cyc": 0.95, "gat": 1.4, "sct": 3.5, "far": 150.0, "own": 100.0, "fly": 1900.0}
+LINES = {
+"v": ("hs0 hs0 off00 hs1 sm00 hs1 off01 v0 sm10 pj0 d00 sx00 so00 sx01 off10 pj1 d01 sm00 so01 off11 sm10 sx11 d00 pj0 so10 sx10 off20 pj1 d01 sm00 so11 off21 sm10 sx20 d00 pj0 so20 sx21 off30 d01 pj1 so21 sm00 off31 sm10 sx31 d00 pj0 sx30 so30 d01 pj1 off40 so31 sm00 off41 sm10 sx00",
+ "d00 pj0 sx01 so40 pj1 d01 off50 so41 bx0 off51 dl00 bx1 dl1 dl01 po0 po1 fail0 poff0 cum0 prod0 poff1 fail1 cum1 prod1 msg0 Xp1 msg1 Xp0 joff0 t20 joff1 pq t21 come got come go goff Xn0 Xn1",
+ "sx01 pj0 pj1 dl1 d00 d01 so41 so40 dl01 dl00 po0 po1 poff0 poff1 Gp1 Mp0 joff0 Gj1 t20 t21 same far jmp Mn0 Mn1",
+ "sm00 <zero2 sm10 pj0 d00 so00 <Mc2 v0 <Zc off10 pj1 d01 <QP <Ma0 so01 sm00 off11 <zero sm10 sx00 <wf pj0 d00 so10 off20 sx01 d01 pj1 sm00 so11 off21 sm10 sx11 pj0 d00 sx20 so20 sx10 d01 pj1 off30 so21 sm00 off31 sx31 sm10 sx21 pj0 d00 sx30 so30 d01 pj1 off40 so31 sm00 off41 sm10 sx00"),
+"a": ("sz0 sz1 xs sz0 sx09 sz1 xs <ob sz0 sx19 sz1 fl5 xs sz0 sz1 sx29 xs sz0 fl4 sz1",
+ "xs sx39 fl3 sx09 q11 fl1 fl2 q10 Gp0 Gp1 Mp0 Mp1 wrap0 Gj0 wrap1 Gj1 alt0 ab0 ab1 alt1 room dv1 mr0 mr1 Tn1 Mn0 Mn1 Tn0",
+ "xs sx39 fl3 sx09 fl1 fl2 Gp0 Mp1 Gj0 ab0 ob ab1",
+ "sz0 sz1 sz0 sz1 xs sz0 xs sz1 sx09 <Ew xs sz0 fl5 sz1 sx29 sx19 xs sz0 sz1 fl4"),
+"p": ("<pu6 pn0 pn1 <pv6 pm0 pm1 pn0 pb4 pn1 pm0 dl5 pm1 pb5 pb6 pn1 pn0 pm0 pm1 pb4 dl4 dl3 pn0 pn1 pm0 pm1 pb6 dl2 pn0 pn1 pb5 pm0 pm1 pb4",
+ "px0 px1 pb6 pc0 py0 pc1 py1 pp0 pp1 pl0 pb5 pr pl1 pb4 pa0 pd4 pw0 pa1 pu4 pd5 pt10 pw1 pt00 pv4 pu5 pt11 pv5 pb5 pt12 pt01 pt02 pb4 pd4 pd5 ph0 ph1",
+ "pb6 pl0 pu7 pb5 pb4 pb6 pd4 pf0 pf1 pd5 pu4 pv4 pu5 pv5",
+ "pn0 pn1 pm0 pm1 pn1 pn0 dl5 pm0 pm1 pb4 pn0 dl4 pm0 pb5 pn1 pm1 pb6 dl3 pn0 pn1 pb4 pm0 pm1 pb6 pb5 pn0 pn1 pm0 pm1 pb4 dl2"),
+}
 BF, FP, I32, U16 = "bfloat16", "float32", "int32", "uint16"
 SCRATCH = {}
 for _dt, _w, _names in (
         (BF, [W], "X M TB"), (I32, [576], "raw loi"), (BF, [576], "hi lo"), (BF, [520], "R"), (BF, [144], "E Ew Ej"),
-        (BF, [128], "ones idn blk tri triA n256"), (BF, [64, 16], "rows"), (FP, [8], "cols"), (BF, [1648], "BM"),
-        (BF, [H, 2], "st0 st1"), (BF, [K, 2], "sx0 sx1"), (FP, [128], "d0 idf nif"), (FP, [S, 128], "so"), (U16, [192], "off"),
+        (BF, [128], "ones idn blk tri triA n256"), (BF, [64, 16], "rows"), (FP, [8], "cols"), (BF, [1856], "BM"),
+        (BF, [H, 2], "st0 st1"), (BF, [K, 2], "sx0 sx1"), (FP, [128], "idf nif"), (FP, [S, 32 * P], "so"),
+        (FP, [32, 4] if P == 4 else [192], "d0"), (BF, [32], "hrow"), (BF, [144], "E16"), (U16, [192], "off"),
         (U16, [32], "poff joff goff"), (FP, [192], "po"), (FP, [64], "go"),
         (I32, [32], "u0s hs"), (I32, [4], "ws"), (FP, [1], "wf got room"), (FP, [32], "i16 ai v0"),
-        (U16, [16], "ma0 ma1 la0 la1"), (U16, [17], "mb0 mb1 lb0 lb1"), (BF, [2 * K], "W2"), (FP, [128], "ob0 ob1 ob2"),
+        (U16, [16], "ma0 ma1 la0 la1"), (U16, [17], "mb0 mb1 lb0 lb1"), (BF, [2 * K], "W2"), (FP, [128], "ob0 ob1 ob2 same far"),
         (BF, [K], "bx qin0 qin1 Gp Gj Mp Xp t2 ab mr xs wrap q1")):
     for _n in _names.split():
         SCRATCH[_n] = ("sbuf", [128] + _w, _dt)
@@ -24,6 +43,23 @@ for _b in range(8):
     SCRATCH["ps%d" % _b] = ("psum", [128, 512], FP)
 SEMAPHORES = ["v", "a", "p", "g", "sent", "rq0", "rq1", "ra0", "ra1", "rb0", "rb1"] + ["d%d" % _i for _i in range(24)]
 ORDER = []
+
+
+def line_up(ops, starts):
+    def tag(o):
+        n = o["w"][0]
+        return n[:-2] + n[-1] if n[:2] in ("ms", "Xn", "Tn", "Mn") else n[:2] if n[:2] == "ob" else n
+    for e, (walk, turn, end, first) in LINES.items():
+        before, used = None, set()
+        for t in range(RO):
+            for name in ((walk if t else first) + " " + (turn if t < RO - 1 else end)).split():
+                a, b = (starts[t], starts[t + 1]) if name[0] == "<" else (starts[t + 1], starts[t + 2])
+                for i in range(a, b):
+                    if ops[i]["e"] == e and ops[i]["kind"] == "op" and i not in used and tag(ops[i]) == name.lstrip("<"):
+                        used.add(i)
+                        ops[i]["behind"] = before
+                        before = i
+                        break
 
 
 def needs(ops):
@@ -50,19 +86,25 @@ def arrange(ops):
             if k in tags:
                 pre[i].append((tags[k], 0.0))
             tags[k] = i
+        if o.get("behind") is not None:
+            pre[i].append((o["behind"], 0.0))
         if o["kind"] == "arrive":
             pre[i].append((i - 1, 0.0))
         elif o["kind"] != "op":
             if o["e"] in inorder:
                 pre[i].append((inorder[o["e"]], -1e6))
             inorder[o["e"]] = i
+    todo, seen = [], set()
+    while len(todo) < n:
+        i = [i for i in range(n) if i not in seen and all(j in seen for j, d in pre[i])][0]
+        todo.append(i)
+        seen.add(i)
     chain = [0.0] * n
-    for i in range(n - 1, -1, -1):
-        chain[i] += ops[i]["c"] + ops[i]["late"]
+    for i in reversed(todo):
+        chain[i] += ops[i]["c"] + ops[i]["late"] + ops[i].get("up", 0.0)
         for j, d in pre[i]:
             chain[j] = max(chain[j], max(d, -ops[j]["late"]) + chain[i])
     start, end, free, bank, pipe = {}, {}, {}, {}, [0.0]
-    todo = list(range(n))
     while todo:
         est, ready = {}, []
         for i in todo[:160]:
@@ -129,6 +171,8 @@ def emit(g, T, ops):
         o["waits"] = []
         if e is not None:
             for j in sorted(deps, key=lambda j: -place[j]):
+                if OPT["war"] and ops[j]["e"] == e and ops[j]["kind"] == o["kind"] == "op" and not set(ops[j]["w"]) & set(o["r"] + o["w"]):
+                    continue
                 key, n = ops[j]["id"]
                 if known[e].get(key, 0) >= n:
                     continue
@@ -191,7 +235,7 @@ def rank_program(g, core, T, topo):
         c = cyc * max(n, 64) + 10
         if gat or sct:
             c = cyc * (gat * OPT["gat"] + sct * OPT["sct"]) + (50 if e == "v" else 65)
-        ops.append({"e": e, "f": f, "r": list(r), "w": list(w), "b": list(b), "sem": None, "kind": "op", "c": c, "late": 0.0})
+        ops.append({"e": e, "f": f, "r": list(r), "w": list(w), "b": list(b), "sem": None, "kind": "op", "c": c, "late": 0.0, "n3": (n, gat, sct)})
 
     def dma(e, out, in_, size, r=(), w=()):
         q = g.sync if e == "s" else g.scalar
@@ -268,9 +312,9 @@ def rank_program(g, core, T, topo):
     both = (0, 1)
 
     for k, src in enumerate((T.par, T.jump, T.ln)):
-        dma("a" if k == 1 else "s", T.raw[32 * k:32 * k + 32, :], src[:], 32 * V, w=["raw%d" % k])
-    dma("a", T.u0s[:], T.u0[:], 128 * 128, w=["u0s"])
-    dma("a", X[:, V:V + K], T.q[:], 256 * K, w=["Xn10", "Xn11"])
+        dma("s" if k == 1 else "a", T.raw[32 * k:32 * k + 32, :], src[:], 32 * V, w=["raw%d" % k])
+    dma("s", T.u0s[:], T.u0[:], 128 * 128, w=["u0s"])
+    dma("s", X[:, V:V + K], T.q[:], 256 * K, w=["Xn10", "Xn11"])
     dma("s", M[:, 0:V], T.m[:], 256 * V, w=["Mn0"])
     dma("s", X[:, 0:V], T.x[:], 256 * V, w=["Xn0"])
     dma("s", T.ws[:, 0:1], T.w[:], 512, w=["ws"])
@@ -279,8 +323,8 @@ def rank_program(g, core, T, topo):
     iota(T.raw[96:128, :], [[1, 576]], 0, 576, [], ["raw3"], 576, False)
     memset(T.ones[:], 1.0, ["ones"])
     memset(T.R[:], 0.0, Rn, 260)
-    segs = [(0, 1, 0, 8, 1.0), (0, 1, 1, 8, 4096.0), (0, 1, 2, 8, 4096.0), (0, 1, 3, 8, -4096.0),
-            (1, 2, 0, 16, -MID), (1, 2, slice(1, 3), 0, -MID * 4096), (1, 2, 3, 16, MID * 4096),
+    segs = [(0, 1, 0, 8, 1 / 256), (0, 1, 1, 8, 16.0), (0, 1, 2, 8, 16.0), (0, 1, 3, 8, -16.0),
+            (1, 2, 0, 16, -MID / 256), (1, 2, slice(1, 3), 0, -MID * 16), (1, 2, 3, 16, MID * 16),
             (2, 3, 1, 8, 1.0), (2, 3, 2, 8, 1.0), (2, 3, 3, 8, -1.0), (3, 4, slice(0, 6, 2), 0, -4128.0),
             (3, 4, 5, 16, -4128.0), (4, 7, 14, 16, 1.0)]
     segs += [(4 + t, 5 + t, 5, 16, float(V + K * t)) for t in range(RO)]
@@ -301,37 +345,45 @@ def rank_program(g, core, T, topo):
             ins = Pe.matmul(ps[7][:, 300 + k:301 + k], T.rows[0:1, 8 * k:8 * k + 8, :], T.ones[0:1, 0:1], True, True)
         return ins
     op("p", turn, ["ones", "rowp"] + rown, ["pu7"], [7], 256)
-    op("a", lambda: Sc.activation(T.d0[:, 1::4], T.ones[:, 0:32], F.Sigmoid, scale=400.0), ["ones"], ["d0c"], (), 1400)
-    act(T.cols[:], ps[7][:, 300:308], F.Identity, ["pu7", "d0c"], ["cols"], [7])
-    act(T.d0[:, 0::4], T.ones[:, 0:32], F.Identity, ["ones"], ["d0a"], scale=0.0)
-    act(T.d0[:, 2::4], T.ones[:, 0:32], F.Identity, ["ones"], ["d0b"], scale=-4097.0)
+    op("a", lambda: Sc.activation(T.hrow[0:1, 0::2], T.ones[0:1, 0:16], F.Sigmoid, scale=-400.0), ["ones"], ["hrow0"], (), 1400)
+    act(T.cols[:], ps[7][:, 300:308], F.Identity, ["pu7", "hrow0"], ["cols"], [7])
+    act(T.E16[:], T.E[:], F.Identity, ["E"], ["E16"], scale=1 / 16, n=144)
+    if P == 4:
+        memset(T.d0[:], 0.0, ["d0a", "d0b"], 128)
+    else:
+        act(T.d0[:, 0::3], T.ones[:, 0:64], F.Identity, ["ones"], ["d0a"], scale=0.0)
+        act(T.d0[:, 2::3], T.ones[:, 0:64], F.Identity, ["ones"], ["d0a"])
+        act(T.d0[:, 3::6], T.ones[:, 0:32], F.Identity, ["ones"], ["d0a", "d0b"])
     for h in both:
-        act(ps[h][:, 1:64:4], T.ones[:, 0:16], F.Identity, ["ones"], ["pk%d" % h], [h], scale=-C0)
+        act(ps[h][:, 0:16 * P:P], T.ones[:, 0:16], F.Identity, ["ones"], ["pk%d" % h], [h], scale=-4097 / 4096)
+        if P == 6:
+            for k in (1, 3):
+                act(ps[h][:, k:96:6], T.ones[:, 0:16], F.Identity, ["ones"], ["pz%d" % h], [h], scale=0.0)
     raws = ["raw%d" % k for k in range(4)]
-    for hf in both:
-        c = slice(288 * hf, 288 * hf + 288)
-        ts(T.loi[:, c], T.raw[:, c], 31, A.bitwise_and, raws, ["loi%d" % hf], n=288)
-        ts(T.hi[:, c], T.raw[:, c], 4112.5, A.add, raws, ["hi%d" % hf], n=288)
-        copy(T.lo[:, c], T.loi[:, c], ["loi%d" % hf], ["lo%d" % hf], n=288)
+    cuts = OPT["cuts"]
+    for hf, (a, e) in enumerate(zip(cuts, cuts[1:])):
+        ts(T.loi[:, a:e], T.raw[:, a:e], 31, A.bitwise_and, raws, ["loi%d" % hf], n=e - a)
+        ts(T.hi[:, a:e], T.raw[:, a:e], 4112.5, A.add, raws, ["hi%d" % hf], n=e - a)
+        copy(T.lo[:, a:e], T.loi[:, a:e], ["loi%d" % hf], ["lo%d" % hf], n=e - a)
     copy(T.off[:, 0:32], T.u0s[:], ["u0s"], ["off00", "off01"])
     Mcn, Man, Mbn = nm("Mc", (2, 3, 4)), nm("Ma", (0, 1, 3, 4)), ["Mb2"]
-    memset(BM[:, 0:768], 0.0, Mcn + Man + Mbn + ["Ms", "Mo", "Mo2", "SLp"], 384)
-    memset(BM[:, 768:1648], 0.0, ["Zc", "Ni", "zero", "crow0", "crow1", "cc0", "cc1", "SLn"], 440)
+    for a, e, w in ((768, 1024, ["Zc", "Ni"]), (1024, 1344, ["zero", "crow0", "crow1"]), (1344, 1648, ["zero2", "cc0", "cc1", "SLn"]), (1648, 1856, ["QP", "QJ"]),
+                    (0, 384, Mcn + ["Mo", "Mo2", "SLp"]), (384, 768, Man + Mbn + ["Ms"])):
+        op("v", lambda a=a, e=e: Ve.memset(BM[:, a:e], 0.0), ["lo%d" % OPT["zat"]], w, (), (e - a) / 2)
     SLp, SLn = BM[:, 0:128], BM[:, 1520:1648]
     parts = []
-    for hf in both:
+    for hf, (a, e) in enumerate(zip(cuts, cuts[1:])):
         for c in range(4):
             i = 4 * hf + c
-            b = 2 + i % 6
-            cs = slice(288 * hf, 288 * hf + 288)
+            b, n = 2 + i % 6, e - a
             wide = ["pb%d" % b, "pu%d" % b]
-            mm(ps[b][:, 0:288], [(T.R[:, 8 + 128 * c:136 + 128 * c], T.hi[:, cs]), (T.R[:, 128 * c:128 * c + 128], T.lo[:, cs])],
-               Rn + ["hi%d" % hf, "lo%d" % hf], wide, [b], 288)
-            out = TB[:, 576 * c + 288 * hf:576 * c + 288 * hf + 288]
+            mm(ps[b][:, 0:n], [(T.R[:, 8 + 128 * c:136 + 128 * c], T.hi[:, a:e]), (T.R[:, 128 * c:128 * c + 128], T.lo[:, a:e])],
+               Rn + ["hi%d" % hf, "lo%d" % hf], wide, [b], n)
+            out = TB[:, 576 * c + a:576 * c + e]
             if i in OPT["tbv"]:
-                ts(out, ps[b][:, 0:288], col(3), A.add, wide + ["cols"], ["tb%d" % i], [b], 288)
+                ts(out, ps[b][:, 0:n], col(3), A.add, wide + ["cols"], ["tb%d" % i], [b], n)
             else:
-                act(out, ps[b][:, 0:288], F.Identity, wide + ["cols"], ["tb%d" % i], [b], bias=col(3), n=288)
+                act(out, ps[b][:, 0:n], F.Identity, wide + ["cols"], ["tb%d" % i], [b], bias=col(3), n=n)
             parts.append("tb%d" % i)
     Mc, Ma, Mb, Ms, Zc, Ni = [BM[:, 128 * k:128 * k + 128] for k in range(2, 8)]
     Mo1, Mo2 = BM[:, 131:163:4], BM[:, 163:195:4]
@@ -358,6 +410,11 @@ def rank_program(g, core, T, topo):
             put(Mo2, [[-16, 8]], -1 - i - d, (1.0, 1.0, -1.0)[i], "Mo2")
             if i == 0:
                 put(Mo1, [[-16, 8]], -d, 1.0, "Mo")
+    for base, name, fs in ((1651, "QP", ((4, 1.0), (12, 1.0), (14, 1.0))), (1683, "QP", ((5, -1.0), (13, -1.0))), (1715, "QP", ((5, 1.0), (13, 1.0))),
+                           (1755, "QJ", ((4, -1.0), (12, -1.0), (14, -1.0))),
+                           (1787, "QJ", ((1, 1.0), (9, 1.0), (2, 1.0), (10, 1.0), (3, -1.0), (11, -1.0)))):
+        for f, c in fs:
+            put(BM[:, base:base + 32:4], [[-16, 8]], -f, c, name)
     put(bm(3, 4, 8), [[-8, 16]], -4, 2.0, "Ma4")
     put(bm(5, 5, 8), [[-8, 16]], -5, 1.0, "Ms")
     put(bm(3, 12, 16), [[-16, 8]], -14, 2.0, "Ma4")
@@ -387,26 +444,26 @@ def rank_program(g, core, T, topo):
         def at(B, offs, a):
             return win(B, t, offs, a, a + 16)
 
-        def node(s, h):
-            return T.so[:, s, 64 * h + 3:64 * h + 64:4]
+        def node(s, hs):
+            return T.so[:, s, 16 * P * hs[0] + P - 2:16 * P * (hs[-1] + 1):P]
 
         def xtest(s):
-            n, b, out = OPT["x4" if s == S - 1 else "xa"], 4 + s % 2, sx[s // 2 % 2]
+            n, b, out, k = OPT["xa"][s], 4 + s % 2, sx[(s + 1) // 2 % 2], (s + 1) % 2
             cut = [32 * ((K - n) // 32 * i // OPT["xn"]) for i in range(OPT["xn"] + 1)]
             for i, (a, e) in enumerate(zip(cut, cut[1:])):
-                tt(out[:, a:e, s % 2], win(X, t, T.off, 32 * s + a // 16, 32 * s + e // 16), X[:, o + a:o + e], A.is_ge,
+                tt(out[:, a:e, k], win(X, t, T.off, 32 * s + a // 16, 32 * s + e // 16), X[:, o + a:o + e], A.is_ge,
                    Xr + qn + nm("off%d" % s, both if e > H else (0,)), ["sx%d%d" % (s % 4, i)], gat=e - a)
             if n:
-                act(T.xs[:, 0:n], win(X, t, T.off, 32 * s + (K - n) // 16, 32 * s + 32), F.Identity, Xr + ["off%d1" % s], ["xs"], gat=n)
+                act(T.xs[:, 0:n], win(X, t, T.off, 32 * s + (K - n) // 16, 32 * s + 32), F.Identity, Xr + nm("off%d" % s, both if n > H else (1,)), ["xs"], gat=n)
                 mm(ps[b][:, 0:n], [(Ni, X[:, o + K - n:o + K]), (T.idn[:], T.xs[:, 0:n])], ["Ni", "idn", "xs"] + qn, ["pb%d" % b], [b], n)
-                act(out[:, K - n:K, s % 2], ps[b][:, 0:n], F.Sigmoid, ["pb%d" % b], ["sx%d9" % (s % 4)], [b], bias=200.0, scale=400.0, n=n)
+                act(out[:, K - n:K, k], ps[b][:, 0:n], F.Sigmoid, ["pb%d" % b], ["sx%d9" % (s % 4)], [b], bias=200.0, scale=400.0, n=n)
 
         def xsum(s0, n):
-            B, b = sx[s0 // 2 % 2], 2 + s0 // 2 % 2
-            mm(ps[b][:, 0:32 * n], turns(T.E, lambda i: B[:, i::16, 0:n]),
+            B, b = sx[(s0 + 1) // 2 % 2], 6
+            mm(ps[b][:, 0:32 * n], turns(T.E, lambda i: B[:, i::16, 2 - n:2]),
                ["E"] + ["sx%d%d" % (s % 4, i) for s in range(s0, s0 + n) for i in list(range(OPT["xn"])) + [9]], ["pb%d" % b], [b])
             for s in range(s0, s0 + n):
-                act(fl(5 - s, 192, 6), ps[b][:, s % 2:32 * n:n], F.Sigmoid, ["pb%d" % b, "zero"], ["fl%d" % (5 - s)], [b], bias=3000.0, scale=-400.0)
+                act(fl(5 - s, 192, 6), ps[b][:, s - s0:32 * n:n], F.Sigmoid, ["pb%d" % b, "zero"], ["fl%d" % (5 - s)], [b], bias=3000.0, scale=-400.0)
 
         for s in range(S):
             for h in both:
@@ -416,51 +473,50 @@ def rank_program(g, core, T, topo):
                     copy(hs, ps[h][:, 192:208], ["ph%d" % h], ["hs%d" % h], [h])
                     ts(hs, hs, K - 1, A.bitwise_and, ["hs%d" % h], ["hs%d" % h])
                     ts(T.off[:, a:a + 16], hs, float(o - K), A.add, ["hs%d" % h], [on])
-                act(st[h][:, :, 1], at(TB, T.off, a), F.Identity, Tr + ["cols", on], ["sz%d" % h], scale=col(0), bias=col(1), gat=H)
-                ops[-1]["line"] = OPT["line"]
-                n = H // OPT["mn"]
-                for i in range(OPT["mn"]):
-                    tt(st[h][:, n * i:n * i + n, 0], win(M, t, T.off, a + n * i // 16, a + (n * i + n) // 16), X[:, o + H * h + n * i:o + H * h + n * i + n],
-                       A.is_ge, Mr + [qn[h], on], ["sm%d%d" % (h, i)], gat=n)
-                mm(ps[h][:, 0:64:2], turns(T.E, lambda i: st[h][:, i::16, :]), ["E", "sz%d" % h] + nm("sm%d" % h, range(OPT["mn"])), ["pm%d" % h, "pz%d" % h], [h])
-            for h in both:
-                a = 32 * s + 16 * h
-                act(T.d0[:, 64 * h + 3:64 * h + 64:4], ps[h][:, 0:64:4], F.Sigmoid, ["pm%d" % h], ["d0%d" % h], [h], bias=-3000.0, scale=400.0)
-                ops[-1]["line"] = OPT["line"]
-                act(ps[h][:, 3:64:4], ps[h][:, 2:64:4], F.Identity, ["pz%d" % h], ["pj%d" % h], [h], bias=C0, scale=1 / 4096)
-                act(ps[h][:, 0:64:4], ps[h][:, 2:64:4], F.Identity, ["pz%d" % h], ["pm%d" % h], [h], bias=C0, scale=1 / 4096)
-                ops[-1]["line"] = OPT["line"]
-                scan(T.so[:, s, 64 * h:64 * h + 64], T.d0[:, 64 * h:64 * h + 64], ps[h][:, 0:64], 0.0, A.mult, A.add,
-                     ["d0a", "d0b", "d0c"] + [n + str(h) for n in ("d0", "pm", "pz", "pj", "pk")], ["so%d%d" % (s, h)], [h])
+                sums = ps[h][:, 1:64:2] if P == 4 else ps[h][:, 2:96:3]
+                act(st[h][:, :, 0], at(TB, T.off, a), F.Identity, Tr + ["cols", on], ["sz%d" % h], scale=col(0), bias=col(1), gat=H)
+                tt(st[h][:, :, 1], at(M, T.off, a), q(h), A.is_ge, Mr + [qn[h], on], ["sm%d0" % h], gat=H)
+                mm(sums, turns(T.E16, lambda i: st[h][:, i::16, :]), ["E16", "sz%d" % h, "sm%d0" % h], ["pm%d" % h], [h])
+                whole = T.d0[:, 16 * h:16 * h + 16, 1:3] if P == 4 else T.d0[:, 96 * h + 1:96 * h + 96:3]
+                ts(whole, sums, C0, A.add, ["pm%d" % h, "d0a"], ["d0%d" % h], [h], 0, C0, A.subtract)
+                z0 = P // 2 - 1
+                ts(ps[h][:, P - 2:16 * P:P], ps[h][:, z0:16 * P:P], 1 / 4096, A.mult, ["pm%d" % h, "pn%d" % h], ["pj%d" % h], [h], 0, C2, A.add)
+                scan(T.so[:, s, 16 * P * h:16 * P * (h + 1)], T.d0[:, 16 * h:16 * h + 16, :] if P == 4 else T.d0[:, 96 * h:96 * h + 96], ps[h][:, 0:16 * P], 0.0,
+                     A.mult, A.add, ["d0a", "d0b"] + [n + str(h) for n in ("d0", "pm", "pn", "pj", "pk", "pz")], ["so%d%d" % (s, h)], [h], 16 * P)
                 if s < S - 1 or not last:
-                    ts(T.off[:, a + 32:a + 48], node(s, h), MID - C0, A.add, ["so%d%d" % (s, h)], ["off%d%d" % (s + 1, h)])
+                    ts(T.off[:, a + 32:a + 48], node(s, (h,)), -BACK, A.add, ["so%d%d" % (s, h)], ["off%d%d" % (s + 1, h)], (), 0, 4096.0, A.mult)
             xtest(s)
-            if s % 2 or s == S - 1:
-                xsum(s - s % 2, 1 + s % 2)
+            if s % 2 == 0:
+                xsum(max(s - 1, 0), min(s + 1, 2))
             if s == 0:
-                ts(T.v0[:], T.hs[:] if t else T.u0s[:], C0 - MID + (o - K if t else 0), A.add, ["hs0", "hs1", "u0s"], ["v0"])
+                ts(T.v0[:], T.hs[:] if t else T.u0s[:], 1 / 4096, A.mult, ["hs0", "hs1", "u0s"], ["v0"], (), 0, BACK + (o - K if t else 0) / 4096, A.add)
             if s < S - 1:
-                a, an = (T.so[:, s - 1, 3::4], nm("so%d" % (s - 1), both)) if s else (T.v0[:], ["v0"])
+                a, an = (node(s - 1, both), nm("so%d" % (s - 1), both)) if s else (T.v0[:], ["v0"])
                 now = nm("so%d" % s, both)
                 if s == 0:
                     mm(dl[:, 5:192:6], [(T.idf[:], a)], ["idf"] + an + now, ["dl5", "pb7"], [7], 256)
-                mm(dl[:, 4 - s:192:6], [(T.nif[:], a), (T.idf[:], T.so[:, s, 3::4])], ["idf", "nif", "dl5"] + an + now, ["dl%d" % (4 - s)], [7], 256)
+                if s < S - 2 or OPT["d3"][last] == "p":
+                    mm(dl[:, 4 - s:192:6], [(T.nif[:], a), (T.idf[:], node(s, both))], ["idf", "nif", "dl5"] + an + now, ["dl%d" % (4 - s)], [7], 256)
         dls = ["dl00", "dl01"] + ["dl%d" % k for k in range(1, 6)]
         fls = ["fl%d" % k for k in range(1, 6)]
-        for h in both:
-            tt(dl[:, 96 * h:96 * h + 96:6], node(S - 1, h), node(S - 2, h), A.subtract, ["so%d%d" % (S - 1, h), "so%d%d" % (S - 2, h), "dl5"], ["dl0%d" % h], [7])
-            c = slice(96 * h, 96 * h + 96)
-            scan(T.po[:, c], fl(c.start, c.stop), dl[:, c], 0.0, A.mult, A.add, ["zero", dls[h]] + dls[2:] + fls, ["po%d" % h], [7], 96)
-            ts(T.poff[:, 16 * h:16 * h + 16], T.po[:, 96 * h + 5:96 * h + 96:6], MID - C0, A.add, ["po%d" % h], ["poff%d" % h])
+        if OPT["d3"][last] == "v":
+            tt(dl[:, 1:192:6], node(S - 2, both), node(S - 3, both), A.subtract, nm("so%d" % (S - 2), both) + nm("so%d" % (S - 3), both) + ["dl5"], ["dl1"], [7])
+        for hs in ([both] if OPT["pm"][last] else [(0,), (1,)]):
+            a, e = hs[0], hs[-1] + 1
+            tt(dl[:, 96 * a:96 * e:6], node(S - 1, hs), node(S - 2, hs), A.subtract,
+               nm("so%d" % (S - 1), hs) + nm("so%d" % (S - 2), hs) + ["dl5"], nm("dl0", hs), [7])
+            scan(T.po[:, 96 * a:96 * e], fl(96 * a, 96 * e), dl[:, 96 * a:96 * e], 0.0, A.mult, A.add, ["zero"] + nm("dl0", hs) + dls[2:] + fls, nm("po", hs), [7], 96 * (e - a))
+            ts(T.poff[:, 16 * a:16 * e], T.po[:, 96 * a + 5:96 * e:6], -BACK, A.add, nm("po", hs), nm("poff", hs), (), 0, 4096.0, A.mult)
 
         if not last:
             msg, land, qin = [T["ma%d" % t], T["mb%d" % t]], [T["la%d" % t], T["lb%d" % t]], T["qin%d" % t]
             for h in both:
                 a, b, n = 16 * h, 2 + h, 16 + h
                 tt(half(T.bx, h), at(X, T.off, 32 * S + a), q(h), A.is_ge, Xr + [qn[h], "off%d%d" % (S, h)], ["bx%d" % h], gat=H)
-                mm(ps[b][:, 64:80], [(T.n256[:], fl(96 * h + k, 96 * h + 96, 6)) for k in range(1, 6)], ["n256"] + fls, ["px%d" % h], [b], stop=False)
-                mm(ps[b][:, 64:80], turns(T.E, lambda i: T.bx[:, H * h + i:H * h + H:16]), ["E", "bx%d" % h], ["py%d" % h], [b], start=False)
-                ts(fail(a, a + 16), ps[b][:, 64:80], 7.5 - 256 * S, A.is_lt, ["px%d" % h, "py%d" % h, "zero"], ["fail%d" % h], [b])
+                mm(ps[b][:, 64:80], [(T.n256[:], fl(96 * h + k, 96 * h + 96, 6)) for k in range(3, 6)], ["n256"] + fls[2:], ["px%d" % h], [b], stop=False)
+                mm(ps[b][:, 64:80], turns(T.E, lambda i: T.bx[:, H * h + i:H * h + H:16]), ["E", "bx%d" % h], ["pc%d" % h], [b], start=False, stop=False)
+                mm(ps[b][:, 64:80], [(T.n256[:], fl(96 * h + k, 96 * h + 96, 6)) for k in (1, 2)], ["n256"] + fls[:2], ["py%d" % h], [b], start=False)
+                ts(fail(a, a + 16), ps[b][:, 64:80], 7.5 - 256 * S, A.is_lt, ["px%d" % h, "py%d" % h, "zero2"], ["fail%d" % h], [b])
                 scan(cum(a + 1, a + 17), fail(a, a + 16), fail(a, a + 16), cum(16, 17) if h else 0.0, A.add, A.max,
                      ["fail%d" % h] + nm("cum", range(h)), ["cum%d" % h])
                 tt(prod(a, a + 16), fail(a, a + 16), cc(a, a + 16), A.mult, ["fail%d" % h, "cc%d" % h], ["prod%d" % h])
@@ -469,6 +525,7 @@ def rank_program(g, core, T, topo):
                    ["ones", "crow0", "idn", "cc%d" % h, "tri", "triA", "Ni", "blk", "fail%d" % h, "prod%d" % h] + nm("cum", range(h + 1)), ["pp%d" % h], [b])
                 copy(msg[h][:], ps[b][:, 96:96 + n], ["pp%d" % h], ["msg%d%d" % (t, h)], [b])
                 send(land[h][:], msg[h][:], 0, "r%s%d" % ("ab"[h], t), ["msg%d%d" % (t, h)], "land%d%d" % (t, h))
+                ops[-2]["up"] = OPT["up"][h]
 
         def gather(dst, name, B, Br, offs, on, h, e):
             if e == "a":
@@ -478,26 +535,30 @@ def rank_program(g, core, T, topo):
 
         ob = T["ob%d" % t]
         for h in both:
+            gather(T.Gp, "Gp", TB, Tr, T.poff, "poff", h, OPT["gp"][last][h])
+        for hs in ([both] if OPT["jm"][last] else [(0,), (1,)]):
+            a, e = hs[0], hs[-1] + 1
+            mm(ps[a][:, 96:96 + 16 * (e - a)], turns(T.Ej, lambda i: T.Gp[:, H * a + i:H * e:16]), ["Ej"] + nm("Gp", hs), ["pl%d" % a], [a])
+            copy(T.joff[:, 16 * a:16 * e], ps[a][:, 96:96 + 16 * (e - a)], ["pl%d" % a], nm("joff", hs), [a])
+        for h in both:
             a, b, b2 = 16 * h, 4 + h, 6 + h
             Gp, Gj, ab, new = half(T.Gp, h), half(T.Gj, h), half(T.ab, h), slice(o + H * h, o + H * h + H)
             G = ["Gp%d" % h, "Gj%d" % h]
-            gather(T.Gp, "Gp", TB, Tr, T.poff, "poff", h, "a")
-            mm(ps[h][:, 64:80], turns(T.Ej, lambda i: T.Gp[:, H * h + i:H * h + H:16]), ["Ej", G[0]], ["pl%d" % h], [h])
-            copy(T.joff[:, a:a + 16], ps[h][:, 64:80], ["pl%d" % h], ["joff%d" % h], [h])
-            gather(T.Gj, "Gj", TB, Tr, T.joff, "joff", h, "a")
+            gather(T.Gj, "Gj", TB, Tr, T.joff, "joff", h, OPT["gj"][last][h])
             gather(T.Mp, "Mp", M, Mr, T.poff, "poff", h, OPT["lmp" if last else "mp"][h])
             tt(half(T.t2, h), at(M, T.joff, a), half(T.Mp, h), A.max, Mr + ["joff%d" % h, "Mp%d" % h], ["t2%d" % h], gat=H)
             pt, tab, pd, dif = nm("pt%d" % h, range(3)), ps[b2][:, 0:H], ["pb%d" % b, "pd%d" % b], ps[b][:, 0:H]
             mm(dif, [(SLp, Gp)], ["SLp", G[0]], pd[:1], [b], H, True, False)
             mm(dif, [(SLn, Gj)], ["SLn", G[1]], pd[1:], [b], H, False, True)
-            mm(tab, ([] if last else [(Ms, TB[:, H * h:H * h + H])]) + [(Ma, Gp)], Man + ["Ms", G[0]] + parts, [pt[0], "pb%d" % b2] + (dls if h else []), [b2], H, True, False)
-            mm(tab, [(Mb, Gj)], Mbn + [G[1]], [pt[1]], [b2], H, False, False)
             if OPT["lab" if last else "ab"][h] == "a":
                 act(ab, dif, F.Abs, pd, ["ab%d" % h], [b], n=H)
             else:
                 ts(ab, dif, 0.0, A.not_equal, pd, ["ab%d" % h], [b], H)
-            mm(tab, [(Mc, ab)], Mcn + ["ab%d" % h], [pt[2]], [b2], H, False, True)
-            act(TB[:, new], tab, F.Relu, pt + ["pb%d" % b2, "cols"], ["Tn%d%d" % (t + 1, h)], [b2], bias=col(4 + t), n=H)
+            if not last:
+                mm(tab, [(Ms, TB[:, H * h:H * h + H]), (Ma, Gp)], Man + ["Ms", G[0]] + parts, [pt[0], "pb%d" % b2] + (dls if h else []), [b2], H, True, False)
+                mm(tab, [(Mb, Gj)], Mbn + [G[1]], [pt[1]], [b2], H, False, False)
+                mm(tab, [(Mc, ab)], Mcn + ["ab%d" % h], [pt[2]], [b2], H, False, True)
+                act(TB[:, new], tab, F.Relu, pt + ["pb%d" % b2, "cols"], ["Tn%d%d" % (t + 1, h)], [b2], bias=col(4 + t), n=H)
             mn, pu, bnd = ["Mn%d%d" % (t + 1, h)], ["pu%d" % b, "pv%d" % b], ps[b][:, H:K]
             onv = last or OPT["bound"][h] == "v"
             mm(bnd, ([] if onv else [(Ni, q(h))]) + [(T.idn[:], half(T.t2, h))], ["idn", "Ni", "t2%d" % h, qn[h]], pu[:1], [b], H, True, False)
@@ -510,25 +571,37 @@ def rank_program(g, core, T, topo):
                 mm(dif, [(T.idn[:], half(T.mr, h))], ["idn", "mr%d" % h], pd[1:], [b], H, False, True)
                 act(M[:, new], dif, F.Identity, pd, mn, [b], n=H)
             dma("s", T.ym[:, K * t + H * h:K * t + H * h + H], M[:, new], 256 * H, mn)
+        if last:
+            def rows(base, G, cs, n=96):
+                return [(BM[:, base + 3 - c:base + 3 + n - c], G[:, 128 * c:128 * c + 128]) for c in cs]
+            fin = ps[6][:, 0:128]
+            mm(ps[7][0:32, H:H + 128], rows(1712, T.Gp, range(4), 32), ["QP", "Gp0", "Gp1"], ["pu7"], [7], 128)
+            act(ob[0:32, :], ps[7][0:32, H:H + 128], F.Identity, ["pu7"], ["obp"], [7], n=128)
+            dma("a", T.ypar[:, K * t:K * t + K], ob[0:32, :], 32 * K, ["obp"])
+            mm(ps[6][0:64, 0:128], rows(1648, T.Gp, range(4), 64), ["QP", "Gp0", "Gp1"], ["pb6"], [6], 128, True, False)
+            for h in both:
+                mm(ps[6][0:64, 0:128], rows(1752, T.Gj, (2 * h, 2 * h + 1), 64), ["QJ", "Gj%d" % h], ["pf%d" % h], [6], 128, False, h == 1)
+            pf = ["pb6", "pf0", "pf1"]
+            ts(T.same[0:32, :], ps[6][0:32, 0:128], 0.0, A.is_equal, pf, ["same"], [6], 128)
+            tt(T.far[0:32, :], ps[6][32:64, 0:128], T.same[0:32, :], A.mult, pf + ["same"], ["far"], [6], 128)
+            tt(ob[32:64, :], ps[7][0:32, H:H + 128], T.far[0:32, :], A.add, ["pu7", "far"], ["jmp"], [7], 128)
+            dma("a", T.yjump[:, K * t:K * t + K], ob[32:64, :], 32 * K, ["jmp"])
+            return
         for h in both:
             mm(ps[6][0:64, H:H + 128], [(BM[:, 131 - c:195 - c], TB[:, o + 128 * c:o + 128 * c + 128]) for c in (2 * h, 2 * h + 1)],
                ["Mo", "Mo2", "Tn%d%d" % (t + 1, h)] + (["Tn%d0" % (t + 1)] if h else []), ["pu6" if h == 0 else "pv6"], [6], 128, h == 0, h == 1)
-        if last and OPT["lout"] == "v":
-            copy(ob[0:64, :], ps[6][0:64, H:H + 128], ["pu6", "pv6"], ["ob%d" % t], [6], 128)
-        else:
-            act(ob[0:64, :], ps[6][0:64, H:H + 128], F.Identity, ["pu6", "pv6"], ["ob%d" % t], [6], n=128)
-        dma("a" if last else "s", T.yjump[:, K * t:K * t + K], ob[32:64, :], 32 * K, ["ob%d" % t])
+        act(ob[0:64, :], ps[6][0:64, H:H + 128], F.Identity, ["pu6", "pv6"], ["ob%d" % t], [6], n=128)
+        dma("s", T.yjump[:, K * t:K * t + K], ob[32:64, :], 32 * K, ["ob%d" % t])
         dma("s", T.ypar[:, K * t:K * t + K], ob[0:32, :], 32 * K, ["ob%d" % t])
-        if last:
-            return
 
         for h in both:
             alt, out, pa = ps[h][:, H:K], T.W2[:, K + H * h:K + H * h + H], ["pa%d" % h, "pw%d" % h]
             if OPT["alt"][h] == "a":
                 gather(T.Xp, "Xp", X, Xr, T.poff, "poff", h, "a")
-                for c, name, b in ((ps[2 + h][:, H:K], "ps%d" % h, 2 + h), (alt, pa[0], h)):
-                    mm(c, [(T.idn[:], q(h)), (T.idn[:], half(T.Xp, h))], ["idn", qn[h], "Xp%d" % h], [name], [b], H, True, b != h)
-                act(half(T.wrap, h), ps[2 + h][:, H:K], F.Sigmoid, ["ps%d" % h], ["wrap%d" % h], [2 + h], bias=400.0 * (t - 255.5), scale=400.0, n=H)
+                terms, tn = [(T.idn[:], q(h)), (T.idn[:], half(T.Xp, h))], ["idn", qn[h], "Xp%d" % h]
+                mm(alt, terms, tn, pa[:1], [h], H)
+                act(half(T.wrap, h), alt, F.Sigmoid, pa[:1], ["wrap%d" % h], [h], bias=400.0 * (t - 255.5), scale=400.0, n=H)
+                mm(alt, terms, tn, pa[:1], [h], H, True, False)
                 t0 = float(t)
             else:
                 act(half(T.q1, h), q(h), F.Identity, [qn[h]], ["q1%d" % h], bias=t - 256.0, n=H)
@@ -556,6 +629,10 @@ def rank_program(g, core, T, topo):
         if t + 2 < RO:
             send(T["qin%d" % (t + 1)][:], X[:, o + K:o + 2 * K], 256 * K, "rq%d" % (t + 1), q2, "qin%d" % (t + 1))
 
+    starts = [0]
     for t in range(RO):
+        starts.append(len(ops))
         one_round(t)
+    line_up(ops, starts + [len(ops)])
+    OPT["starts"] = starts + [len(ops)]
     emit(g, T, ops)

from concourse.mybir import AluOpType as A, ActivationFunctionType as F

V, K, CAP, S, RO = 2304, 512, 192, 5, 3
W = V + RO * K
H = K // 2
BIG = 32768.0
MID = 1920.0
C0 = 12582913.0
C2 = 3072.0
BACK = C2 - MID / 4096
P = 6
OPT = {"war": 0, "up": (0.0, 0.0), "dup": 0.0, "xa": (320, 320, 320, 320, 160), "xn": 2, "bound": "aa", "mp": "aa", "alt": "vv", "ab": "aa", "lmp": "va", "lab": "aa",
       "line": ("S",), "mn": 1, "tbv": (12, 13, 14, 15), "cuts": (0, 144, 288, 432, 576), "zat": 3,
       "d3": "vv", "pm": (0, 0), "jm": (0, 1), "gp": ("aa", "av"), "gj": ("aa", "av"), "cyc": 0.95, "gat": 1.4, "sct": 3.5, "far": 150.0, "own": 100.0, "fly": 1900.0}
LINES = {
"v": ("hs0 hs0 off00 hs1 sm00 hs1 off01 v0 sm10 pj0 d00 sx00 so00 sx01 off10 pj1 d01 sm00 so01 off11 sm10 sx11 d00 pj0 so10 sx10 off20 pj1 d01 sm00 so11 off21 sm10 sx20 d00 pj0 so20 sx21 off30 d01 pj1 so21 sm00 off31 sm10 sx31 d00 pj0 sx30 so30 d01 pj1 off40 so31 sm00 off41 sm10 sx00",
 "d00 pj0 sx01 so40 pj1 d01 off50 so41 bx0 off51 dl00 bx1 dl1 dl01 po0 po1 fail0 poff0 cum0 prod0 poff1 fail1 cum1 prod1 msg0 Xp1 msg1 Xp0 joff0 t20 joff1 pq t21 come got come go goff Xn0 Xn1",
 "sx01 pj0 pj1 dl1 d00 d01 so41 so40 dl01 dl00 po0 po1 poff0 poff1 Gp1 Mp0 joff0 Gj1 t20 t21 same far jmp Mn0 Mn1",
 "sm00 <zero2 sm10 pj0 d00 so00 <Mc2 v0 <Zc off10 pj1 d01 <QP <Ma0 so01 sm00 off11 <zero sm10 sx00 <wf pj0 d00 so10 off20 sx01 d01 pj1 sm00 so11 off21 sm10 sx11 pj0 d00 sx20 so20 sx10 d01 pj1 off30 so21 sm00 off31 sx31 sm10 sx21 pj0 d00 sx30 so30 d01 pj1 off40 so31 sm00 off41 sm10 sx00"),
"a": ("sz0 sz1 xs sz0 sx09 sz1 xs <ob sz0 sx19 sz1 fl5 xs sz0 sz1 sx29 xs sz0 fl4 sz1",
 "xs sx39 fl3 sx09 q11 fl1 fl2 q10 Gp0 Gp1 Mp0 Mp1 wrap0 Gj0 wrap1 Gj1 alt0 ab0 ab1 alt1 room dv1 mr0 mr1 Tn1 Mn0 Mn1 Tn0",
 "xs sx39 fl3 sx09 fl1 fl2 Gp0 Mp1 Gj0 ab0 ob ab1",
 "sz0 sz1 sz0 sz1 xs sz0 xs sz1 sx09 <Ew xs sz0 fl5 sz1 sx29 sx19 xs sz0 sz1 fl4"),
"p": ("<pu6 pn0 pn1 <pv6 pm0 pm1 pn0 pb4 pn1 pm0 dl5 pm1 pb5 pb6 pn1 pn0 pm0 pm1 pb4 dl4 dl3 pn0 pn1 pm0 pm1 pb6 dl2 pn0 pn1 pb5 pm0 pm1 pb4",
 "px0 px1 pb6 pc0 py0 pc1 py1 pp0 pp1 pl0 pb5 pr pl1 pb4 pa0 pd4 pw0 pa1 pu4 pd5 pt10 pw1 pt00 pv4 pu5 pt11 pv5 pb5 pt12 pt01 pt02 pb4 pd4 pd5 ph0 ph1",
 "pb6 pl0 pu7 pb5 pb4 pb6 pd4 pf0 pf1 pd5 pu4 pv4 pu5 pv5",
 "pn0 pn1 pm0 pm1 pn1 pn0 dl5 pm0 pm1 pb4 pn0 dl4 pm0 pb5 pn1 pm1 pb6 dl3 pn0 pn1 pb4 pm0 pm1 pb6 pb5 pn0 pn1 pm0 pm1 pb4 dl2"),
}
BF, FP, I32, U16 = "bfloat16", "float32", "int32", "uint16"
SCRATCH = {}
for _dt, _w, _names in (
        (BF, [W], "X M TB"), (I32, [576], "raw loi"), (BF, [576], "hi lo"), (BF, [520], "R"), (BF, [144], "E Ew Ej"),
        (BF, [128], "ones idn blk tri triA n256"), (BF, [64, 16], "rows"), (FP, [8], "cols"), (BF, [1856], "BM"),
        (BF, [H, 2], "st0 st1"), (BF, [K, 2], "sx0 sx1"), (FP, [128], "idf nif"), (FP, [S, 32 * P], "so"),
        (FP, [32, 4] if P == 4 else [192], "d0"), (BF, [32], "hrow"), (BF, [144], "E16"), (U16, [192], "off"),
        (U16, [32], "poff joff goff"), (FP, [192], "po"), (FP, [64], "go"),
        (I32, [32], "u0s hs"), (I32, [4], "ws"), (FP, [1], "wf got room"), (FP, [32], "i16 ai v0"),
        (U16, [16], "ma0 ma1 la0 la1"), (U16, [17], "mb0 mb1 lb0 lb1"), (BF, [2 * K], "W2"), (FP, [128], "ob0 ob1 ob2 same far"),
        (BF, [K], "bx qin0 qin1 Gp Gj Mp Xp t2 ab mr xs wrap q1")):
    for _n in _names.split():
        SCRATCH[_n] = ("sbuf", [128] + _w, _dt)
for _b in range(8):
    SCRATCH["ps%d" % _b] = ("psum", [128, 512], FP)
SEMAPHORES = ["v", "a", "p", "g", "sent", "rq0", "rq1", "ra0", "ra1", "rb0", "rb1"] + ["d%d" % _i for _i in range(24)]
ORDER = []


def line_up(ops, starts):
    def tag(o):
        n = o["w"][0]
        return n[:-2] + n[-1] if n[:2] in ("ms", "Xn", "Tn", "Mn") else n[:2] if n[:2] == "ob" else n
    for e, (walk, turn, end, first) in LINES.items():
        before, used = None, set()
        for t in range(RO):
            for name in ((walk if t else first) + " " + (turn if t < RO - 1 else end)).split():
                a, b = (starts[t], starts[t + 1]) if name[0] == "<" else (starts[t + 1], starts[t + 2])
                for i in range(a, b):
                    if ops[i]["e"] == e and ops[i]["kind"] == "op" and i not in used and tag(ops[i]) == name.lstrip("<"):
                        used.add(i)
                        ops[i]["behind"] = before
                        before = i
                        break


def needs(ops):
    lastw, readers, out = {}, {}, []
    for i, o in enumerate(ops):
        deps = set(lastw[r] for r in o["r"] + o["w"] if r in lastw)
        for r in o["w"]:
            deps.update(readers.get(r, []))
        for r in o["r"]:
            readers.setdefault(r, []).append(i)
        for r in o["w"]:
            lastw[r] = i
            readers[r] = []
        out.append(deps - {i})
    return out


def arrange(ops):
    n = len(ops)
    pre = [[(j, OPT["own"] if ops[j]["e"] == ops[i]["e"] and ops[j]["kind"] == "op" else OPT["far"]) for j in d] for i, d in enumerate(needs(ops))]
    inorder, tags = {}, {}
    for i, o in enumerate(ops):
        for k in o.get("line", ()):
            if k in tags:
                pre[i].append((tags[k], 0.0))
            tags[k] = i
        if o.get("behind") is not None:
            pre[i].append((o["behind"], 0.0))
        if o["kind"] == "arrive":
            pre[i].append((i - 1, 0.0))
        elif o["kind"] != "op":
            if o["e"] in inorder:
                pre[i].append((inorder[o["e"]], -1e6))
            inorder[o["e"]] = i
    todo, seen = [], set()
    while len(todo) < n:
        i = [i for i in range(n) if i not in seen and all(j in seen for j, d in pre[i])][0]
        todo.append(i)
        seen.add(i)
    chain = [0.0] * n
    for i in reversed(todo):
        chain[i] += ops[i]["c"] + ops[i]["late"] + ops[i].get("up", 0.0)
        for j, d in pre[i]:
            chain[j] = max(chain[j], max(d, -ops[j]["late"]) + chain[i])
    start, end, free, bank, pipe = {}, {}, {}, {}, [0.0]
    while todo:
        est, ready = {}, []
        for i in todo[:160]:
            o, ok = ops[i], True
            t = free.get(o["e"], 0.0)
            for j, d in pre[i]:
                if j in end:
                    t = max(t, end[j] + d)
                else:
                    ok = False
                    t = max(t, est[j] + ops[j]["c"] + ops[j]["late"] + d)
            for b in o["b"]:
                if b in bank and bank[b][0] != o["e"]:
                    t = max(t, bank[b][1] + OPT["far"])
            est[i] = t
            if ok:
                ready.append(i)
        ready.sort(key=lambda i: (est[i], -chain[i]))
        pick = None
        for i in ready:
            a, c = est[i], ops[i]["c"]
            if not any(ops[h]["e"] == ops[i]["e"] and h != i and est[h] < a + c and chain[h] > chain[i]
                       and max(est[h] + chain[h], est[h] + ops[h]["c"] + chain[i]) < max(a + chain[i], a + c + chain[h]) for h in est):
                pick = i
                break
        if pick is None:
            pick = max(ready, key=lambda i: chain[i] - est[i])
        o = ops[pick]
        start[pick] = est[pick]
        end[pick] = free[o["e"]] = est[pick] + o["c"]
        if o["kind"] == "dma":
            pipe[0] = max(pipe[0], end[pick] + 800.0) + o["late"] - 1300.0
            end[pick] = pipe[0] + 500.0
        elif o["kind"] == "send":
            end[pick] += o["late"]
        if o["e"] is None:
            free[None] = 0.0
        for b in o["b"]:
            bank[b] = (o["e"], end[pick])
        todo.remove(pick)
    return list(start)


def emit(g, T, ops):
    Q = {"v": g.vector, "a": g.scalar, "p": g.tensor, "g": g, "s": g.sync}
    before = needs(ops)
    if not ORDER:
        ORDER.extend(arrange(ops))
    order = ORDER
    place = {i: k for k, i in enumerate(order)}
    bank = {}
    known = {e: {} for e in Q}
    seq = {e: 0 for e in Q}
    need = set()
    for i in order:
        o = ops[i]
        e = o["e"]
        deps = set(before[i])
        for b in o["b"]:
            for e2, j in bank.get(b, {}).items():
                if e2 != e:
                    deps.add(j)
            bank.setdefault(b, {})[e] = i
        o["waits"] = []
        if e is not None:
            for j in sorted(deps, key=lambda j: -place[j]):
                if OPT["war"] and ops[j]["e"] == e and ops[j]["kind"] == o["kind"] == "op" and not set(ops[j]["w"]) & set(o["r"] + o["w"]):
                    continue
                key, n = ops[j]["id"]
                if known[e].get(key, 0) >= n:
                    continue
                o["waits"].append(j)
                need.add(j)
                for k2, n2 in ops[j]["clock"].items():
                    if known[e].get(k2, 0) < n2:
                        known[e][k2] = n2
        if o["sem"] is None:
            seq[e] += 1
            o["id"] = (e, seq[e])
        else:
            o["id"] = (o["sem"], 1)
        o["clock"] = dict(known[e]) if e is not None else {}
        o["clock"][o["id"][0]] = o["id"][1]
    total, waited = {}, {}
    for i in order:
        o = ops[i]
        if o["sem"] is None:
            if i in need:
                total[o["e"]] = total.get(o["e"], 0) + 1
                o["sig"] = (o["e"], total[o["e"]])
        else:
            total[o["sem"]] = total.get(o["sem"], 0) + o["n"]
            o["sig"] = (o["sem"], total[o["sem"]])
    for i in order:
        o = ops[i]
        if o["e"] is None:
            continue
        for j in o["waits"]:
            s, n = ops[j]["sig"]
            Q[o["e"]].wait_ge(T.sem[s], n)
            waited[s] = max(waited.get(s, 0), n)
        ins = o["f"]()
        if o["kind"] == "dma":
            ins.then_inc(T.sem[o["sem"]], 16)
        elif o["kind"] == "op" and i in need:
            ins.then_inc(T.sem[o["e"]], 1)
    for s in total:
        if waited.get(s, 0) < total[s]:
            g.wait_ge(T.sem[s], total[s])


def rank_program(g, core, T, topo):
    rank = T.rank_of(core)
    if rank is None:
        return
    N = len(T.cores)
    nxt, prv = T.cores[(rank + 1) % N], T.cores[(rank - 1) % N]
    rid, pid = topo.addr(nxt, core)
    mask, n_out, n_in = topo.mask(core, nxt), len(topo.engines(core, nxt)), len(topo.engines(prv, core))
    Ve, Sc, Pe = g.vector, g.scalar, g.tensor
    ops, nd = [], [0]
    ps = [T["ps%d" % b] for b in range(8)]
    st, sx = [T.st0, T.st1], [T.sx0, T.sx1]
    X, M, TB, BM = T.X, T.M, T.TB, T.BM
    cyc = OPT["cyc"]

    def op(e, f, r=(), w=(), b=(), n=0, gat=0, sct=0):
        c = cyc * max(n, 64) + 10
        if gat or sct:
            c = cyc * (gat * OPT["gat"] + sct * OPT["sct"]) + (50 if e == "v" else 65)
        ops.append({"e": e, "f": f, "r": list(r), "w": list(w), "b": list(b), "sem": None, "kind": "op", "c": c, "late": 0.0, "n3": (n, gat, sct)})

    def dma(e, out, in_, size, r=(), w=()):
        q = g.sync if e == "s" else g.scalar
        ops.append({"e": e, "f": lambda: q.dma_start(out, in_), "r": list(r), "w": list(w), "b": [],
                    "sem": "d%d" % nd[0], "n": 16, "kind": "dma", "c": 60.0, "late": 1500.0 + size / 250.0})
        nd[0] += 1

    def send(out, in_, size, sem, r, land):
        ops.append({"e": "g", "f": lambda: g.remote_dma(out, in_, T.sem[sem], T.sem.sent, pid, rid, mask),
                    "r": list(r), "w": [], "b": [], "sem": "sent", "n": n_out, "kind": "send", "c": 300.0, "late": OPT["fly"] + size / 128.0})
        ops.append({"e": None, "r": [], "w": [land], "b": [], "sem": sem, "n": n_in, "kind": "arrive", "c": 0.0, "late": 0.0})

    def mm(out, pairs, r, w, b, n=64, start=True, stop=True, line=True):
        def f():
            for i, (l, x) in enumerate(pairs):
                ins = Pe.matmul(out, l, x, start and i == 0, stop and i == len(pairs) - 1)
            return ins
        op("p", f, r, w, b, len(pairs) * max(n, 64) / 2)
        ops[-1]["line"] = b if line else ()

    def turns(lh, rhs):
        return [(lh[:, 15 - i:143 - i], rhs(i)) for i in range(16)]

    def memset(ap, c, w, n=0):
        op("v", lambda: Ve.memset(ap, c), (), w, (), n)

    def act(out, in_, fn, r, w, b=(), bias=0.0, scale=1.0, n=0, gat=0):
        op("a", lambda: Sc.activation(out, in_, fn, bias=bias, scale=scale), r, w, b, n, gat)

    def copy(out, in_, r, w, b=(), n=0, gat=0, sct=0):
        op("v", lambda: Ve.tensor_copy(out, in_), r, w, b, n, gat, sct)

    def tt(out, a, c, f, r, w, b=(), n=0, gat=0):
        op("v", lambda: Ve.tensor_tensor(out, a, c, f), r, w, b, n, gat)

    def ts(out, a, s1, f1, r, w, b=(), n=0, s2=None, f2=None):
        if f2 is None:
            op("v", lambda: Ve.tensor_scalar(out, a, s1, None, f1), r, w, b, n)
        else:
            op("v", lambda: Ve.tensor_scalar(out, a, s1, s2, f1, f2), r, w, b, n)

    def scan(out, a, c, first, f1, f2, r, w, b=(), n=0):
        op("v", lambda: Ve.tensor_tensor_scan(out, a, c, first, f1, f2), r, w, b, n)

    def iota(out, pat, base, cm, r, w, n, small=True):
        if small:
            op("g", lambda: g.iota(out, pat, base, cm, allow_small_or_imprecise_dtypes=True), r, w, (), 2 * n + 140)
        else:
            op("g", lambda: g.iota(out, pat, base, cm), r, w, (), 2 * n + 140)

    def sel(out, in_, pat, cmp, fill, base, cm, r, w, n=128):
        op("g", lambda: g.affine_select(out, in_, pat, cmp, fill, base, cm), r, w, (), 2 * n + 180)

    def put(ap, pat, base, val, name, n=16):
        sel(ap, ap, pat, A.not_equal, val, base, 1, [name], [name], n)

    def col(k):
        return T.cols[:, k:k + 1]

    def xr(t):
        return ["n0"] + ["n%d%d" % (i, h) for i in range(1, t + 1) for h in (0, 1)]

    def win(B, t, offs, a, b):
        return B[:, 0:V + K * t].indirect(offs[:, a:b])

    def nm(n, hs):
        return [n + str(h) for h in hs]

    def part(base):
        return lambda a, b, step=1: BM[:, base + a:base + b:step]
    fl, dv, fail, cum, prod, cc = part(1040), part(1232), part(1344), part(1384), part(1424), part(1464)
    crow0, crow1 = BM[0:1, 1296:1312], BM[0:1, 1312:1344]
    dl = ps[7]
    both = (0, 1)

    for k, src in enumerate((T.par, T.jump, T.ln)):
        dma("s" if k == 1 else "a", T.raw[32 * k:32 * k + 32, :], src[:], 32 * V, w=["raw%d" % k])
    dma("s", T.u0s[:], T.u0[:], 128 * 128, w=["u0s"])
    dma("s", X[:, V:V + K], T.q[:], 256 * K, w=["Xn10", "Xn11"])
    dma("s", M[:, 0:V], T.m[:], 256 * V, w=["Mn0"])
    dma("s", X[:, 0:V], T.x[:], 256 * V, w=["Xn0"])
    dma("s", T.ws[:, 0:1], T.w[:], 512, w=["ws"])
    Rf = (0, 2, 4, 5)
    Rn = ["R%d" % f for f in Rf]
    iota(T.raw[96:128, :], [[1, 576]], 0, 576, [], ["raw3"], 576, False)
    memset(T.ones[:], 1.0, ["ones"])
    memset(T.R[:], 0.0, Rn, 260)
    segs = [(0, 1, 0, 8, 1 / 256), (0, 1, 1, 8, 16.0), (0, 1, 2, 8, 16.0), (0, 1, 3, 8, -16.0),
            (1, 2, 0, 16, -MID / 256), (1, 2, slice(1, 3), 0, -MID * 16), (1, 2, 3, 16, MID * 16),
            (2, 3, 1, 8, 1.0), (2, 3, 2, 8, 1.0), (2, 3, 3, 8, -1.0), (3, 4, slice(0, 6, 2), 0, -4128.0),
            (3, 4, 5, 16, -4128.0), (4, 7, 14, 16, 1.0)]
    segs += [(4 + t, 5 + t, 5, 16, float(V + K * t)) for t in range(RO)]
    rown = ["row%d" % k for k in range(len(segs))]
    memset(T.rows[0:1, 0:56, :], 0.0, rown, 448)
    memset(T.E[:], 0.0, ["E"], 72)
    iota(T.rows[0:1, 56:64, :], [[0, 8], [1, 16]], 0, 0, ["raw3"], ["rowp"], 128)
    for k, f in enumerate(Rf):
        sel(T.R[:, 8 + f:520:16], T.ones[:, 0:32], [[-1, 4], [0 if k == 3 else -4, 8]], A.is_equal, 0.0, -32 * k, 1, ["ones"], ["R%d" % f], 32)
    sel(T.E[:, 15::16], T.ones[:, 0:9], [[-16, 9]], A.is_ge, 0.0, 0, 1, ["ones"], ["E"], 9)
    iota(T.i16[:], [[16, 32]], 0, 0, [], ["i16"], 32)
    sel(T.E[:, 15::16], T.E[:, 15::16], [[16, 9]], A.is_ge, 0.0, 15, -1, ["E"], ["E"], 9)
    for i, (a, b, f, step, c) in enumerate(segs):
        memset(T.rows[0:1, 8 * a:8 * b, slice(f, 16, step) if step else f], c, [rown[i]])

    def turn():
        for k in range(8):
            ins = Pe.matmul(ps[7][:, 300 + k:301 + k], T.rows[0:1, 8 * k:8 * k + 8, :], T.ones[0:1, 0:1], True, True)
        return ins
    op("p", turn, ["ones", "rowp"] + rown, ["pu7"], [7], 256)
    op("a", lambda: Sc.activation(T.hrow[0:1, 0::2], T.ones[0:1, 0:16], F.Sigmoid, scale=-400.0), ["ones"], ["hrow0"], (), 1400)
    act(T.cols[:], ps[7][:, 300:308], F.Identity, ["pu7", "hrow0"], ["cols"], [7])
    act(T.E16[:], T.E[:], F.Identity, ["E"], ["E16"], scale=1 / 16, n=144)
    if P == 4:
        memset(T.d0[:], 0.0, ["d0a", "d0b"], 128)
    else:
        act(T.d0[:, 0::3], T.ones[:, 0:64], F.Identity, ["ones"], ["d0a"], scale=0.0)
        act(T.d0[:, 2::3], T.ones[:, 0:64], F.Identity, ["ones"], ["d0a"])
        act(T.d0[:, 3::6], T.ones[:, 0:32], F.Identity, ["ones"], ["d0a", "d0b"])
    for h in both:
        act(ps[h][:, 0:16 * P:P], T.ones[:, 0:16], F.Identity, ["ones"], ["pk%d" % h], [h], scale=-4097 / 4096)
        if P == 6:
            for k in (1, 3):
                act(ps[h][:, k:96:6], T.ones[:, 0:16], F.Identity, ["ones"], ["pz%d" % h], [h], scale=0.0)
    raws = ["raw%d" % k for k in range(4)]
    cuts = OPT["cuts"]
    for hf, (a, e) in enumerate(zip(cuts, cuts[1:])):
        ts(T.loi[:, a:e], T.raw[:, a:e], 31, A.bitwise_and, raws, ["loi%d" % hf], n=e - a)
        ts(T.hi[:, a:e], T.raw[:, a:e], 4112.5, A.add, raws, ["hi%d" % hf], n=e - a)
        copy(T.lo[:, a:e], T.loi[:, a:e], ["loi%d" % hf], ["lo%d" % hf], n=e - a)
    copy(T.off[:, 0:32], T.u0s[:], ["u0s"], ["off00", "off01"])
    Mcn, Man, Mbn = nm("Mc", (2, 3, 4)), nm("Ma", (0, 1, 3, 4)), ["Mb2"]
    for a, e, w in ((768, 1024, ["Zc", "Ni"]), (1024, 1344, ["zero", "crow0", "crow1"]), (1344, 1648, ["zero2", "cc0", "cc1", "SLn"]), (1648, 1856, ["QP", "QJ"]),
                    (0, 384, Mcn + ["Mo", "Mo2", "SLp"]), (384, 768, Man + Mbn + ["Ms"])):
        op("v", lambda a=a, e=e: Ve.memset(BM[:, a:e], 0.0), ["lo%d" % OPT["zat"]], w, (), (e - a) / 2)
    SLp, SLn = BM[:, 0:128], BM[:, 1520:1648]
    parts = []
    for hf, (a, e) in enumerate(zip(cuts, cuts[1:])):
        for c in range(4):
            i = 4 * hf + c
            b, n = 2 + i % 6, e - a
            wide = ["pb%d" % b, "pu%d" % b]
            mm(ps[b][:, 0:n], [(T.R[:, 8 + 128 * c:136 + 128 * c], T.hi[:, a:e]), (T.R[:, 128 * c:128 * c + 128], T.lo[:, a:e])],
               Rn + ["hi%d" % hf, "lo%d" % hf], wide, [b], n)
            out = TB[:, 576 * c + a:576 * c + e]
            if i in OPT["tbv"]:
                ts(out, ps[b][:, 0:n], col(3), A.add, wide + ["cols"], ["tb%d" % i], [b], n)
            else:
                act(out, ps[b][:, 0:n], F.Identity, wide + ["cols"], ["tb%d" % i], [b], bias=col(3), n=n)
            parts.append("tb%d" % i)
    Mc, Ma, Mb, Ms, Zc, Ni = [BM[:, 128 * k:128 * k + 128] for k in range(2, 8)]
    Mo1, Mo2 = BM[:, 131:163:4], BM[:, 163:195:4]

    def bm(k, f, step):
        return BM[:, 128 * k + f:128 * k + 128:step]
    sel(T.idn[:], T.ones[:], [[-1, 128]], A.is_equal, 0.0, 0, 1, ["ones"], ["idn"])
    sel(T.idf[:], T.ones[:], [[-1, 128]], A.is_equal, 0.0, 0, 1, ["ones"], ["idf"])
    sel(T.blk[:], T.ones[:], [[-16, 8], [0, 16]], A.is_ge, 0.0, 0, 1, ["ones"], ["blk"])
    put(Ni, [[-1, 128]], 0, -1.0, "Ni", 128)
    sel(T.blk[:], T.blk[:], [[16, 8], [0, 16]], A.is_ge, 0.0, 15, -1, ["blk"], ["blk"])
    sel(T.nif[:], T.idf[:], [[-1, 128]], A.not_equal, -1.0, 0, 1, ["idf"], ["nif"])
    sel(T.n256[:], T.idn[:], [[-1, 128]], A.not_equal, -256.0, 0, 1, ["idn"], ["n256"])
    put(Zc, [[-16, 8], [0, 16]], -6, -BIG, "Zc", 128)
    sel(T.tri[:], T.blk[:], [[16, 8], [1, 16]], A.is_ge, 0.0, -1, -1, ["blk"], ["tri"])
    sel(T.triA[:], T.tri[:], [[-1, 128]], A.not_equal, -float(H), 0, 1, ["tri"], ["triA"])
    for i, f in enumerate((4, 12, 14)):
        put(BM[:, 6:128:16], [[-16, 8]], -f, 1.0, "SLp")
        put(BM[:, 902 + 624:1024 + 624:16], [[-16, 8]], -f, -1.0, "SLn")
        put(bm(2, i + 2, 8), [[-16, 8], [0, 2]], -6, -BIG, "Mc%d" % (i + 2))
        put(bm(4, 2, 8), [[-8, 16]], -1 - i, (1.0, 1.0, -1.0)[i], "Mb2")
        put(bm(3, (0, 1, 3)[i], 8), [[-8, 16]], -5, 1.0, "Ma%d" % (0, 1, 3)[i])
        for d in (0, 8):
            put(Mo2, [[-16, 8]], -1 - i - d, (1.0, 1.0, -1.0)[i], "Mo2")
            if i == 0:
                put(Mo1, [[-16, 8]], -d, 1.0, "Mo")
    for base, name, fs in ((1651, "QP", ((4, 1.0), (12, 1.0), (14, 1.0))), (1683, "QP", ((5, -1.0), (13, -1.0))), (1715, "QP", ((5, 1.0), (13, 1.0))),
                           (1755, "QJ", ((4, -1.0), (12, -1.0), (14, -1.0))),
                           (1787, "QJ", ((1, 1.0), (9, 1.0), (2, 1.0), (10, 1.0), (3, -1.0), (11, -1.0)))):
        for f, c in fs:
            put(BM[:, base:base + 32:4], [[-16, 8]], -f, c, name)
    put(bm(3, 4, 8), [[-8, 16]], -4, 2.0, "Ma4")
    put(bm(5, 5, 8), [[-8, 16]], -5, 1.0, "Ms")
    put(bm(3, 12, 16), [[-16, 8]], -14, 2.0, "Ma4")
    send(T.qin0[:], X[:, V:V + K], 256 * K, "rq0", ["Xn10", "Xn11", "Xn0", "Mn0"], "qin0")
    act(T.ai[:], T.i16[:], F.Identity, ["i16", "cols"], ["ai"], bias=col(7))
    act(T.Ej[:], T.E[:], F.Identity, ["E", "cols"], ["Ej"], scale=col(2), n=144)
    for h in both:
        act(cc(16 * h, 16 * h + 16), T.ai[:, 0:16], F.Identity, ["ai"], ["cc%d" % h], bias=H - 1.0, scale=-1.0)
    act(T.ai[:], T.ai[:], F.Identity, ["ai"], ["ai"], bias=K - CAP + 0.5)
    act(crow0, T.ones[0:1, 0:16], F.Identity, ["ones"], ["crow0"], scale=float(H))
    act(crow1, T.ones[0:1, 0:32], F.Identity, ["ones"], ["crow1"], scale=H - CAP + 0.5)
    copy(T.wf[:], T.ws[:, 0:1], ["ws"], ["wf"])
    act(T.Ew[:], T.E[:], F.Identity, ["E", "wf"], ["Ew"], scale=T.wf[:, 0:1], n=144)

    def one_round(t):
        o = V + K * t
        last = t == RO - 1
        Xr, Mr, Tr = ["X" + n for n in xr(t)], ["M" + n for n in xr(t)], parts + ["T" + n for n in xr(t)[1:]]
        qn = nm("Xn%d" % (t + 1), both)

        def q(h):
            return X[:, o + H * h:o + H * h + H]

        def half(B, h):
            return B[:, H * h:H * h + H]

        def at(B, offs, a):
            return win(B, t, offs, a, a + 16)

        def node(s, hs):
            return T.so[:, s, 16 * P * hs[0] + P - 2:16 * P * (hs[-1] + 1):P]

        def xtest(s):
            n, b, out, k = OPT["xa"][s], 4 + s % 2, sx[(s + 1) // 2 % 2], (s + 1) % 2
            cut = [32 * ((K - n) // 32 * i // OPT["xn"]) for i in range(OPT["xn"] + 1)]
            for i, (a, e) in enumerate(zip(cut, cut[1:])):
                tt(out[:, a:e, k], win(X, t, T.off, 32 * s + a // 16, 32 * s + e // 16), X[:, o + a:o + e], A.is_ge,
                   Xr + qn + nm("off%d" % s, both if e > H else (0,)), ["sx%d%d" % (s % 4, i)], gat=e - a)
            if n:
                act(T.xs[:, 0:n], win(X, t, T.off, 32 * s + (K - n) // 16, 32 * s + 32), F.Identity, Xr + nm("off%d" % s, both if n > H else (1,)), ["xs"], gat=n)
                mm(ps[b][:, 0:n], [(Ni, X[:, o + K - n:o + K]), (T.idn[:], T.xs[:, 0:n])], ["Ni", "idn", "xs"] + qn, ["pb%d" % b], [b], n)
                act(out[:, K - n:K, k], ps[b][:, 0:n], F.Sigmoid, ["pb%d" % b], ["sx%d9" % (s % 4)], [b], bias=200.0, scale=400.0, n=n)

        def xsum(s0, n):
            B, b = sx[(s0 + 1) // 2 % 2], 6
            mm(ps[b][:, 0:32 * n], turns(T.E, lambda i: B[:, i::16, 2 - n:2]),
               ["E"] + ["sx%d%d" % (s % 4, i) for s in range(s0, s0 + n) for i in list(range(OPT["xn"])) + [9]], ["pb%d" % b], [b])
            for s in range(s0, s0 + n):
                act(fl(5 - s, 192, 6), ps[b][:, s - s0:32 * n:n], F.Sigmoid, ["pb%d" % b, "zero"], ["fl%d" % (5 - s)], [b], bias=3000.0, scale=-400.0)

        for s in range(S):
            for h in both:
                a, on = 32 * s + 16 * h, "off%d%d" % (s, h)
                if s == 0 and t > 0:
                    hs = T.hs[:, 16 * h:16 * h + 16]
                    copy(hs, ps[h][:, 192:208], ["ph%d" % h], ["hs%d" % h], [h])
                    ts(hs, hs, K - 1, A.bitwise_and, ["hs%d" % h], ["hs%d" % h])
                    ts(T.off[:, a:a + 16], hs, float(o - K), A.add, ["hs%d" % h], [on])
                sums = ps[h][:, 1:64:2] if P == 4 else ps[h][:, 2:96:3]
                act(st[h][:, :, 0], at(TB, T.off, a), F.Identity, Tr + ["cols", on], ["sz%d" % h], scale=col(0), bias=col(1), gat=H)
                tt(st[h][:, :, 1], at(M, T.off, a), q(h), A.is_ge, Mr + [qn[h], on], ["sm%d0" % h], gat=H)
                mm(sums, turns(T.E16, lambda i: st[h][:, i::16, :]), ["E16", "sz%d" % h, "sm%d0" % h], ["pm%d" % h], [h])
                whole = T.d0[:, 16 * h:16 * h + 16, 1:3] if P == 4 else T.d0[:, 96 * h + 1:96 * h + 96:3]
                ts(whole, sums, C0, A.add, ["pm%d" % h, "d0a"], ["d0%d" % h], [h], 0, C0, A.subtract)
                z0 = P // 2 - 1
                ts(ps[h][:, P - 2:16 * P:P], ps[h][:, z0:16 * P:P], 1 / 4096, A.mult, ["pm%d" % h, "pn%d" % h], ["pj%d" % h], [h], 0, C2, A.add)
                scan(T.so[:, s, 16 * P * h:16 * P * (h + 1)], T.d0[:, 16 * h:16 * h + 16, :] if P == 4 else T.d0[:, 96 * h:96 * h + 96], ps[h][:, 0:16 * P], 0.0,
                     A.mult, A.add, ["d0a", "d0b"] + [n + str(h) for n in ("d0", "pm", "pn", "pj", "pk", "pz")], ["so%d%d" % (s, h)], [h], 16 * P)
                if s < S - 1 or not last:
                    ts(T.off[:, a + 32:a + 48], node(s, (h,)), -BACK, A.add, ["so%d%d" % (s, h)], ["off%d%d" % (s + 1, h)], (), 0, 4096.0, A.mult)
            xtest(s)
            if s % 2 == 0:
                xsum(max(s - 1, 0), min(s + 1, 2))
            if s == 0:
                ts(T.v0[:], T.hs[:] if t else T.u0s[:], 1 / 4096, A.mult, ["hs0", "hs1", "u0s"], ["v0"], (), 0, BACK + (o - K if t else 0) / 4096, A.add)
            if s < S - 1:
                a, an = (node(s - 1, both), nm("so%d" % (s - 1), both)) if s else (T.v0[:], ["v0"])
                now = nm("so%d" % s, both)
                if s == 0:
                    mm(dl[:, 5:192:6], [(T.idf[:], a)], ["idf"] + an + now, ["dl5", "pb7"], [7], 256)
                if s < S - 2 or OPT["d3"][last] == "p":
                    mm(dl[:, 4 - s:192:6], [(T.nif[:], a), (T.idf[:], node(s, both))], ["idf", "nif", "dl5"] + an + now, ["dl%d" % (4 - s)], [7], 256)
        dls = ["dl00", "dl01"] + ["dl%d" % k for k in range(1, 6)]
        fls = ["fl%d" % k for k in range(1, 6)]
        if OPT["d3"][last] == "v":
            tt(dl[:, 1:192:6], node(S - 2, both), node(S - 3, both), A.subtract, nm("so%d" % (S - 2), both) + nm("so%d" % (S - 3), both) + ["dl5"], ["dl1"], [7])
        for hs in ([both] if OPT["pm"][last] else [(0,), (1,)]):
            a, e = hs[0], hs[-1] + 1
            tt(dl[:, 96 * a:96 * e:6], node(S - 1, hs), node(S - 2, hs), A.subtract,
               nm("so%d" % (S - 1), hs) + nm("so%d" % (S - 2), hs) + ["dl5"], nm("dl0", hs), [7])
            scan(T.po[:, 96 * a:96 * e], fl(96 * a, 96 * e), dl[:, 96 * a:96 * e], 0.0, A.mult, A.add, ["zero"] + nm("dl0", hs) + dls[2:] + fls, nm("po", hs), [7], 96 * (e - a))
            ts(T.poff[:, 16 * a:16 * e], T.po[:, 96 * a + 5:96 * e:6], -BACK, A.add, nm("po", hs), nm("poff", hs), (), 0, 4096.0, A.mult)

        if not last:
            msg, land, qin = [T["ma%d" % t], T["mb%d" % t]], [T["la%d" % t], T["lb%d" % t]], T["qin%d" % t]
            for h in both:
                a, b, n = 16 * h, 2 + h, 16 + h
                tt(half(T.bx, h), at(X, T.off, 32 * S + a), q(h), A.is_ge, Xr + [qn[h], "off%d%d" % (S, h)], ["bx%d" % h], gat=H)
                mm(ps[b][:, 64:80], [(T.n256[:], fl(96 * h + k, 96 * h + 96, 6)) for k in range(3, 6)], ["n256"] + fls[2:], ["px%d" % h], [b], stop=False)
                mm(ps[b][:, 64:80], turns(T.E, lambda i: T.bx[:, H * h + i:H * h + H:16]), ["E", "bx%d" % h], ["pc%d" % h], [b], start=False, stop=False)
                mm(ps[b][:, 64:80], [(T.n256[:], fl(96 * h + k, 96 * h + 96, 6)) for k in (1, 2)], ["n256"] + fls[:2], ["py%d" % h], [b], start=False)
                ts(fail(a, a + 16), ps[b][:, 64:80], 7.5 - 256 * S, A.is_lt, ["px%d" % h, "py%d" % h, "zero2"], ["fail%d" % h], [b])
                scan(cum(a + 1, a + 17), fail(a, a + 16), fail(a, a + 16), cum(16, 17) if h else 0.0, A.add, A.max,
                     ["fail%d" % h] + nm("cum", range(h)), ["cum%d" % h])
                tt(prod(a, a + 16), fail(a, a + 16), cc(a, a + 16), A.mult, ["fail%d" % h, "cc%d" % h], ["prod%d" % h])
                first = [] if h else [(T.ones[0:1, :], crow0)]
                mm(ps[b][:, 96:96 + n], first + [(T.idn[:], cc(a, a + n)), (T.tri[:] if h else T.triA[:], fail(a, a + n)), (T.blk[:], cum(a, a + n)), (Ni, prod(a, a + n))],
                   ["ones", "crow0", "idn", "cc%d" % h, "tri", "triA", "Ni", "blk", "fail%d" % h, "prod%d" % h] + nm("cum", range(h + 1)), ["pp%d" % h], [b])
                copy(msg[h][:], ps[b][:, 96:96 + n], ["pp%d" % h], ["msg%d%d" % (t, h)], [b])
                send(land[h][:], msg[h][:], 0, "r%s%d" % ("ab"[h], t), ["msg%d%d" % (t, h)], "land%d%d" % (t, h))
                ops[-2]["up"] = OPT["up"][h]

        def gather(dst, name, B, Br, offs, on, h, e):
            if e == "a":
                act(half(dst, h), at(B, offs, 16 * h), F.Identity, Br + [on + str(h)], [name + str(h)], gat=H)
            else:
                copy(half(dst, h), at(B, offs, 16 * h), Br + [on + str(h)], [name + str(h)], gat=H)

        ob = T["ob%d" % t]
        for h in both:
            gather(T.Gp, "Gp", TB, Tr, T.poff, "poff", h, OPT["gp"][last][h])
        for hs in ([both] if OPT["jm"][last] else [(0,), (1,)]):
            a, e = hs[0], hs[-1] + 1
            mm(ps[a][:, 96:96 + 16 * (e - a)], turns(T.Ej, lambda i: T.Gp[:, H * a + i:H * e:16]), ["Ej"] + nm("Gp", hs), ["pl%d" % a], [a])
            copy(T.joff[:, 16 * a:16 * e], ps[a][:, 96:96 + 16 * (e - a)], ["pl%d" % a], nm("joff", hs), [a])
        for h in both:
            a, b, b2 = 16 * h, 4 + h, 6 + h
            Gp, Gj, ab, new = half(T.Gp, h), half(T.Gj, h), half(T.ab, h), slice(o + H * h, o + H * h + H)
            G = ["Gp%d" % h, "Gj%d" % h]
            gather(T.Gj, "Gj", TB, Tr, T.joff, "joff", h, OPT["gj"][last][h])
            gather(T.Mp, "Mp", M, Mr, T.poff, "poff", h, OPT["lmp" if last else "mp"][h])
            tt(half(T.t2, h), at(M, T.joff, a), half(T.Mp, h), A.max, Mr + ["joff%d" % h, "Mp%d" % h], ["t2%d" % h], gat=H)
            pt, tab, pd, dif = nm("pt%d" % h, range(3)), ps[b2][:, 0:H], ["pb%d" % b, "pd%d" % b], ps[b][:, 0:H]
            mm(dif, [(SLp, Gp)], ["SLp", G[0]], pd[:1], [b], H, True, False)
            mm(dif, [(SLn, Gj)], ["SLn", G[1]], pd[1:], [b], H, False, True)
            if OPT["lab" if last else "ab"][h] == "a":
                act(ab, dif, F.Abs, pd, ["ab%d" % h], [b], n=H)
            else:
                ts(ab, dif, 0.0, A.not_equal, pd, ["ab%d" % h], [b], H)
            if not last:
                mm(tab, [(Ms, TB[:, H * h:H * h + H]), (Ma, Gp)], Man + ["Ms", G[0]] + parts, [pt[0], "pb%d" % b2] + (dls if h else []), [b2], H, True, False)
                mm(tab, [(Mb, Gj)], Mbn + [G[1]], [pt[1]], [b2], H, False, False)
                mm(tab, [(Mc, ab)], Mcn + ["ab%d" % h], [pt[2]], [b2], H, False, True)
                act(TB[:, new], tab, F.Relu, pt + ["pb%d" % b2, "cols"], ["Tn%d%d" % (t + 1, h)], [b2], bias=col(4 + t), n=H)
            mn, pu, bnd = ["Mn%d%d" % (t + 1, h)], ["pu%d" % b, "pv%d" % b], ps[b][:, H:K]
            onv = last or OPT["bound"][h] == "v"
            mm(bnd, ([] if onv else [(Ni, q(h))]) + [(T.idn[:], half(T.t2, h))], ["idn", "Ni", "t2%d" % h, qn[h]], pu[:1], [b], H, True, False)
            mm(bnd, [(Zc, ab)], ["Zc", "ab%d" % h], pu[1:], [b], H, False, True)
            if onv:
                tt(M[:, new], bnd, q(h), A.max, pu + [qn[h]], mn, [b], H)
            else:
                mm(dif, [(T.idn[:], q(h))], ["idn", qn[h]], pd[:1], [b], H, True, False)
                act(half(T.mr, h), bnd, F.Relu, pu, ["mr%d" % h], [b], n=H)
                mm(dif, [(T.idn[:], half(T.mr, h))], ["idn", "mr%d" % h], pd[1:], [b], H, False, True)
                act(M[:, new], dif, F.Identity, pd, mn, [b], n=H)
            dma("s", T.ym[:, K * t + H * h:K * t + H * h + H], M[:, new], 256 * H, mn)
        if last:
            def rows(base, G, cs, n=96):
                return [(BM[:, base + 3 - c:base + 3 + n - c], G[:, 128 * c:128 * c + 128]) for c in cs]
            fin = ps[6][:, 0:128]
            mm(ps[7][0:32, H:H + 128], rows(1712, T.Gp, range(4), 32), ["QP", "Gp0", "Gp1"], ["pu7"], [7], 128)
            act(ob[0:32, :], ps[7][0:32, H:H + 128], F.Identity, ["pu7"], ["obp"], [7], n=128)
            dma("a", T.ypar[:, K * t:K * t + K], ob[0:32, :], 32 * K, ["obp"])
            mm(ps[6][0:64, 0:128], rows(1648, T.Gp, range(4), 64), ["QP", "Gp0", "Gp1"], ["pb6"], [6], 128, True, False)
            for h in both:
                mm(ps[6][0:64, 0:128], rows(1752, T.Gj, (2 * h, 2 * h + 1), 64), ["QJ", "Gj%d" % h], ["pf%d" % h], [6], 128, False, h == 1)
            pf = ["pb6", "pf0", "pf1"]
            ts(T.same[0:32, :], ps[6][0:32, 0:128], 0.0, A.is_equal, pf, ["same"], [6], 128)
            tt(T.far[0:32, :], ps[6][32:64, 0:128], T.same[0:32, :], A.mult, pf + ["same"], ["far"], [6], 128)
            tt(ob[32:64, :], ps[7][0:32, H:H + 128], T.far[0:32, :], A.add, ["pu7", "far"], ["jmp"], [7], 128)
            dma("a", T.yjump[:, K * t:K * t + K], ob[32:64, :], 32 * K, ["jmp"])
            return
        for h in both:
            mm(ps[6][0:64, H:H + 128], [(BM[:, 131 - c:195 - c], TB[:, o + 128 * c:o + 128 * c + 128]) for c in (2 * h, 2 * h + 1)],
               ["Mo", "Mo2", "Tn%d%d" % (t + 1, h)] + (["Tn%d0" % (t + 1)] if h else []), ["pu6" if h == 0 else "pv6"], [6], 128, h == 0, h == 1)
        act(ob[0:64, :], ps[6][0:64, H:H + 128], F.Identity, ["pu6", "pv6"], ["ob%d" % t], [6], n=128)
        dma("s", T.yjump[:, K * t:K * t + K], ob[32:64, :], 32 * K, ["ob%d" % t])
        dma("s", T.ypar[:, K * t:K * t + K], ob[0:32, :], 32 * K, ["ob%d" % t])

        for h in both:
            alt, out, pa = ps[h][:, H:K], T.W2[:, K + H * h:K + H * h + H], ["pa%d" % h, "pw%d" % h]
            if OPT["alt"][h] == "a":
                gather(T.Xp, "Xp", X, Xr, T.poff, "poff", h, "a")
                terms, tn = [(T.idn[:], q(h)), (T.idn[:], half(T.Xp, h))], ["idn", qn[h], "Xp%d" % h]
                mm(alt, terms, tn, pa[:1], [h], H)
                act(half(T.wrap, h), alt, F.Sigmoid, pa[:1], ["wrap%d" % h], [h], bias=400.0 * (t - 255.5), scale=400.0, n=H)
                mm(alt, terms, tn, pa[:1], [h], H, True, False)
                t0 = float(t)
            else:
                act(half(T.q1, h), q(h), F.Identity, [qn[h]], ["q1%d" % h], bias=t - 256.0, n=H)
                tt(half(T.Xp, h), at(X, T.poff, 16 * h), half(T.q1, h), A.add, Xr + ["q1%d" % h, "poff%d" % h], ["Xp%d" % h], gat=H)
                mm(alt, [(T.idn[:], half(T.Xp, h))], ["idn", "Xp%d" % h], pa[:1], [h], H, True, False)
                act(half(T.wrap, h), half(T.Xp, h), F.Sigmoid, ["Xp%d" % h], ["wrap%d" % h], bias=200.0, scale=400.0, n=H)
                t0 = 256.0
            mm(alt, [(T.n256[:], half(T.wrap, h))], ["n256", "wrap%d" % h], pa[1:], [h], H, False, True)
            act(out, alt, F.Identity, pa, ["alt%d" % h], [h], bias=t0, n=H)
            if h:
                copy(T.got[:], land[1][:, 16:17], ["land%d1" % t], ["got"])
            copy(T.W2[:, 0:K].indirect(land[h][:, 0:16]), half(qin, h), ["land%d%d" % (t, h), "qin%d" % t], ["come"], sct=H)
        mm(ps[3][:, 129:192:2], [(T.ones[0:1, :], crow1), (T.triA[:], fail(0, 32)), (T.blk[:], cum(0, 32))],
           ["ones", "crow1", "triA", "blk", "fail0", "fail1", "cum0", "cum1"], ["pr"], [3])
        tt(ps[3][:, 128:192:2], T.ai[:], ps[3][:, 129:192:2], A.subtract, ["ai", "pr"], ["pq"], [3])
        act(T.room[:], T.got[:], F.Relu, ["got"], ["room"], bias=400.0 * CAP, scale=-400.0)
        act(dv(1, 64, 2), ps[3][:, 129:192:2], F.Sigmoid, ["pr", "room", "zero"], ["dv1"], [3], bias=T.room[:, 0:1], scale=400.0)
        scan(T.go[:], dv(0, 64), ps[3][:, 128:192], 0.0, A.mult, A.add, ["zero", "dv1", "pr", "pq"], ["go"], [3])
        ts(T.goff[:], T.go[:, 1::2], CAP - 0.5, A.add, ["go"], ["goff"])
        q2 = nm("Xn%d" % (t + 2), both)
        for h in both:
            c0 = o + K + H * h
            copy(X[:, c0:c0 + H], T.W2[:, 0:2 * K].indirect(T.goff[:, 16 * h:16 * h + 16]), ["come", "alt0", "alt1", "goff"], [q2[h]], gat=H)
            mm(ps[h][:, 192:208], turns(T.Ew, lambda i: X[:, c0 + i:c0 + H:16]), ["Ew", q2[h]], ["ph%d" % h], [h])
        if t + 2 < RO:
            send(T["qin%d" % (t + 1)][:], X[:, o + K:o + 2 * K], 256 * K, "rq%d" % (t + 1), q2, "qin%d" % (t + 1))

    starts = [0]
    for t in range(RO):
        starts.append(len(ops))
        one_round(t)
    line_up(ops, starts + [len(ops)])
    OPT["starts"] = starts + [len(ops)]
    emit(g, T, ops)
